import numpy as np, ml_dtypes
CORES = [40,41,42,43,44,45,46,47]
N = 8
import mx_ref
BF = ml_dtypes.bfloat16
def gcols(t, e):
    v = np.concatenate([t.reshape(8, 16, -1, 4), np.zeros((8, 16, 1, 4), BF)], axis=2)
    return np.ascontiguousarray(np.stack([v[g][:, e[g]] for g in range(8)])).reshape(128, -1)
def tile(rs):
    return np.stack(rs, axis=2).reshape(128, -1).astype(BF)
def pick(q, e):
    c = np.concatenate([q[0].reshape(128, -1, 4), np.zeros((128, 1, 4), np.uint8)], axis=1); s = np.concatenate([q[1], np.ones((16, 1), np.uint8)], axis=1)
    return (np.ascontiguousarray(c[:, e].reshape(128, -1)), np.ascontiguousarray(s[:, e]))
def join(*qs):
    return (np.concatenate([q[0] for q in qs], axis=1), np.concatenate([q[1] for q in qs], axis=1))
def put(q, e, v):
    c, s = q[0].reshape(128, -1, 4).copy(), q[1].copy(); c[:, e] = v[0].reshape(128, -1, 4); s[:, e] = v[1]
    return (c.reshape(128, -1), s)
def pk(c, s):
    return (np.ascontiguousarray(c), mx_ref.live(s))
def emit(q):
    return q[0], q[1]
def packed(v, rng):
    q = [mx_ref.quantize(np.ascontiguousarray(v[r])) for r in range(N)]
    return np.stack([a for a, b in q]), np.stack([mx_ref.plane(b, rng) for a, b in q])
def values_of_codes():
    e, c = np.zeros((128, 128, 4), np.float32), np.zeros((128, 2, 4), np.uint8)
    e[np.arange(128), np.arange(128), 0] = 1
    c[:127, :, 0] = np.arange(256).reshape(2, 128).T[:127]
    return mx_ref.matmul(mx_ref.quantize(e.reshape(128, 512).astype(BF)), (c.reshape(128, 8), np.full((16, 2), 127, np.uint8))).T.reshape(-1).astype(np.float64)
CODE_VALUE, SCALE_VALUE = values_of_codes(), 2.0 ** (np.arange(256) - 127.0)
def decode(q):
    return (CODE_VALUE[q[0]].reshape(16, 8, -1, 4) * SCALE_VALUE[q[1]][:, None, :, None] + 0.0).reshape(128, -1).astype(np.float32)
def f(rng, *shape):
    return mx_ref.flush((rng.standard_normal(shape, dtype=np.float32) * np.exp2(rng.integers(-2, 3, shape[:-1] + (1,)))).astype(BF))
def wide(rng, *shape, cols=0):
    v = rng.standard_normal(shape, dtype=np.float32) * np.exp2(rng.integers(-12, 13, shape)).astype(np.float32)
    if cols: v *= np.repeat(np.exp2(rng.integers(-cols, cols + 1, shape[:-2] + (1, shape[-1] // 4))) * (rng.random(shape[:-2] + (1, shape[-1] // 4)) > 0.0625), 4, axis=-1).astype(np.float32)
    return mx_ref.flush(v.astype(BF))
C, A, STEP = 256, 16, [1, 2]
def big(v):
    v = v.astype(np.float32)
    v[np.abs(v) < np.float32(2.0 ** -16)] = 0
    return v.astype(BF)
def numbers_of(rng):
    return {"x": big(f(rng, N, 128, 4 * C)), "u": np.array(f(rng, N, 128, 512)), "v": np.array(f(rng, N, 128, 512))}
def layers(rng):
    return big(rng.random((N, 128, 2048), dtype=np.float32) * 2 - 1).reshape(N, 8, 16, 4, 8, 16, 4)
def weights(rng, w):
    c, s = packed(np.ascontiguousarray(w).reshape(N, 128, 2048), rng)
    return {"wc": c, "ws": s}
def setup_inputs(rng):
    return {**numbers_of(rng), **weights(rng, layers(rng))}
def setup_inputs_ties(rng):
    d = numbers_of(rng)
    o = rng.permutation(N)
    x = d["x"].reshape(N, 8, 16, C, 4)
    x[:, :, :8] = 0
    x[:, :, 0, :, 0] = rng.integers(0, 4, (N, 8, C)).astype(np.float32).astype(BF)
    t = rng.integers(-1, 2, (N, 8, C, 3))
    t[o[0]] = -1
    t[o[0], :, A::A + 1, 0] = 1
    t[o[1]] = 1
    x[:, :, 1, :, :3] = t.astype(np.float32).astype(BF)
    u = d["u"].reshape(N, 128, 128, 4)
    for i in range(4): u[:, :, i::16] = 0
    for r in range(N):
        for h in range(0, 128, 16):
            u[r, h, h, 0] = 0.0 if r == o[0] else -1.0 if r == o[2] else 1.0
            for i in range(3): u[r, h + 1, h + 1 + i, i] = 1.0
    w = layers(rng)
    w[:, :, :, :, :, :8] = 0
    return {"x": x.reshape(N, 128, 4 * C), "u": u.reshape(N, 128, 512), "v": d["v"], **weights(rng, w)}
def setup_inputs_near(rng):
    d = numbers_of(rng)
    x = d["x"].astype(np.float32).reshape(N, 8, 16, C, 4)
    x[:, :, 0] = 0
    x[:, :, 8:] = 0
    u = d["u"].reshape(N, 128, 128, 4)
    for i in range(4): u[:, :, i::16] = 0
    o = rng.permutation(N) % 4
    for r in range(N):
        tiny = o[r] == 2
        k = 2.0 ** -30 if o[r] == 1 else 1.0
        if tiny:
            m = rng.integers(0, 8, (8, C))
            x[r, :, 8, :, 0] = (8 + m) * 2.0 ** -33
            x[r, :, 9, :, 0] = (15 - m) * 2.0 ** -33
        else:
            s = rng.integers(0, 16, (8, C))
            x[r, :, 0, :, 0] = 1.0 if o[r] == 0 else -1.0 if o[r] == 1 else rng.choice([-1.0, 1.0], (8, C))
            x[r, :, 8] = ((s[:, :, None] >> np.arange(4)) & 1) * np.exp2(np.arange(4) - 23.0)
            x[r, :, 11, :, 0] = 2.0 ** -10
        x[r, :, 12:15, :, 0] = rng.integers(-1, 2, (8, 3, C)) * (2.0 ** -30 if tiny else 2.0 ** -22)
        if o[r] in (0, 2):
            for g in rng.permutation(8)[:4]: x[r, g, 0, rng.integers(C), 1] = rng.choice([-1.0, 1.0]) * 2.0 ** 21
        for h in range(0, 128, 16):
            if tiny:
                u[r, h + 8, h, 0] = 1.125 * 2.0 ** -30
                u[r, h + 9, h, 0] = 2.0 ** -30
            else:
                u[r, h, h, 0] = k
                u[r, h + 8, h] = k
                u[r, h + 11, h, 0] = k
            if o[r] in (0, 2): u[r, h, h, 1] = 2.0 ** 9
            for i in range(3): u[r, h + 12 + i, h + 1 + i, 0] = 2.0 ** -30
    w = layers(rng)
    for i in [0, 8, 9, 10, 11, 12, 13, 14, 15]:
        w[:, :, i] = 0
        w[:, :, :, :, :, i] = 0
    return {"x": x.reshape(N, 128, 4 * C).astype(BF), "u": u.reshape(N, 128, 512), "v": d["v"], **weights(rng, w)}
def setup_inputs_ends(rng):
    d = numbers_of(rng)
    e = rng.permutation(N)
    top = e[0] ^ STEP[0] ^ STEP[1]
    mate = top ^ STEP[0]
    rest = [r for r in e[1:] if r not in (top, mate)]
    e = [e[0]] + rest[:N // 2 - 1] + [top, mate] + rest[N // 2 - 1:]
    c = rng.integers(8)
    x = np.zeros((N, 8, 16, C, 4), np.float32)
    u = d["u"].astype(np.float32).reshape(N, 8, 16, 128, 4)
    for i in range(4): u[:, :, :, i::16] = 0
    v = rng.choice([-1.0, 1.0], (N, 128, 512)).astype(np.float32)
    sign = lambda *s: rng.choice([-1.0, 1.0], s)
    for r in range(N):
        h = rng.permutation(8)
        if r in e[:N // 2]:
            t = sign(4, 1, 1, 1)
            if r == e[0]: t[:] = -1
            m = sign(8, 1, C, 1) * rng.choice([0.5, 0.75, 0.875, 1.0], (8, 1, C, 1))
            m[h[4:, None], 0, rng.permutation(C)[:64], 0] = -rng.choice([0.75, 0.875, 1.0], (4, 64))
            p = (m[h[4:]] > 0).all(axis=0)
            m[h[4]][p] *= -1
            m[h[:4]] = t
            x[r] = 2.0 ** 21 * m
            v[r] *= np.float32(2.0 ** 30)
            for n in range(8):
                g = h[n]
                if n < 4: u[r, h[:4], :, 16 * g] = -2.0 ** 30 * t[:, :, 0]
                if n in (2, 3): u[r, h[4:], :, 16 * g] = 2.0 ** 29 if n == 2 else 2.0 ** 30
                if n >= 4: u[r, h[4:], :, 16 * g] = 2.0 ** 30 * sign(4, 1, 1)
                for i in range(3): u[r, rng.choice(h[4:]), :, 16 * g + 1 + i] = 2.0 ** 30 * rng.choice([-1.0, 1.0])
        elif r == top:
            x[r] = 2.0 ** 21
            s = (rng.permutation(C)[:, None] >> np.arange(8)) & 1
            x[r, c, :2] = 2.0 ** 21 * (2.0 * s - 1.0).reshape(C, 2, 4).transpose(1, 0, 2)
            v[r] *= np.float32(2.0 ** 30)
            for n in range(8):
                g = h[n]
                u[r, :, :, 16 * g] = -2.0 ** 30 if n < 4 else 2.0 ** 30
                k = 4.0 * rng.permutation(2)[:, None] + rng.permutation(4)
                u[r, c, :2, 16 * g] *= np.exp2(-k).astype(np.float32)
        else:
            x[r, :, :8] = 2.0 ** -30 * sign(8, 1, C, 1)
            x[r, :, 8:] = sign(8, 1, C, 1)
            v[r] *= np.float32(2.0 ** -30)
            for n in range(8):
                g = h[n]
                if n >= 2: u[r, :, :8, 16 * g] = 2.0 ** -30 * sign(8, 1, 1)
                for i in range(3): u[r, rng.integers(8), :8, 16 * g + 1 + i] = 2.0 ** -30 * rng.choice([-1.0, 1.0])
    w = rng.choice([-1.0, 1.0], (N, 8, 16, 4, 8, 16, 4)).astype(np.float32)
    w[e[0]] = 1
    w[e[1]] = 0
    w[:, :, :8] = 0
    w[:, :, :, :, :, :8] = 0
    w[mate] = 1
    w[mate, c, :2] = 0
    return {"x": x.reshape(N, 128, 4 * C).astype(BF), "u": u.reshape(N, 128, 512).astype(BF), "v": v.astype(BF), **weights(rng, w.astype(BF))}
def setup_inputs_blocks(rng):
    d = numbers_of(rng)
    k = np.exp2(rng.integers(14, 19, (N, 8, 2, 1, C, 1)).astype(np.float64))
    s = (N, 8, 2, 8, C, 4)
    a = k * np.exp2(-rng.integers(8, 15, s).astype(np.float64)) * (1 + (2 * rng.integers(0, 64, s) + 1) * 2.0 ** -7) * rng.choice([-1.0, 1.0], s)
    a[:, :, :, 0, :, 0] = 1.96875 * k[:, :, :, 0, :, 0] * rng.choice([-1.0, 1.0], (N, 8, 2, C))
    u = d["u"].reshape(N, 128, 128, 4)
    e = rng.integers(N)
    for i in range(4): u[e, :, i::16] = 0
    w = layers(rng)
    w[:, :, ::8] = 0
    return {"x": a.astype(np.float32).reshape(N, 128, 4 * C).astype(BF), "u": u.reshape(N, 128, 512), "v": d["v"], **weights(rng, w)}
def setup_inputs_spread(rng):
    d = setup_inputs(rng)
    d["x"] = big(np.clip(wide(rng, N, 128, 4 * C, cols=6).astype(np.float32), -2.0 ** 21, 2.0 ** 21))
    return d
def check_inputs(d):
    b = []
    for k, top in (("x", 2.0 ** 21), ("u", 2.0 ** 30), ("v", 2.0 ** 30)):
        a = np.abs(d[k].astype(np.float32))
        if not (np.isfinite(a).all() and ((a == 0) | (a >= 2.0 ** -30) & (a <= top)).all()): b.append("a value of " + k)
    none, least, most = [emit(mx_ref.quantize(np.full((128, 16), k, np.float32).astype(BF)))[1][0, 0] for k in (0.0, 2.0 ** -30, 1.0)]
    for r in range(N):
        if ((d["wc"][r] == 0x7F) | (d["wc"][r] == 0xFF)).any(): b.append("wc: a code that is no number")
        s = mx_ref.live(d["ws"][r])
        if ((s != none) & ((s < least) | (s > most))).any(): b.append("ws: a scale out of range")
        elif (np.abs(decode(pk(d["wc"][r], d["ws"][r]))) > 1).any(): b.append("a number of W beyond 1")
    return b
def sources(s):
    order = np.argsort(-(s[::16] + np.float32(0.0)), axis=1, kind="stable")
    place = np.argsort(order, axis=1, kind="stable")
    kind = 1 * (s[1::16] > 0) + 2 * (s[2::16] > 0) + 4 * (s[3::16] > 0)
    used, j = np.zeros((C, 8), bool), np.arange(C)
    c = np.zeros((8, C), np.int64)
    for g in range(8):
        look = order[g][(place[(g + 1) % 8][:, None] + np.arange(A)) % C]
        new = ~used[j[:, None], kind[g][look]]
        c[g] = look[j, np.argmax(new, axis=1)]
        used[j, kind[g][c[g]]] = True
    return c
def reference(x, u, v, wc, ws):
    qu = [mx_ref.quantize(u[r]) for r in range(N)]
    lay = [[pick(pk(wc[r], ws[r]), np.arange(128 * b, 128 * b + 128)) for b in range(4)] for r in range(N)]
    now = [x[r] for r in range(N)]
    for h in STEP:
        q = [mx_ref.quantize(now[r]) for r in range(N)]
        own = [decode(q[r]) for r in range(N)]
        took = [sources(mx_ref.matmul(qu[r], q[r])) for r in range(N)]
        z = [mx_ref.quantize(gcols(own[r].astype(BF), took[r])) for r in range(N)]
        made = []
        for r in range(N):
            e = r ^ h
            back = mx_ref.quantize(tile([mx_ref.matmul(lay[e][b], z[r]) * np.float32(0.03125) + own[e][:, b::4] for b in range(4)]))
            first = np.full((8, C), -1)
            for g in range(8):
                for j in range(C - 1, -1, -1): first[g, took[r][g, j]] = j
            made.append((own[r] + gcols(decode(back).astype(BF), first).astype(np.float32)).astype(BF))
        now = made
    y, src = np.zeros((N, 128, C), np.float32), np.zeros((N, 8, C), np.float32)
    oc, osc = np.zeros((N, 128, 4 * C), np.uint8), np.zeros((N, 16, C), np.uint8)
    for r in range(N):
        p = mx_ref.quantize(now[r])
        y[r] = mx_ref.matmul(mx_ref.quantize(v[r]), p)
        src[r] = took[r]
        oc[r], osc[r] = emit(p)
    return {"y": y, "src": src, "oc": oc, "osc": osc}

@@ -1,0 +1,496 @@
+import numpy as np
+from concourse.bass import DstId, RemoteDMATransfer
+from concourse.mybir import dt, AluOpType, AxisListType, ActivationFunctionType
+
+OP = AluOpType
+AF = ActivationFunctionType
+BIG = 8e28
+K16 = 201326592.0
+EPS = 2.0 ** -19
+KE16, KE256 = 384.0, 6144.0
+W = 48
+STEP = [1, 2]
+
+F4, BF, I4, U2, CODE, U1 = "float32", "bfloat16", "int32", "uint16", "float8_e4m3fn_x4", "uint8"
+SCRATCH, PART = {}, {}
+
+
+def _add(dtype, **bufs):
+    for k, n in bufs.items():
+        SCRATCH[k] = ("sbuf", [128, n], dtype)
+
+
+def _pieces(base, dtype, **bufs):
+    at = 0
+    for k, n in bufs.items():
+        PART[k] = (base, at, n)
+        at += (n + 15) // 16 * 16
+    SCRATCH[base] = ("sbuf", [128, at], dtype)
+
+
+_add(BF, x0=1024, x1=1024, x2=1024, ut=512, vt=512, zz=512, kk=256, sg=256, cw=512, rot=512, ebig=2048, tc=1536,
+     mv=512, bt=1024, zs=272, z=256, d0=272, d1=272, tb=272, w0=272, w1=272, rt=512, tt=1024, ex=512, et=256, ets=256,
+     cm=4096, fo=1024, fp=1024, zt=1024, yt=1024, dy=1088, crow=256, eq=4096, pm=4096, fz=1024)
+_add(F4, ikf=256, maskd=256, hd=256, kz=256, kbi=256, lb=512, ab=256, sd=256, sx=256, junk=4096, fb=16 * W, so=16 * W,
+     srow=256, yout=256)
+_pieces("f4s", F4, pf=16, mask16=16, kcol=16, cb0=16, cb1=16, cb2=16, gm=8, ig8=8, iposf=50, nega=50, negb=50, negc=50, sig=48,
+        wt0=8, wt1=8, pos2=48, pos3=48, fbp=48, fbz=48, kai2=16, acc=16, acc2=16, rl=16, dah=16, dhh=16, ddb=16, dda=16)
+_pieces("i4s", I4, ip=1, pi=8, ikp=256, iposi=48, iu=8, kai=256, im=16)
+_pieces("u2s", U2, ul=8, l1=16, l2=16, l4=16)
+_add(U2, lc0=16, lc1=16, plc0=16, plc1=16)
+for _n, _w in (("uq", 128), ("ur", 128), ("vq", 128), ("wq", 512), ("xqa", 256), ("xqb", 256), ("xqc", 256), ("pxa", 256), ("pxb", 256),
+               ("cwq", 128), ("rotq", 128), ("eq_", 512), ("tcq", 384), ("mvq", 128), ("btq", 256), ("rtq", 128), ("ttq", 256),
+               ("exq", 128), ("zqa", 256), ("zqb", 256), ("yqa", 256), ("yqb", 256), ("pya", 256), ("pyb", 256)):
+    SCRATCH[_n] = ("sbuf", [128, _w], CODE)
+    SCRATCH[_n + "S"] = ("sbuf", [128, _w], U1)
+for _k in range(8):
+    SCRATCH["ps%d" % _k] = ("psum", [128, 512], F4)
+
+NDMA = 16
+SEMAPHORES = (["V", "A", "P", "G"] + ["d%d" % k for k in range(NDMA)] + [k + "%d" % r for k in ("rx", "lx", "rl", "ll") for r in (0, 1)]
+              + [k + "%d%d" % (r, h) for k in ("ry", "ly") for r in (0, 1) for h in (0, 1)])
+
+
+def rank_program(g, core, T, topo):
+    rank = T.rank_of(core)
+    if rank is None:
+        return
+    eng = {"V": g.vector, "A": g.scalar, "P": g.tensor, "G": g, "S": g.sync}
+    cnt = {"V": 0, "A": 0, "P": 0, "G": 0}
+    seen = {q: {} for q in eng}
+    log = {}
+    ndma = [0]
+    final = {}
+
+    def B(name, a=0, b=None, s=1):
+        if name in PART:
+            base, at, n = PART[name]
+            name, a, b = base, a + at, at + (n if b is None else b)
+        elif b is None:
+            b = SCRATCH[name][1][1]
+        ap = T[name][:, a:b] if s == 1 else T[name][:, a:b:s]
+        return (ap, name, a, b, s)
+
+    def U8(v):
+        return (v[0].bitcast(dt.uint8),) + v[1:]
+
+    def clash(u, v):
+        if u[3] <= v[2] or v[3] <= u[2]:
+            return False
+        return not (u[4] == v[4] > 1 and (u[2] - v[2]) % u[4])
+
+    def need(q, sem, val):
+        if seen[q].get(sem, 0) < val:
+            eng[q].wait_ge(T.sem[sem], val)
+            seen[q][sem] = val
+
+    def order(q, reads, writes, free=()):
+        wants = {}
+        for kind, views in (("r", reads), ("w", writes)):
+            for v in views:
+                ps = v[1][:2] == "ps"
+                for k, u, uq, sem, val in log.get(v[1], ()):
+                    if ps:
+                        hit = uq != q or ((kind, k) != ("r", "r") and (kind == "r" or k == "r" or v[1] not in free))
+                    else:
+                        hit = (kind, k) != ("r", "r") and clash(v, u)
+                    if hit:
+                        wants[sem] = max(val, wants.get(sem, 0))
+        for sem, val in wants.items():
+            need(q, sem, val)
+
+    def note(q, reads, writes, sem, val):
+        for v in writes:
+            old = log.get(v[1], [])
+            keep = [e for e in old if not (v[1][:2] == "ps" or (v[4] == 1 and v[2] <= e[1][2] and e[1][3] <= v[3])
+                                           or (v[4] == e[1][4] and v[2] == e[1][2] and v[3] == e[1][3]))]
+            log[v[1]] = keep + [("w", v, q, sem, val)]
+        for v in reads:
+            log.setdefault(v[1], []).append(("r", v, q, sem, val))
+
+    def run(q, fn, outs, ins, free=()):
+        order(q, ins, outs, free)
+        cnt[q] += 1
+        fn(eng[q]).then_inc(T.sem[q], 1)
+        note(q, ins, outs, q, cnt[q])
+
+    def dma(q, out, in_, outs, ins):
+        order(q, ins, outs)
+        sem = "d%d" % ndma[0]
+        ndma[0] += 1
+        eng[q].dma_start(out, in_).then_inc(T.sem[sem], 16)
+        final[sem] = 16
+        note(q, ins, outs, sem, 16)
+
+    def ts(out, a, s1, s2, op0, op1=None):
+        ins = [a] + [s for s in (s1, s2) if isinstance(s, tuple)]
+        v1, v2 = [s[0] if isinstance(s, tuple) else s for s in (s1, s2)]
+        if op1 is None:
+            run("V", lambda e: e.tensor_scalar(out[0], a[0], v1, None, op0), [out], ins)
+        else:
+            run("V", lambda e: e.tensor_scalar(out[0], a[0], v1, v2, op0, op1), [out], ins)
+
+    def tt(out, a, b, op):
+        run("V", lambda e: e.tensor_tensor(out[0], a[0], b[0], op), [out], [a, b])
+
+    def cp(out, a):
+        run("V", lambda e: e.tensor_copy(out[0], a[0]), [out], [a])
+
+    def scan(out, a, b, init, op0, op1):
+        run("V", lambda e: e.tensor_tensor_scan(out[0], a[0], b[0], init, op0, op1), [out], [a, b])
+
+    def fill(out, c):
+        run("V", lambda e: e.memset(out[0], c), [out], [])
+
+    def quant(code, a, n, tile):
+        run("V", lambda e: e.quantize_mx(T[code][:, a:a + n], T[code + "S"][:, a:a + n], tile[0]),
+            [B(code, a, a + n), B(code + "S", a, a + n)], [tile])
+
+    def act(out, a, func=AF.Copy, scale=1.0, bias=None, accum=None):
+        ins = [a] + [s for s in (scale,) if isinstance(s, tuple)]
+        outs = [out] + ([accum] if accum is not None else [])
+        kw = {}
+        if bias is not None:
+            kw["bias"] = bias
+        if isinstance(scale, tuple):
+            kw["scale"] = scale[0]
+        elif scale != 1.0:
+            kw["scale"] = scale
+        if accum is not None:
+            kw["accum_out"] = accum[0]
+        run("A", lambda e: e.activation(out[0], a[0], func, **kw), outs, ins)
+
+    def mm(bank, n, st, a, mvg, b, start=True, stop=True):
+        name = "ps%d" % bank
+        run("P", lambda e: e.matmul_mx(T[name][:, 0:n], T[st][:, a:a + 128], T[st + "S"][:, a:a + 128],
+                                       T[mvg][:, b:b + n], T[mvg + "S"][:, b:b + n], start, stop),
+            [B(name, 0, n)], [B(st, a, a + 128), B(st + "S", a, a + 128), B(mvg, b, b + n), B(mvg + "S", b, b + n)],
+            free=() if start else (name,))
+
+    def gather(q, out, win, off):
+        w = win[0].indirect(off[0])
+        if q == "V":
+            run("V", lambda e: e.tensor_copy(out[0], w), [out], [win, off])
+        else:
+            run("A", lambda e: e.activation(out[0], w, AF.Copy), [out], [win, off])
+
+    def iota(out, pattern, base, cm):
+        out = B(out) if isinstance(out, str) else out
+        if SCRATCH[out[1]][2] != I4:
+            run("G", lambda e: e.iota(out[0], pattern, base, cm, allow_small_or_imprecise_dtypes=True), [out], [])
+        else:
+            run("G", lambda e: e.iota(out[0], pattern, base, cm), [out], [])
+
+    def mark(out, in_, pattern, fill, base, cm):
+        run("G", lambda e: e.affine_select(out[0], in_[0], pattern, OP.not_equal, fill, base, cm), [out], [in_])
+
+    def send(parts, dst, rsem, lsem):
+        engs = topo.engines(core, dst)
+        rid, pid, _s = topo.addr(dst)
+        m = topo.mask(core, dst)
+        order("G", [s for d, s in parts], [])
+        tot = 0
+        for d, s in parts:
+            g.remote_dma(d[0], s[0], T.sem[rsem], T.sem[lsem], pid, rid, m)
+            tot += len(engs)
+        final[lsem] = tot
+        final[rsem] = tot
+        for d, s in parts:
+            note("G", [s], [], lsem, tot)
+            note("R", [], [d], rsem, tot)
+
+    dma("S", T.x0[:], T.x[:], [B("x0")], [])
+    dma("A", T.ut[:], T.u[:], [B("ut")], [])
+    fill(B("zz"), 0.0)
+    iota("iu", [[16, 8]], 0, 0)
+    iota("ip", [[0, 1]], 0, 1)
+    iota("ikp", [[1, 256]], 128, -1)
+    iota("kbi", [[0, 16], [1, 16]], 0, 0)
+    iota("ikf", [[1, 256]], 0, 0)
+    iota("cb0", [[0, 8], [-1024, 2]], 512, 0)
+    iota("cb1", [[0, 4], [-1024, 2], [0, 2]], 512, 0)
+    iota("cb2", [[0, 2], [-1024, 2], [0, 4]], 512, 0)
+    iota("ig8", [[1, 8]], 0, 0)
+    iota("iposf", [[1, 50]], -2, 0)
+    iota("iposi", [[1, 48]], 0, 0)
+    iota("im", [[16, 16]], 0, 0)
+
+    cp(B("ul"), B("iu"))
+    for name in ("cw", "bt", "mv", "rt"):
+        fill(B(name), 0.0)
+    pi = lambda k: B("pi", k, k + 1)
+    pf = lambda k: B("pf", k, k + 1)
+    ts(pi(1), B("ip"), 15, None, OP.bitwise_and)
+    ts(pi(2), B("ip"), 7, None, OP.bitwise_and)
+    ts(pi(3), B("ip"), 4, None, OP.arith_shift_right)
+    ts(pi(4), B("ip"), 3, 1, OP.arith_shift_right, OP.bitwise_and)
+    ts(B("kai"), B("ikp"), 15, None, OP.bitwise_and)
+    cp(B("pf", 1, 5), B("pi", 1, 5))
+    ts(B("hd"), B("kbi"), 0.0, BIG, OP.is_equal, OP.mult)
+    ts(B("maskd"), B("kai"), 0.0, BIG, OP.is_gt, OP.mult)
+    ts(B("sg"), B("kbi"), 0.0, None, OP.is_gt)
+    act(B("kk"), B("ikf"), AF.Identity, bias=-127.5)
+    quant("xqa", 0, 256, B("x0"))
+    quant("uq", 0, 128, B("ut"))
+    ul = B("ul")
+    run("V", lambda e: e.tensor_copy(T.ur[:].bitcast(dt.uint32), T.uq[:].bitcast(dt.uint32).indirect(ul[0])), [B("ur")], [B("uq"), ul])
+    run("A", lambda e: e.activation(T.urS[:], T.uqS[:].indirect(ul[0]), AF.Copy), [B("urS")], [B("uqS"), ul])
+
+    def constants_g():
+        for b in range(4):
+            mark(B("ebig", 512 * b, 512 * b + 512), B("zz"), [[1, 512]], 32.0, -b, -4)
+        for t in (2, 3):
+            iota(B("tc", t, 1536, 4), [[0, 384]], 0, 0)
+        for t in range(2):
+            o = B("rot", t, 512, 4)
+            mark(o, B("zz", 0, 128), [[1, 128]], 1.0, 16, -1)
+            mark(o, o, [[1, 128]], 1.0, -112, -1)
+            iota(B("rot", t + 2, 512, 4), [[0, 128]], 0, 0)
+        for t in (2, 3):
+            iota(B("tt", t, 1024, 4), [[0, 256]], 0, 0)
+        for b in range(4):
+            iota(B("dy", 272 * b + 256, 272 * b + 272), [[0, 16]], 0, 0)
+
+    todo = []
+
+    def later(f, *a, **k):
+        todo.append(lambda: f(*a, **k))
+
+    def constants_v():
+        for b in range(3):
+            later(ts, pf(8 + b), pf(1), 1.0 + b, None, OP.is_equal)
+        later(ts, B("gm"), B("ig8"), pf(3), None, OP.is_equal)
+        for b in range(3):
+            later(ts, B("cb%d" % b), B("cb%d" % b), pf(8 + b), None, OP.mult)
+        later(ts, pf(6), pf(4), 500.0 - 1e6, 1e6, OP.mult, OP.add)
+        later(tt, B("cb0"), B("cb0"), B("cb1"), OP.add)
+        later(ts, pf(7), pf(4), 999.0, 1.0, OP.mult, OP.add)
+        later(tt, B("cb0"), B("cb0"), B("cb2"), OP.add)
+        for gg in range(8):
+            later(act, B("cw", 64 * gg, 64 * gg + 64, 4), B("cb0"), scale=B("gm", gg, gg + 1))
+        later(ts, B("kz"), B("kk"), pf(4), 1536.0, OP.mult, OP.add)
+        later(ts, B("mask16"), B("kai2"), 0.0, None, OP.is_equal)
+        for h in range(2):
+            for d in range(2):
+                later(ts, B("mv", 32 * h + 2 * h + d, 32 * h + 32, 4), B("ig8"), pf(3), 1.0 / EPS, OP.is_equal, OP.mult)
+        later(quant, "mvq", 0, 128, B("mv"))
+        later(ts, B("kcol"), B("im"), pf(1), -127.5, OP.add, OP.add)
+        later(ts, B("pos2"), B("iposf", 2, 50), 30.5, None, OP.is_gt)
+        later(ts, B("kai", 0, 48), B("iposi"), 1, None, OP.bitwise_and)
+        later(ts, pf(11), pf(2), 2.0, None, OP.mult)
+        later(tt, B("pos3"), B("pos2"), B("kai", 0, 48), OP.max)
+        later(ts, pf(12), pf(2), -2.0, 30.0, OP.mult, OP.add)
+        later(ts, B("fbp"), B("pos3"), 1e6, 7936 * EPS, OP.mult, OP.add)
+        later(ts, pf(13), pf(2), 2.0, 30.0, OP.mult, OP.add)
+        later(cp, B("fbz"), B("fbp"))
+        later(ts, B("nega"), B("iposf"), pf(11), None, OP.is_equal)
+        later(ts, B("fbz", 0, 15, 2), B("fbz", 0, 15, 2), 0.0, None, OP.mult)
+        later(ts, B("negb"), B("iposf"), pf(12), None, OP.is_equal)
+        later(ts, B("negc"), B("iposf"), pf(13), None, OP.is_equal)
+        later(tt, B("nega"), B("nega"), B("negb"), OP.max)
+        later(ts, pf(14), pf(4), EPS - 512 * EPS, 512 * EPS, OP.mult, OP.add)
+        later(tt, B("nega"), B("nega"), B("negc"), OP.max)
+        later(ts, pf(15), pf(4), EPS, None, OP.mult)
+        later(tt, B("sig"), B("nega", 0, 48), B("nega", 2, 50), OP.subtract)
+        later(ts, B("wt0"), B("ig8"), pf(3), pf(14), OP.is_equal, OP.mult)
+        later(ts, B("wt1"), B("ig8"), pf(3), pf(15), OP.is_equal, OP.mult)
+
+    def constants_a():
+        for gg in range(8):
+            for t in range(2):
+                act(B("tc", 4 * W * gg + t, 4 * W * gg + 4 * W, 4), B("sig"), scale=B("wt%d" % t, gg, gg + 1))
+        for c in range(16):
+            act(B("fb", W * c, W * c + W), B("fbz" if c < 2 else "fbp"))
+
+    TB = ((0, 1), (2, 7))
+    HB = ((3, 4, 5, 6), (0, 1, 2, 7))
+    for r in range(2):
+        dst = T.cores[rank ^ STEP[r]]
+        L = "abc"
+        xq, px, zq, yq, py = "xq" + L[r], "px" + L[r], "zq" + L[r], "yq" + L[r], "py" + L[r]
+        lc, plc = "lc%d" % r, "plc%d" % r
+        send([(U8(B(px)), U8(B(xq))), (B(px + "S"), B(xq + "S"))], dst, "rx%d" % r, "lx%d" % r)
+        if r == 0:
+            constants_g()
+        mm(1, 256, "ur", 0, xq, 0)
+        mm(0, 256, "ur", 0, xq, 0)
+        mm(2, 256, "uq", 0, xq, 0)
+        act(B("ab"), B("ps0", 0, 256), AF.Abs, scale=0.6 * 2.0 ** -23, bias=2.0 ** -122)
+        act(B("lb", 0, 256), B("ps0", 0, 256))
+        act(B("bt", 0, 1024, 4), B("ps2", 0, 256), AF.Sign, bias=-2.0 ** -100)
+        if r == 0:
+            ts(B("kai2"), B("kai", 0, 16), 1.0, None, OP.mult)
+            constants_v()
+        tt(B("sd"), B("ps1", 0, 256), B("maskd"), OP.add)
+        scan(B("sx"), B("hd"), B("sd"), 0.0, OP.add, OP.min)
+        tt(B("lb", 256, 512), B("ps1", 0, 256), B("ab"), OP.add)
+        for m in range(16):
+            ts(B("cm", 256 * m, 256 * m + 256), B("lb", 16 * m + 16, 16 * m + 272), B("sx", 16 * m + 15, 16 * m + 16), None, OP.is_le)
+            act(B("junk", 256 * m, 256 * m + 256), B("cm", 256 * m, 256 * m + 256), AF.Identity, bias=-257 / 512, accum=B("acc", m, m + 1))
+            for f in todo[:5]:
+                f()
+            del todo[:5]
+            if m == (5 if r == 0 else 2):
+                if r == 0:
+                    quant("cwq", 0, 128, B("cw"))
+                quant("btq", 0, 256, B("bt"))
+                mm(2, 256, "cwq", 0, "btq", 0)
+        tt(B("et"), B("ps1", 0, 256), B("sx"), OP.is_equal)
+        tt(B("z"), B("ps2", 0, 256), B("kz"), OP.add)
+        scan(B("ets"), B("sg"), B("et"), 0.0, OP.mult, OP.add)
+        for f in todo:
+            f()
+        del todo[:]
+        if r == 0:
+            constants_a()
+            quant("eq_", 0, 512, B("ebig"))
+            dma("S", T.wq[:].bitcast(dt.uint8), T.wc[:], [B("wq")], [B("ets")])
+            dma("S", T.wqS[:], T.ws[:], [B("wqS")], [B("ets")])
+        for b in range(4):
+            mm(3 + b, 256, "eq_", 128 * b, xq, 0)
+        tt(B("rl"), B("acc"), B("ets", 15, 256, 16), OP.add)
+        ts(B("l1"), B("rl"), 127.5, None, OP.add)
+        ts(B("rt", 0, 64, 4), B("rl"), K16, K16, OP.add, OP.subtract)
+        l1 = B("l1")
+        run("V", lambda e: e.tensor_copy(T.zs[:, 16:272].indirect(l1[0]), T.z[:]), [B("zs", 16, 272)], [B("z"), l1])
+        tt(B("rt", 1, 64, 4), B("rl"), B("rt", 0, 64, 4), OP.subtract)
+        cp(B("zs", 0, 16), B("zs", 256, 272))
+        if r == 0:
+            quant("rotq", 0, 128, B("rot"))
+        quant("rtq", 0, 128, B("rt"))
+        mm(7, 128, "rotq", 0, "rtq", 0)
+        ts(B("d0"), B("zs"), pf(6), pf(7), OP.is_lt, OP.mult)
+        ts(B("d1"), B("zs"), K16, K16, OP.add, OP.subtract)
+        scan(B("tb"), B("d0"), B("zs"), 64.0, OP.add, OP.min)
+        scan(B("w0"), B("d0"), B("d1"), 64.0, OP.add, OP.min)
+        ts(B("l2"), B("ps7", 0, 16), 127.5, None, OP.add)
+        tt(B("w1", 16, 272), B("tb", 16, 272), B("w0", 16, 272), OP.subtract)
+        gather("V", B("tt", 0, 1024, 4), B("w0", 16, 272), B("l2"))
+        if r == 0:
+            quant("tcq", 0, 384, B("tc"))
+        gather("A", B("tt", 1, 1024, 4), B("w1", 16, 272), B("l2"))
+        for b in range(4):
+            act(B("fo", 256 * b, 256 * b + 256), B("ps%d" % (3 + b), 0, 256), scale=1 / 32)
+        quant("ttq", 0, 256, B("tt"))
+        for k in range(2):
+            for h in range(2):
+                mm(TB[k][h], 4 * W, "ttq", 128 * h, "tcq", 4 * W * k)
+        for b in range(4):
+            mm(3 + b, 256, "eq_", 128 * b, px, 0)
+
+        def digits(a, b, first):
+            ev = B("so", W * a + 46, W * b, W)
+            if first:
+                ts(B("dah", a, b), ev, KE16, KE16, OP.add, OP.subtract)
+                ts(B("dhh", a, b), ev, KE256, KE256, OP.add, OP.subtract)
+            else:
+                tt(B("ddb", a, b), ev, B("dah", a, b), OP.subtract)
+                tt(B("dda", a, b), B("dah", a, b), B("dhh", a, b), OP.subtract)
+
+        def spread(k0, k1):
+            for kk in range(k0, k1):
+                for d in (1, 0):
+                    for h in range(2):
+                        o = B("ex", 64 * kk + 2 * h + d, 64 * kk + 64, 4)
+                        col = B(("dda", "ddb")[d], 2 * kk + h, 2 * kk + h + 1)
+                        if kk > 5 and h == 1:
+                            ts(o, B("mask16"), col, None, OP.mult)
+                        else:
+                            act(o, B("mask16"), scale=col)
+        batch = {2: (0, 2), 4: (2, 4), 6: (4, 6), 7: (6, 8)}
+        for k in range(8):
+            for h in range(2):
+                c = W * (2 * k + h)
+                scan(B("so", c, c + W - 1), B("ps%d" % TB[k // 4][h], W * (k % 4), W * (k % 4) + W - 1), B("fb", c, c + W - 1), -100.0,
+                     OP.subtract, OP.min)
+            if k in batch:
+                digits(2 * batch[k][0], 2 * batch[k][1], True)
+            for h in range(2):
+                c = W * (2 * k + h)
+                if k < 7:
+                    tt(B("fb", c + 2 * W, c + 2 * W + 15, 2), B("fb", c, c + 15, 2), B("so", c + 31, c + 46, 2), OP.is_ge)
+            if k in batch:
+                digits(2 * batch[k][0], 2 * batch[k][1], False)
+                spread(*batch[k])
+        for b in range(4):
+            act(B("fp", 256 * b, 256 * b + 256), B("ps%d" % (3 + b), 0, 256), scale=1 / 32)
+        quant("exq", 0, 128, B("ex"))
+        mm(7, 128, "exq", 0, "mvq", 0)
+        ts(B(lc), B("ps7", 0, 16), 127.5, None, OP.add)
+        send([(B(plc), B(lc))], dst, "rl%d" % r, "ll%d" % r)
+        if r == 1:
+            dma("S", T.vt[:], T.v[:], [B("vt")], [B(lc)])
+        for h in range(2):
+            for b in range(4):
+                mm(HB[h][b], 128, "eq_", 128 * b, xq, 128 * h, True, False)
+        gather("A", B("crow"), B("kk"), B(lc))
+        if r == 0:
+            fill(B("fz"), 1.0)
+            ts(B("fz", 0, 1024, 256), B("fz", 0, 1024, 256), 0.0, None, OP.mult)
+
+        def taken(q):
+            for m in range(4 * q, 4 * q + 4):
+                ts(B("eq", 256 * m, 256 * m + 256), B("crow"), B("kcol", m, m + 1), None, OP.is_equal)
+            scan(B("pm", 1024 * q, 1024 * q + 1024), B("fz"), B("eq", 1024 * q, 1024 * q + 1024), 0.0, OP.mult, OP.max)
+
+        def counted(m0, m1):
+            for m in range(m0, m1):
+                act(B("junk", 256 * m, 256 * m + 256), B("pm", 256 * m, 256 * m + 256), accum=B("acc2", m, m + 1))
+        taken(0)
+        taken(1)
+        counted(0, 2)
+        for h in range(2):
+            for b in range(4):
+                gather("VVAA"[b], B("zt", 512 * h + b, 512 * h + 512, 4), B("fp", 256 * b, 256 * b + 256), B(plc, 8 * h, 8 * h + 8))
+            quant(zq, 128 * h, 128, B("zt", 512 * h, 512 * h + 512))
+            for b in range(4):
+                mm(HB[h][b], 128, "wq", 128 * b, zq, 128 * h, False, True)
+        for h in range(2):
+            for b in range(4):
+                o, i = B("yt", 512 * h + b, 512 * h + 512, 4), B("ps%d" % HB[h][b], 0, 128)
+                if b % 2 == 0:
+                    ts(o, i, 0.03125, None, OP.mult)
+                else:
+                    act(o, i, scale=0.03125)
+            quant(yq, 128 * h, 128, B("yt", 512 * h, 512 * h + 512))
+            q = (128 * h, 128 * h + 128)
+            send([(U8(B(py, *q)), U8(B(yq, *q))), (B(py + "S", *q), B(yq + "S", *q))], dst, "ry%d%d" % (r, h), "ly%d%d" % (r, h))
+        counted(2, 8)
+        taken(2)
+        counted(8, 12)
+        taken(3)
+        counted(12, 14)
+        for m in range(14, 16):
+            o, i = B("acc2", m, m + 1), B("pm", 256 * m, 256 * m + 256)
+            run("V", lambda e: e.tensor_reduce(o[0], i[0], AxisListType.X, OP.add), [o], [i])
+        ts(B("l4"), B("acc2"), -1.0, 256.0, OP.mult, OP.add)
+        if r == 1:
+            ts(B("srow"), B("crow"), 127.5, None, OP.add)
+            dma("S", T.src[:], T.srow[0:128:16, :], [], [B("srow")])
+            quant("vq", 0, 128, B("vt"))
+        for h in range(2):
+            for b in range(4):
+                mm(HB[h][b], 128, "eq_", 128 * b, py, 128 * h)
+        for h in range(2):
+            for b in range(4):
+                o, i = B("dy", 272 * b + 128 * h, 272 * b + 128 * h + 128), B("ps%d" % HB[h][b], 0, 128)
+                if b % 2 == 0:
+                    ts(o, i, 1 / 32, None, OP.mult)
+                else:
+                    act(o, i, scale=1 / 32)
+        xn, l4 = "x%d" % (r + 1), B("l4")
+        for b in range(4):
+            win = B("dy", 272 * b, 272 * b + 272)
+            w, o, f = win[0].indirect(l4[0]), B(xn, b, 1024, 4), B("fo", 256 * b, 256 * b + 256)
+            run("V", lambda e: e.tensor_tensor(o[0], w, f[0], OP.add), [o], [win, l4, f])
+        quant("xq" + L[r + 1], 0, 256, B(xn))
+    dma("S", T.oc[:], T.xqc[:].bitcast(dt.uint8), [], [B("xqc")])
+    for k in range(4):
+        dma("A", T.osc[4 * k:4 * k + 4, :], T.xqcS[32 * k:32 * k + 4, :], [], [B("xqcS")])
+    mm(2, 256, "vq", 0, "xqc", 0)
+    cp(B("yout"), B("ps2", 0, 256))
+    dma("S", T.y[:], T.yout[:], [], [B("yout")])
+    for q in ("V", "A", "P", "G"):
+        need("G", q, cnt[q])
+    for sem, val in final.items():
+        need("G", sem, val)

@@ -5,10 +5,16 @@ from concourse.mybir import dt, AluOpType, AxisListType, ActivationFunctionType
 OP = AluOpType
 AF = ActivationFunctionType
 BIG = 8e28
-K16 = 201326592.0
-EPS = 2.0 ** -19
-KE16, KE256 = 384.0, 6144.0
-W = 48
+
+
+def grid(step):
+    return 1.5 * 2.0 ** 23 * step
+
+
+EPS = 2.0 ** -9
+COL = 2.0 ** -13
+W = 34
+NA = 7
 STEP = [1, 2]
 
 F4, BF, I4, U2, CODE, U1 = "float32", "bfloat16", "int32", "uint16", "float8_e4m3fn_x4", "uint8"
@@ -28,26 +34,28 @@ def _pieces(base, dtype, **bufs):
     SCRATCH[base] = ("sbuf", [128, at], dtype)
 
 
-_add(BF, x0=1024, x1=1024, x2=1024, ut=512, vt=512, zz=512, kk=256, sg=256, cw=512, rot=512, ebig=2048, tc=1536,
-     mv=512, bt=1024, zs=272, z=256, d0=272, d1=272, tb=272, w0=272, w1=272, rt=512, tt=1024, ex=512, et=256, ets=256,
-     cm=4096, fo=1024, fp=1024, zt=1024, yt=1024, dy=1088, crow=256, eq=4096, pm=4096, fz=1024)
-_add(F4, ikf=256, maskd=256, hd=256, kz=256, kbi=256, lb=512, ab=256, sd=256, sx=256, junk=4096, fb=16 * W, so=16 * W,
-     srow=256, yout=256)
-_pieces("f4s", F4, pf=16, mask16=16, kcol=16, cb0=16, cb1=16, cb2=16, gm=8, ig8=8, iposf=50, nega=50, negb=50, negc=50, sig=48,
-        wt0=8, wt1=8, pos2=48, pos3=48, fbp=48, fbz=48, kai2=16, acc=16, acc2=16, rl=16, dah=16, dhh=16, ddb=16, dda=16)
-_pieces("i4s", I4, ip=1, pi=8, ikp=256, iposi=48, iu=8, kai=256, im=16)
-_pieces("u2s", U2, ul=8, l1=16, l2=16, l4=16)
-_add(U2, lc0=16, lc1=16, plc0=16, plc1=16)
+_add(BF, x0=1024, x1=1024, x2=1024, ut=512, vt=512, zz=512, wk=1024, ex=512, ct=1600, ebig=2112, kbi=288, ramp=272, ones=272, t256=288, t512=288,
+     mh=272, kt=272, sg=256, et=256, ets=256, sn=4096, cm=4096, cs=4096, fo=1024, fp=1024, fs=1088, zt=1024, yt=1024, dy=1088,
+     fb=14 * W, av=272, s1=272, s2=256, rowt=272, rowk=256, s3=256, orow=272)
+_add(F4, maskd=256, hd=256, kz=256, lb=512, ab=256, sd=256, sx=256, z=256, zs=272, tb=272, sh=272, so=14 * W, key=256, srow=256, yout=256)
+_pieces("f4s", F4, pf=16, cb0=16, cb1=16, cb2=16, gm=8, ig8=8, a16=16, sig=W, mneg=16, acc=16, rl=16, r16=17, r256=17)
+_pieces("i4s", I4, ip=1, pi=8, iu=8)
+_pieces("u2s", U2, ul=8, l1=16, l2=16, l3=17, l4=16, lt=16)
+_add(U2, lq0=16, lq1=16, plq0=16, plq1=16, lo0=32, lo1=32, plo0=32, plo1=32)
 for _n, _w in (("uq", 128), ("ur", 128), ("vq", 128), ("wq", 512), ("xqa", 256), ("xqb", 256), ("xqc", 256), ("pxa", 256), ("pxb", 256),
-               ("cwq", 128), ("rotq", 128), ("eq_", 512), ("tcq", 384), ("mvq", 128), ("btq", 256), ("rtq", 128), ("ttq", 256),
+               ("ctq", 400), ("eq_", 528), ("btq", 256), ("rtq", 128), ("ttq", 256), ("r2q", 128),
                ("exq", 128), ("zqa", 256), ("zqb", 256), ("yqa", 256), ("yqb", 256), ("pya", 256), ("pyb", 256)):
     SCRATCH[_n] = ("sbuf", [128, _w], CODE)
     SCRATCH[_n + "S"] = ("sbuf", [128, _w], U1)
 for _k in range(8):
     SCRATCH["ps%d" % _k] = ("psum", [128, 512], F4)
+UNP = (272, 400, 0, 128)
+ROT = (16, 144)
+MV, TC, CW = 0, 16, 272
 
 NDMA = 16
-SEMAPHORES = (["V", "A", "P", "G"] + ["d%d" % k for k in range(NDMA)] + [k + "%d" % r for k in ("rx", "lx", "rl", "ll") for r in (0, 1)]
+SEMAPHORES = (["V", "A", "P", "G"] + ["d%d" % k for k in range(NDMA)]
+              + [k + "%d" % r for k in ("rx", "lx", "rl", "ll", "ro", "lo") for r in (0, 1)]
               + [k + "%d%d" % (r, h) for k in ("ry", "ly") for r in (0, 1) for h in (0, 1)])
 
 
@@ -122,19 +130,25 @@ def rank_program(g, core, T, topo):
         final[sem] = 16
         note(q, ins, outs, sem, 16)
 
-    def ts(out, a, s1, s2, op0, op1=None):
-        ins = [a] + [s for s in (s1, s2) if isinstance(s, tuple)]
+    def picked(a, off):
+        return (a[0], [a]) if off is None else (a[0].indirect(off[0]), [a, off])
+
+    def ts(out, a, s1, s2, op0, op1=None, off=None):
+        src, ins = picked(a, off)
+        ins = ins + [s for s in (s1, s2) if isinstance(s, tuple)]
         v1, v2 = [s[0] if isinstance(s, tuple) else s for s in (s1, s2)]
         if op1 is None:
-            run("V", lambda e: e.tensor_scalar(out[0], a[0], v1, None, op0), [out], ins)
+            run("V", lambda e: e.tensor_scalar(out[0], src, v1, None, op0), [out], ins)
         else:
-            run("V", lambda e: e.tensor_scalar(out[0], a[0], v1, v2, op0, op1), [out], ins)
+            run("V", lambda e: e.tensor_scalar(out[0], src, v1, v2, op0, op1), [out], ins)
 
-    def tt(out, a, b, op):
-        run("V", lambda e: e.tensor_tensor(out[0], a[0], b[0], op), [out], [a, b])
+    def tt(out, a, b, op, off=None):
+        src, ins = picked(a, off)
+        run("V", lambda e: e.tensor_tensor(out[0], src, b[0], op), [out], ins + [b])
 
-    def cp(out, a):
-        run("V", lambda e: e.tensor_copy(out[0], a[0]), [out], [a])
+    def cp(out, a, off=None):
+        src, ins = picked(a, off)
+        run("V", lambda e: e.tensor_copy(out[0], src), [out], ins)
 
     def scan(out, a, b, init, op0, op1):
         run("V", lambda e: e.tensor_tensor_scan(out[0], a[0], b[0], init, op0, op1), [out], [a, b])
@@ -142,23 +156,27 @@ def rank_program(g, core, T, topo):
     def fill(out, c):
         run("V", lambda e: e.memset(out[0], c), [out], [])
 
+    def rounded(out, a, step, off=None):
+        ts(out, a, grid(step), grid(step), OP.add, OP.subtract, off)
+
     def quant(code, a, n, tile):
         run("V", lambda e: e.quantize_mx(T[code][:, a:a + n], T[code + "S"][:, a:a + n], tile[0]),
             [B(code, a, a + n), B(code + "S", a, a + n)], [tile])
 
-    def act(out, a, func=AF.Copy, scale=1.0, bias=None, accum=None):
-        ins = [a] + [s for s in (scale,) if isinstance(s, tuple)]
+    def act(out, a, func=AF.Copy, scale=1.0, bias=None, accum=None, off=None):
+        src, ins = picked(a, off)
+        ins = ins + [s for s in (scale, bias) if isinstance(s, tuple)]
         outs = [out] + ([accum] if accum is not None else [])
         kw = {}
         if bias is not None:
-            kw["bias"] = bias
+            kw["bias"] = bias[0] if isinstance(bias, tuple) else bias
         if isinstance(scale, tuple):
             kw["scale"] = scale[0]
         elif scale != 1.0:
             kw["scale"] = scale
         if accum is not None:
             kw["accum_out"] = accum[0]
-        run("A", lambda e: e.activation(out[0], a[0], func, **kw), outs, ins)
+        run("A", lambda e: e.activation(out[0], src, func, **kw), outs, ins)
 
     def mm(bank, n, st, a, mvg, b, start=True, stop=True):
         name = "ps%d" % bank
@@ -167,12 +185,12 @@ def rank_program(g, core, T, topo):
             [B(name, 0, n)], [B(st, a, a + 128), B(st + "S", a, a + 128), B(mvg, b, b + n), B(mvg + "S", b, b + n)],
             free=() if start else (name,))
 
+    def digits(bank, views, code, stop=True):
+        mm(bank, 128, "eq_", views[0], code, 0, True, False)
+        mm(bank, 128, "eq_", views[1], code, 0, False, stop)
+
     def gather(q, out, win, off):
-        w = win[0].indirect(off[0])
-        if q == "V":
-            run("V", lambda e: e.tensor_copy(out[0], w), [out], [win, off])
-        else:
-            run("A", lambda e: e.activation(out[0], w, AF.Copy), [out], [win, off])
+        (cp if q == "V" else act)(out, win, off=off)
 
     def iota(out, pattern, base, cm):
         out = B(out) if isinstance(out, str) else out
@@ -181,8 +199,9 @@ def rank_program(g, core, T, topo):
         else:
             run("G", lambda e: e.iota(out[0], pattern, base, cm), [out], [])
 
-    def mark(out, in_, pattern, fill, base, cm):
-        run("G", lambda e: e.affine_select(out[0], in_[0], pattern, OP.not_equal, fill, base, cm), [out], [in_])
+    def unpacker(at, n, b):
+        o, i = B("ebig", 4 * at, 4 * (at + n)), B("zz", 0, 4 * n)
+        run("G", lambda e: e.affine_select(o[0], i[0], [[1, 4 * n]], OP.not_equal, 32.0, -b, -4), [o], [i])
 
     def send(parts, dst, rsem, lsem):
         engs = topo.engines(core, dst)
@@ -199,252 +218,215 @@ def rank_program(g, core, T, topo):
             note("G", [s], [], lsem, tot)
             note("R", [], [d], rsem, tot)
 
+    def own(out, row, n):
+        scan(out, B("mh", 0, n), row, 0.0, OP.add, OP.min)
+
     dma("S", T.x0[:], T.x[:], [B("x0")], [])
     dma("A", T.ut[:], T.u[:], [B("ut")], [])
-    fill(B("zz"), 0.0)
-    iota("iu", [[16, 8]], 0, 0)
     iota("ip", [[0, 1]], 0, 1)
-    iota("ikp", [[1, 256]], 128, -1)
-    iota("kbi", [[0, 16], [1, 16]], 0, 0)
-    iota("ikf", [[1, 256]], 0, 0)
-    iota("cb0", [[0, 8], [-1024, 2]], 512, 0)
-    iota("cb1", [[0, 4], [-1024, 2], [0, 2]], 512, 0)
-    iota("cb2", [[0, 2], [-1024, 2], [0, 4]], 512, 0)
+    iota("kbi", [[0, 18], [1, 16]], 0, 0)
+    iota("iu", [[16, 8]], 0, 0)
     iota("ig8", [[1, 8]], 0, 0)
-    iota("iposf", [[1, 50]], -2, 0)
-    iota("iposi", [[1, 48]], 0, 0)
-    iota("im", [[16, 16]], 0, 0)
-
-    cp(B("ul"), B("iu"))
-    for name in ("cw", "bt", "mv", "rt"):
-        fill(B(name), 0.0)
+    iota("cb0", [[0, 8], [-64, 2]], 32, 0)
+    iota("cb1", [[0, 4], [-64, 2], [0, 2]], 32, 0)
+    iota("cb2", [[0, 2], [-64, 2], [0, 4]], 32, 0)
+    iota("a16", [[1, 8], [0, 2]], 0, 0)
+    iota("ramp", [[1, 272]], 0, 0)
+    fill(B("zz"), 0.0)
+    fill(B("wk"), 0.0)
     pi = lambda k: B("pi", k, k + 1)
     pf = lambda k: B("pf", k, k + 1)
     ts(pi(1), B("ip"), 15, None, OP.bitwise_and)
-    ts(pi(2), B("ip"), 7, None, OP.bitwise_and)
-    ts(pi(3), B("ip"), 4, None, OP.arith_shift_right)
-    ts(pi(4), B("ip"), 3, 1, OP.arith_shift_right, OP.bitwise_and)
-    ts(B("kai"), B("ikp"), 15, None, OP.bitwise_and)
-    cp(B("pf", 1, 5), B("pi", 1, 5))
-    ts(B("hd"), B("kbi"), 0.0, BIG, OP.is_equal, OP.mult)
-    ts(B("maskd"), B("kai"), 0.0, BIG, OP.is_gt, OP.mult)
-    ts(B("sg"), B("kbi"), 0.0, None, OP.is_gt)
-    act(B("kk"), B("ikf"), AF.Identity, bias=-127.5)
+    ts(pi(2), B("ip"), 4, None, OP.arith_shift_right)
+    fill(B("ct"), 0.0)
+    cp(B("pf", 1, 3), B("pi", 1, 3))
+    cp(B("ul"), B("iu"))
+    ts(B("maskd"), B("kbi", 0, 256), pf(1), BIG, OP.not_equal, OP.mult)
+    ts(B("sg"), B("kbi", 0, 256), 0.0, None, OP.is_gt)
+    act(B("hd"), B("sg"), AF.Identity, scale=-BIG, bias=BIG)
+    ts(B("t256"), B("kbi"), pf(1), 256.0, OP.is_equal, OP.mult)
+    act(B("t512"), B("t256"), scale=2.0)
+    for b in range(3):
+        ts(pf(8 + b), pf(1), 1.0 + b, None, OP.is_equal)
+    ts(B("gm"), B("ig8"), pf(2), None, OP.is_equal)
+    for b in range(3):
+        ts(B("cb%d" % b), B("cb%d" % b), pf(8 + b), None, OP.mult)
+    tt(B("cb0"), B("cb0"), B("cb1"), OP.add)
+    fill(B("sig"), 0.0)
+    tt(B("cb0"), B("cb0"), B("cb2"), OP.add)
+    for gg in range(8):
+        act(B("ct", 4 * CW + 64 * gg, 4 * CW + 64 * gg + 64, 4), B("cb0"), scale=B("gm", gg, gg + 1))
+    act(B("kz"), B("ramp", 0, 256), AF.Identity, scale=COL, bias=80.0 - 127.5 * COL)
     quant("xqa", 0, 256, B("x0"))
     quant("uq", 0, 128, B("ut"))
     ul = B("ul")
     run("V", lambda e: e.tensor_copy(T.ur[:].bitcast(dt.uint32), T.uq[:].bitcast(dt.uint32).indirect(ul[0])), [B("ur")], [B("uq"), ul])
     run("A", lambda e: e.activation(T.urS[:], T.uqS[:].indirect(ul[0]), AF.Copy), [B("urS")], [B("uqS"), ul])
-
-    def constants_g():
-        for b in range(4):
-            mark(B("ebig", 512 * b, 512 * b + 512), B("zz"), [[1, 512]], 32.0, -b, -4)
-        for t in (2, 3):
-            iota(B("tc", t, 1536, 4), [[0, 384]], 0, 0)
-        for t in range(2):
-            o = B("rot", t, 512, 4)
-            mark(o, B("zz", 0, 128), [[1, 128]], 1.0, 16, -1)
-            mark(o, o, [[1, 128]], 1.0, -112, -1)
-            iota(B("rot", t + 2, 512, 4), [[0, 128]], 0, 0)
-        for t in (2, 3):
-            iota(B("tt", t, 1024, 4), [[0, 256]], 0, 0)
-        for b in range(4):
-            iota(B("dy", 272 * b + 256, 272 * b + 272), [[0, 16]], 0, 0)
-
-    todo = []
-
-    def later(f, *a, **k):
-        todo.append(lambda: f(*a, **k))
+    unpacker(0, 128, 2)
+    unpacker(128, 128, 3)
+    unpacker(256, 16, 2)
 
     def constants_v():
-        for b in range(3):
-            later(ts, pf(8 + b), pf(1), 1.0 + b, None, OP.is_equal)
-        later(ts, B("gm"), B("ig8"), pf(3), None, OP.is_equal)
-        for b in range(3):
-            later(ts, B("cb%d" % b), B("cb%d" % b), pf(8 + b), None, OP.mult)
-        later(ts, pf(6), pf(4), 500.0 - 1e6, 1e6, OP.mult, OP.add)
-        later(tt, B("cb0"), B("cb0"), B("cb1"), OP.add)
-        later(ts, pf(7), pf(4), 999.0, 1.0, OP.mult, OP.add)
-        later(tt, B("cb0"), B("cb0"), B("cb2"), OP.add)
-        for gg in range(8):
-            later(act, B("cw", 64 * gg, 64 * gg + 64, 4), B("cb0"), scale=B("gm", gg, gg + 1))
-        later(ts, B("kz"), B("kk"), pf(4), 1536.0, OP.mult, OP.add)
-        later(ts, B("mask16"), B("kai2"), 0.0, None, OP.is_equal)
-        for h in range(2):
-            for d in range(2):
-                later(ts, B("mv", 32 * h + 2 * h + d, 32 * h + 32, 4), B("ig8"), pf(3), 1.0 / EPS, OP.is_equal, OP.mult)
-        later(quant, "mvq", 0, 128, B("mv"))
-        later(ts, B("kcol"), B("im"), pf(1), -127.5, OP.add, OP.add)
-        later(ts, B("pos2"), B("iposf", 2, 50), 30.5, None, OP.is_gt)
-        later(ts, B("kai", 0, 48), B("iposi"), 1, None, OP.bitwise_and)
-        later(ts, pf(11), pf(2), 2.0, None, OP.mult)
-        later(tt, B("pos3"), B("pos2"), B("kai", 0, 48), OP.max)
-        later(ts, pf(12), pf(2), -2.0, 30.0, OP.mult, OP.add)
-        later(ts, B("fbp"), B("pos3"), 1e6, 7936 * EPS, OP.mult, OP.add)
-        later(ts, pf(13), pf(2), 2.0, 30.0, OP.mult, OP.add)
-        later(cp, B("fbz"), B("fbp"))
-        later(ts, B("nega"), B("iposf"), pf(11), None, OP.is_equal)
-        later(ts, B("fbz", 0, 15, 2), B("fbz", 0, 15, 2), 0.0, None, OP.mult)
-        later(ts, B("negb"), B("iposf"), pf(12), None, OP.is_equal)
-        later(ts, B("negc"), B("iposf"), pf(13), None, OP.is_equal)
-        later(tt, B("nega"), B("nega"), B("negb"), OP.max)
-        later(ts, pf(14), pf(4), EPS - 512 * EPS, 512 * EPS, OP.mult, OP.add)
-        later(tt, B("nega"), B("nega"), B("negc"), OP.max)
-        later(ts, pf(15), pf(4), EPS, None, OP.mult)
-        later(tt, B("sig"), B("nega", 0, 48), B("nega", 2, 50), OP.subtract)
-        later(ts, B("wt0"), B("ig8"), pf(3), pf(14), OP.is_equal, OP.mult)
-        later(ts, B("wt1"), B("ig8"), pf(3), pf(15), OP.is_equal, OP.mult)
+        ts(B("sig", 0, 16), B("a16"), pf(1), -EPS, OP.is_equal, OP.mult)
+        ts(B("sig", 17, 33), B("a16"), pf(1), EPS, OP.is_equal, OP.mult)
+        ts(B("mneg"), B("kbi", 0, 16), pf(1), 15 / 16, OP.is_equal, OP.mult)
+        ts(pf(3), pf(1), 15.0, 256.0, OP.is_lt, OP.mult)
+        fill(B("ones"), 1.0)
+        fill(B("fb"), 1.0)
+        fill(B("ex"), 0.0)
+        ts(B("mneg"), B("mneg"), -1.0, None, OP.add)
+        ts(B("fb", W - 1, 14 * W, W), B("fb", W - 1, 14 * W, W), EPS, None, OP.mult)
 
     def constants_a():
-        for gg in range(8):
-            for t in range(2):
-                act(B("tc", 4 * W * gg + t, 4 * W * gg + 4 * W, 4), B("sig"), scale=B("wt%d" % t, gg, gg + 1))
-        for c in range(16):
-            act(B("fb", W * c, W * c + W), B("fbz" if c < 2 else "fbp"))
+        act(B("ct", 4 * TC + 1, 4 * TC + 64, 4), B("sig", 17, 33), scale=B("gm", 0, 1))
+        for gg in range(1, 8):
+            at = 4 * (TC + 16 + W * (gg - 1))
+            act(B("ct", at + 1, at + 4 * W, 4), B("sig"), scale=B("gm", gg, gg + 1))
+        for h in range(2):
+            act(B("ct", 4 * MV + 32 * h + h, 4 * MV + 32 * h + 32, 4), B("gm"), scale=-32 * 16 / EPS)
 
-    TB = ((0, 1), (2, 7))
     HB = ((3, 4, 5, 6), (0, 1, 2, 7))
     for r in range(2):
         dst = T.cores[rank ^ STEP[r]]
         L = "abc"
         xq, px, zq, yq, py = "xq" + L[r], "px" + L[r], "zq" + L[r], "yq" + L[r], "py" + L[r]
-        lc, plc = "lc%d" % r, "plc%d" % r
+        lq, plq, lo, plo = "lq%d" % r, "plq%d" % r, "lo%d" % r, "plo%d" % r
         send([(U8(B(px)), U8(B(xq))), (B(px + "S"), B(xq + "S"))], dst, "rx%d" % r, "lx%d" % r)
         if r == 0:
-            constants_g()
+            unpacker(UNP[0], 128, 0)
+            unpacker(UNP[1], 128, 1)
+            for b in range(4):
+                iota(B("dy", 272 * b + 256, 272 * b + 272), [[0, 16]], 0, 0)
         mm(1, 256, "ur", 0, xq, 0)
         mm(0, 256, "ur", 0, xq, 0)
         mm(2, 256, "uq", 0, xq, 0)
         act(B("ab"), B("ps0", 0, 256), AF.Abs, scale=0.6 * 2.0 ** -23, bias=2.0 ** -122)
         act(B("lb", 0, 256), B("ps0", 0, 256))
-        act(B("bt", 0, 1024, 4), B("ps2", 0, 256), AF.Sign, bias=-2.0 ** -100)
+        act(B("wk", 0, 1024, 4), B("ps2", 0, 256), AF.Sign, bias=-2.0 ** -100)
         if r == 0:
-            ts(B("kai2"), B("kai", 0, 16), 1.0, None, OP.mult)
             constants_v()
         tt(B("sd"), B("ps1", 0, 256), B("maskd"), OP.add)
         scan(B("sx"), B("hd"), B("sd"), 0.0, OP.add, OP.min)
         tt(B("lb", 256, 512), B("ps1", 0, 256), B("ab"), OP.add)
-        for m in range(16):
-            ts(B("cm", 256 * m, 256 * m + 256), B("lb", 16 * m + 16, 16 * m + 272), B("sx", 16 * m + 15, 16 * m + 16), None, OP.is_le)
-            act(B("junk", 256 * m, 256 * m + 256), B("cm", 256 * m, 256 * m + 256), AF.Identity, bias=-257 / 512, accum=B("acc", m, m + 1))
-            for f in todo[:5]:
-                f()
-            del todo[:5]
-            if m == (5 if r == 0 else 2):
+        row = lambda m: B("lb", 16 * m + 16, 16 * m + 272)
+        mine = lambda m: B("sx", 16 * m + 15, 16 * m + 16)
+        blk = lambda name, m, n=1: B(name, 256 * m, 256 * (m + n))
+        for m in range(NA):
+            act(blk("sn", m), row(m), AF.Sign, scale=-1.0, bias=mine(m))
+            if m:
+                act(blk("cm", m - 1), blk("sn", m - 1), AF.Relu, scale=-1.0, accum=B("acc", m - 1, m))
+        act(blk("cm", NA - 1), blk("sn", NA - 1), AF.Relu, scale=-1.0, accum=B("acc", NA - 1, NA))
+        if r == 0:
+            fill(B("sn", 256 * NA, 256 * NA + 768), 1.0)
+            ts(B("sn", 256 * NA, 256 * NA + 768, 256), B("sn", 256 * NA, 256 * NA + 768, 256), 0.0, None, OP.mult)
+        for m0 in range(NA, 16, 3):
+            n = min(3, 16 - m0)
+            for m in range(m0, m0 + n):
+                ts(blk("cm", m), row(m), mine(m), None, OP.is_gt)
+            if m0 == NA:
                 if r == 0:
-                    quant("cwq", 0, 128, B("cw"))
-                quant("btq", 0, 256, B("bt"))
-                mm(2, 256, "cwq", 0, "btq", 0)
-        tt(B("et"), B("ps1", 0, 256), B("sx"), OP.is_equal)
-        tt(B("z"), B("ps2", 0, 256), B("kz"), OP.add)
-        scan(B("ets"), B("sg"), B("et"), 0.0, OP.mult, OP.add)
-        for f in todo:
-            f()
-        del todo[:]
+                    quant("ctq", CW, 128, B("ct", 4 * CW, 4 * CW + 512))
+                quant("btq", 0, 256, B("wk"))
+                mm(2, 256, "ctq", CW, "btq", 0)
+                tt(B("et"), B("ps1", 0, 256), B("sx"), OP.is_equal)
+            elif m0 == NA + 3:
+                scan(B("ets"), B("sg"), B("et"), 0.0, OP.mult, OP.add)
+                if r == 0:
+                    quant("eq_", 0, 272, B("ebig", 0, 1088))
+            else:
+                tt(B("z"), B("ps2", 0, 256), B("kz"), OP.add)
+            scan(blk("cs", m0, n), blk("sn", NA, n), blk("cm", m0, n), 0.0, OP.mult, OP.add)
+        tt(B("rl", 0, NA), B("ets", 15, 16 * NA, 16), B("acc", 0, NA), OP.subtract)
+        tt(B("rl", NA, 16), B("ets", 16 * NA + 15, 256, 16), B("cs", 256 * NA + 255, 4096, 256), OP.subtract)
         if r == 0:
             constants_a()
-            quant("eq_", 0, 512, B("ebig"))
             dma("S", T.wq[:].bitcast(dt.uint8), T.wc[:], [B("wq")], [B("ets")])
             dma("S", T.wqS[:], T.ws[:], [B("wqS")], [B("ets")])
-        for b in range(4):
-            mm(3 + b, 256, "eq_", 128 * b, xq, 0)
-        tt(B("rl"), B("acc"), B("ets", 15, 256, 16), OP.add)
-        ts(B("l1"), B("rl"), 127.5, None, OP.add)
-        ts(B("rt", 0, 64, 4), B("rl"), K16, K16, OP.add, OP.subtract)
+        ts(B("l1"), B("rl"), 255.0, None, OP.add)
+        rounded(B("wk", 2, 64, 4), B("rl"), 16)
+        tt(B("wk", 3, 64, 4), B("rl"), B("wk", 2, 64, 4), OP.subtract)
+        quant("rtq", 0, 128, B("wk", 0, 512))
+        digits(7, ROT, "rtq")
+        digits(0, ROT, "rtq", False)
         l1 = B("l1")
         run("V", lambda e: e.tensor_copy(T.zs[:, 16:272].indirect(l1[0]), T.z[:]), [B("zs", 16, 272)], [B("z"), l1])
-        tt(B("rt", 1, 64, 4), B("rl"), B("rt", 0, 64, 4), OP.subtract)
+        ts(B("l2"), B("ps7", 0, 16), 1 / 32, 255.0, OP.mult, OP.add)
         cp(B("zs", 0, 16), B("zs", 256, 272))
         if r == 0:
-            quant("rotq", 0, 128, B("rot"))
-        quant("rtq", 0, 128, B("rt"))
-        mm(7, 128, "rotq", 0, "rtq", 0)
-        ts(B("d0"), B("zs"), pf(6), pf(7), OP.is_lt, OP.mult)
-        ts(B("d1"), B("zs"), K16, K16, OP.add, OP.subtract)
-        scan(B("tb"), B("d0"), B("zs"), 64.0, OP.add, OP.min)
-        scan(B("w0"), B("d0"), B("d1"), 64.0, OP.add, OP.min)
-        ts(B("l2"), B("ps7", 0, 16), 127.5, None, OP.add)
-        tt(B("w1", 16, 272), B("tb", 16, 272), B("w0", 16, 272), OP.subtract)
-        gather("V", B("tt", 0, 1024, 4), B("w0", 16, 272), B("l2"))
-        if r == 0:
-            quant("tcq", 0, 384, B("tc"))
-        gather("A", B("tt", 1, 1024, 4), B("w1", 16, 272), B("l2"))
+            quant("eq_", 272, 256, B("ebig", 1088, 2112))
+        for b in range(4):
+            mm(3 + b, 256, "eq_", UNP[b], xq, 0)
         for b in range(4):
             act(B("fo", 256 * b, 256 * b + 256), B("ps%d" % (3 + b), 0, 256), scale=1 / 32)
-        quant("ttq", 0, 256, B("tt"))
-        for k in range(2):
-            for h in range(2):
-                mm(TB[k][h], 4 * W, "ttq", 128 * h, "tcq", 4 * W * k)
-        for b in range(4):
-            mm(3 + b, 256, "eq_", 128 * b, px, 0)
-
-        def digits(a, b, first):
-            ev = B("so", W * a + 46, W * b, W)
-            if first:
-                ts(B("dah", a, b), ev, KE16, KE16, OP.add, OP.subtract)
-                ts(B("dhh", a, b), ev, KE256, KE256, OP.add, OP.subtract)
-            else:
-                tt(B("ddb", a, b), ev, B("dah", a, b), OP.subtract)
-                tt(B("dda", a, b), B("dah", a, b), B("dhh", a, b), OP.subtract)
-
-        def spread(k0, k1):
-            for kk in range(k0, k1):
-                for d in (1, 0):
-                    for h in range(2):
-                        o = B("ex", 64 * kk + 2 * h + d, 64 * kk + 64, 4)
-                        col = B(("dda", "ddb")[d], 2 * kk + h, 2 * kk + h + 1)
-                        if kk > 5 and h == 1:
-                            ts(o, B("mask16"), col, None, OP.mult)
-                        else:
-                            act(o, B("mask16"), scale=col)
-        batch = {2: (0, 2), 4: (2, 4), 6: (4, 6), 7: (6, 8)}
-        for k in range(8):
-            for h in range(2):
-                c = W * (2 * k + h)
-                scan(B("so", c, c + W - 1), B("ps%d" % TB[k // 4][h], W * (k % 4), W * (k % 4) + W - 1), B("fb", c, c + W - 1), -100.0,
-                     OP.subtract, OP.min)
-            if k in batch:
-                digits(2 * batch[k][0], 2 * batch[k][1], True)
-            for h in range(2):
-                c = W * (2 * k + h)
-                if k < 7:
-                    tt(B("fb", c + 2 * W, c + 2 * W + 15, 2), B("fb", c, c + 15, 2), B("so", c + 31, c + 46, 2), OP.is_ge)
-            if k in batch:
-                digits(2 * batch[k][0], 2 * batch[k][1], False)
-                spread(*batch[k])
-        for b in range(4):
-            act(B("fp", 256 * b, 256 * b + 256), B("ps%d" % (3 + b), 0, 256), scale=1 / 32)
-        quant("exq", 0, 128, B("ex"))
-        mm(7, 128, "exq", 0, "mvq", 0)
-        ts(B(lc), B("ps7", 0, 16), 127.5, None, OP.add)
-        send([(B(plc), B(lc))], dst, "rl%d" % r, "ll%d" % r)
-        if r == 1:
-            dma("S", T.vt[:], T.v[:], [B("vt")], [B(lc)])
-        for h in range(2):
-            for b in range(4):
-                mm(HB[h][b], 128, "eq_", 128 * b, xq, 128 * h, True, False)
-        gather("A", B("crow"), B("kk"), B(lc))
+        scan(B("tb"), B("ones"), B("zs"), 48.0, OP.add, OP.min)
         if r == 0:
-            fill(B("fz"), 1.0)
-            ts(B("fz", 0, 1024, 256), B("fz", 0, 1024, 256), 0.0, None, OP.mult)
-
-        def taken(q):
-            for m in range(4 * q, 4 * q + 4):
-                ts(B("eq", 256 * m, 256 * m + 256), B("crow"), B("kcol", m, m + 1), None, OP.is_equal)
-            scan(B("pm", 1024 * q, 1024 * q + 1024), B("fz"), B("eq", 1024 * q, 1024 * q + 1024), 0.0, OP.mult, OP.max)
-
-        def counted(m0, m1):
-            for m in range(m0, m1):
-                act(B("junk", 256 * m, 256 * m + 256), B("pm", 256 * m, 256 * m + 256), accum=B("acc2", m, m + 1))
-        taken(0)
-        taken(1)
-        counted(0, 2)
+            quant("ctq", 0, CW, B("ct", 0, 4 * CW))
+        rounded(B("wk", 1, 1024, 4), B("tb", 16, 272), 1, off=B("l2"))
+        if r == 0:
+            tt(B("mh"), B("t512", 16, 288), B("t256", 15, 287), OP.subtract)
+        quant("ttq", 0, 256, B("wk"))
+        for h in range(2):
+            mm(1 + h, 256, "ttq", 128 * h, "ctq", TC)
+        for b in range(4):
+            mm(3 + b, 256, "eq_", UNP[b], px, 0)
+        own(B("sh"), B("zs"), 272)
+        ends = B("sh", 15, 272, 16)
+        rounded(B("r16"), ends, 16 * COL)
+        rounded(B("r256"), ends, 256 * COL)
+        tt(B("ex", 3, 68, 4), ends, B("r16"), OP.subtract)
+        tt(B("ex", 2, 68, 4), B("r16"), B("r256"), OP.subtract)
+        at = lambda k, h: W * (2 * (k - 1) + h)
+        for h in range(2):
+            ts(B("fb", at(1, h), at(1, h) + 16, 2), B("ps%d" % (1 + h), 0, 16, 2), -15.5 * EPS, None, OP.is_le)
+        quant("r2q", 0, 128, B("ex"))
+        digits(7, UNP[2:], "r2q")
+        for k in range(1, 8):
+            for h in range(2):
+                c, p = at(k, h), 16 + W * (k - 1)
+                scan(B("so", c, c + W), B("ps%d" % (1 + h), p, p + W), B("fb", c, c + W), EPS / 128, OP.subtract, OP.min)
+            for h in range(2):
+                c = at(k, h)
+                if k < 7:
+                    tt(B("fb", c + 2 * W, c + 2 * W + 16, 2), B("fb", c, c + 16, 2), B("so", c + 17, c + 33, 2), OP.is_ge)
+            if k == 1:
+                ts(B(lo, 0, 18), B("ps7", 0, 18), 1 / (32 * COL), 127.5, OP.mult, OP.add)
+                send([(B(plo, 0, 18), B(lo, 0, 18))], dst, "ro%d" % r, "lo%d" % r)
+                digits(7, ROT, "r2q")
+            if k == 3:
+                ts(B("l3"), B("ps7", 0, 17), 1 / (32 * COL), 127.5, OP.mult, OP.add)
+            if k <= 4:
+                b = k - 1
+                act(B("fp", 256 * b, 256 * b + 256), B("ps%d" % (3 + b), 0, 256), scale=1 / 32)
+            for h in range(2):
+                c = at(k, h)
+                act(B("ex", 64 * k + h, 64 * k + 64, 4), B("mneg"), AF.Relu, scale=B("so", c + 15, c + 16), bias=B("so", c + 33, c + 34))
+        quant("exq", 0, 128, B("ex"))
+        mm(0, 128, "exq", 0, "ctq", MV, False, True)
+        ts(B(lq), B("ps0", 0, 16), 1 / 32, 271.25, OP.mult, OP.add)
+        send([(B(plq), B(lq))], dst, "rl%d" % r, "ll%d" % r)
+        if r == 1:
+            dma("S", T.vt[:], T.v[:], [B("vt")], [B(lq)])
+        else:
+            act(B("kt"), B("kbi", 0, 272), scale=1024.0)
+            ts(pf(4), pf(1), -1024.0, None, OP.mult)
         for h in range(2):
             for b in range(4):
-                gather("VVAA"[b], B("zt", 512 * h + b, 512 * h + 512, 4), B("fp", 256 * b, 256 * b + 256), B(plc, 8 * h, 8 * h + 8))
+                mm(HB[h][b], 128, "eq_", UNP[b], xq, 128 * h, True, False)
+        for b in (2, 3):
+            gather("A", B("fs", 272 * b, 272 * b + 272), B("fp", 256 * b, 256 * b + 256), B(plo, 0, 17))
+        tt(B("key"), B("kt"), B("ramp", 0, 256), OP.add, off=B(lq))
+        act(B("av"), B("key"), AF.Abs, bias=pf(4), off=B("l3"))
+        for b in (0, 1):
+            gather("V", B("fs", 272 * b, 272 * b + 272), B("fp", 256 * b, 256 * b + 256), B(plo, 0, 17))
+        scan(B("s1"), B("t256", 0, 272), B("av"), 256.0, OP.max, OP.min)
+        own(B("s2"), B("s1", 15, 271), 256)
+        for h in range(2):
+            for b in range(4):
+                gather("VVAA"[b], B("zt", 512 * h + b, 512 * h + 512, 4), B("fs", 272 * b, 272 * b + 272), B(plq, 8 * h, 8 * h + 8))
             quant(zq, 128 * h, 128, B("zt", 512 * h, 512 * h + 512))
             for b in range(4):
                 mm(HB[h][b], 128, "wq", 128 * b, zq, 128 * h, False, True)
+        ts(B("lt"), B("s2", 15, 256, 16), pf(3), None, OP.add)
         for h in range(2):
             for b in range(4):
                 o, i = B("yt", 512 * h + b, 512 * h + 512, 4), B("ps%d" % HB[h][b], 0, 128)
@@ -455,22 +437,19 @@ def rank_program(g, core, T, topo):
             quant(yq, 128 * h, 128, B("yt", 512 * h, 512 * h + 512))
             q = (128 * h, 128 * h + 128)
             send([(U8(B(py, *q)), U8(B(yq, *q))), (B(py + "S", *q), B(yq + "S", *q))], dst, "ry%d%d" % (r, h), "ly%d%d" % (r, h))
-        counted(2, 8)
-        taken(2)
-        counted(8, 12)
-        taken(3)
-        counted(12, 14)
-        for m in range(14, 16):
-            o, i = B("acc2", m, m + 1), B("pm", 256 * m, 256 * m + 256)
-            run("V", lambda e: e.tensor_reduce(o[0], i[0], AxisListType.X, OP.add), [o], [i])
-        ts(B("l4"), B("acc2"), -1.0, 256.0, OP.mult, OP.add)
+        gather("A", B("rowt", 0, 256), B("ramp"), B("lt"))
+        act(B("rowt", 256, 272), B("rowt", 0, 16))
+        gather("A", B("rowk"), B("rowt", 16, 272), l1)
+        own(B("s3"), B("rowk"), 256)
+        ts(B("l4"), B("s3", 15, 256, 16), pf(3), None, OP.add)
         if r == 1:
-            ts(B("srow"), B("crow"), 127.5, None, OP.add)
+            gather("A", B("orow"), B("ramp"), B(lo, 0, 17))
+            gather("A", B("srow"), B("orow"), B(lq))
             dma("S", T.src[:], T.srow[0:128:16, :], [], [B("srow")])
             quant("vq", 0, 128, B("vt"))
         for h in range(2):
             for b in range(4):
-                mm(HB[h][b], 128, "eq_", 128 * b, py, 128 * h)
+                mm(HB[h][b], 128, "eq_", UNP[b], py, 128 * h)
         for h in range(2):
             for b in range(4):
                 o, i = B("dy", 272 * b + 128 * h, 272 * b + 128 * h + 128), B("ps%d" % HB[h][b], 0, 128)
@@ -478,11 +457,9 @@ def rank_program(g, core, T, topo):
                     ts(o, i, 1 / 32, None, OP.mult)
                 else:
                     act(o, i, scale=1 / 32)
-        xn, l4 = "x%d" % (r + 1), B("l4")
+        xn = "x%d" % (r + 1)
         for b in range(4):
-            win = B("dy", 272 * b, 272 * b + 272)
-            w, o, f = win[0].indirect(l4[0]), B(xn, b, 1024, 4), B("fo", 256 * b, 256 * b + 256)
-            run("V", lambda e: e.tensor_tensor(o[0], w, f[0], OP.add), [o], [win, l4, f])
+            tt(B(xn, b, 1024, 4), B("dy", 272 * b, 272 * b + 272), B("fo", 256 * b, 256 * b + 256), OP.add, off=B("l4"))
         quant("xq" + L[r + 1], 0, 256, B(xn))
     dma("S", T.oc[:], T.xqc[:].bitcast(dt.uint8), [], [B("xqc")])
     for k in range(4):

@@ -4,7 +4,7 @@ from concourse.mybir import dt, AluOpType, AxisListType, ActivationFunctionType
 
 OP = AluOpType
 AF = ActivationFunctionType
-BIG = 8e28
+BIG = 2.0 ** 90
 
 
 def grid(step):
@@ -13,7 +13,7 @@ def grid(step):
 
 EPS = 2.0 ** -9
 COL = 2.0 ** -13
-W = 34
+W, H1, WS = 70, 36, 72
 NA = 7
 STEP = [1, 2]
 
@@ -34,16 +34,16 @@ def _pieces(base, dtype, **bufs):
     SCRATCH[base] = ("sbuf", [128, at], dtype)
 
 
-_add(BF, x0=1024, x1=1024, x2=1024, ut=512, vt=512, zz=512, wk=1024, ex=512, ct=1600, ebig=2112, kbi=288, ramp=272, ones=272, t256=288, t512=288,
-     mh=272, kt=272, sg=256, et=256, ets=256, sn=4096, cm=4096, cs=4096, fo=1024, fp=1024, fs=1088, zt=1024, yt=1024, dy=1088,
-     fb=14 * W, av=272, s1=272, s2=256, rowt=272, rowk=256, s3=256, orow=272)
-_add(F4, maskd=256, hd=256, kz=256, lb=512, ab=256, sd=256, sx=256, z=256, zs=272, tb=272, sh=272, so=14 * W, key=256, srow=256, yout=256)
-_pieces("f4s", F4, pf=16, cb0=16, cb1=16, cb2=16, gm=8, ig8=8, a16=16, sig=W, mneg=16, acc=16, rl=16, r16=17, r256=17)
+_add(BF, x0=1024, x1=1024, x2=1024, ut=512, vt=512, zz=512, wk=1024, ex=512, ct=2600, ebig=2112, kbi=288, ramp=272, ones=272, t256=288, t512=272,
+     tneg=288, mh=272, kt=272, sg=256, et=256, ets=256, sn=4096, cm=4096, cs=2048, fo=1024, fp=1024, fs=1088, zt=1024, yt=1024, dy=1088,
+     fb=7 * WS, sig=4 * W, av=272, s1=272, s2=256, rowt=272, rowk=256, s3=256, orow=272)
+_add(F4, maskd=288, hd=256, kz=256, lb=512, ab=256, sd=256, sx=256, z=256, zs=272, tb=272, sh=272, so=7 * WS, key=256, srow=256, yout=256)
+_pieces("f4s", F4, pf=16, cb0=16, cb1=16, cb2=16, gm=8, ig8=8, a16=16, mneg=8, acc=16, r16=17, r256=17)
 _pieces("i4s", I4, ip=1, pi=8, iu=8)
 _pieces("u2s", U2, ul=8, l1=16, l2=16, l3=17, l4=16, lt=16)
 _add(U2, lq0=16, lq1=16, plq0=16, plq1=16, lo0=32, lo1=32, plo0=32, plo1=32)
 for _n, _w in (("uq", 128), ("ur", 128), ("vq", 128), ("wq", 512), ("xqa", 256), ("xqb", 256), ("xqc", 256), ("pxa", 256), ("pxb", 256),
-               ("ctq", 400), ("eq_", 528), ("btq", 256), ("rtq", 128), ("ttq", 256), ("r2q", 128),
+               ("ctq", 650), ("eq_", 528), ("btq", 256), ("rtq", 128), ("ttq", 128), ("r2q", 128),
                ("exq", 128), ("zqa", 256), ("zqb", 256), ("yqa", 256), ("yqb", 256), ("pya", 256), ("pyb", 256)):
     SCRATCH[_n] = ("sbuf", [128, _w], CODE)
     SCRATCH[_n + "S"] = ("sbuf", [128, _w], U1)
@@ -51,7 +51,7 @@ for _k in range(8):
     SCRATCH["ps%d" % _k] = ("psum", [128, 512], F4)
 UNP = (272, 400, 0, 128)
 ROT = (16, 144)
-MV, TC, CW = 0, 16, 272
+CW, MV, TC = 0, 128, 144
 
 NDMA = 16
 SEMAPHORES = (["V", "A", "P", "G"] + ["d%d" % k for k in range(NDMA)]
@@ -151,7 +151,8 @@ def rank_program(g, core, T, topo):
         run("V", lambda e: e.tensor_copy(out[0], src), [out], ins)
 
     def scan(out, a, b, init, op0, op1):
-        run("V", lambda e: e.tensor_tensor_scan(out[0], a[0], b[0], init, op0, op1), [out], [a, b])
+        col = isinstance(init, tuple)
+        run("V", lambda e: e.tensor_tensor_scan(out[0], a[0], b[0], init[0] if col else init, op0, op1), [out], [a, b] + [init] * col)
 
     def fill(out, c):
         run("V", lambda e: e.memset(out[0], c), [out], [])
@@ -189,6 +190,18 @@ def rank_program(g, core, T, topo):
         mm(bank, 128, "eq_", views[0], code, 0, True, False)
         mm(bank, 128, "eq_", views[1], code, 0, False, stop)
 
+    def scaled(q, out, a, c):
+        if q == "V":
+            ts(out, a, c, None, OP.mult)
+        else:
+            act(out, a, scale=c)
+
+    def unpack(name, code, queues):
+        for b in range(4):
+            mm(3 + b, 256, "eq_", UNP[b], code, 0)
+        for b in range(4):
+            scaled(queues[b], B(name, 256 * b, 256 * b + 256), B("ps%d" % (3 + b), 0, 256), 1 / 32)
+
     def gather(q, out, win, off):
         (cp if q == "V" else act)(out, win, off=off)
 
@@ -224,8 +237,8 @@ def rank_program(g, core, T, topo):
     dma("S", T.x0[:], T.x[:], [B("x0")], [])
     dma("A", T.ut[:], T.u[:], [B("ut")], [])
     iota("ip", [[0, 1]], 0, 1)
-    iota("kbi", [[0, 18], [1, 16]], 0, 0)
     iota("iu", [[16, 8]], 0, 0)
+    iota("kbi", [[0, 18], [1, 16]], 0, 0)
     iota("ig8", [[1, 8]], 0, 0)
     iota("cb0", [[0, 8], [-64, 2]], 32, 0)
     iota("cb1", [[0, 4], [-64, 2], [0, 2]], 32, 0)
@@ -233,57 +246,60 @@ def rank_program(g, core, T, topo):
     iota("a16", [[1, 8], [0, 2]], 0, 0)
     iota("ramp", [[1, 272]], 0, 0)
     fill(B("zz"), 0.0)
-    fill(B("wk"), 0.0)
     pi = lambda k: B("pi", k, k + 1)
     pf = lambda k: B("pf", k, k + 1)
     ts(pi(1), B("ip"), 15, None, OP.bitwise_and)
     ts(pi(2), B("ip"), 4, None, OP.arith_shift_right)
-    fill(B("ct"), 0.0)
-    cp(B("pf", 1, 3), B("pi", 1, 3))
+    ts(pi(3), B("ip"), 7, None, OP.bitwise_and)
+    ts(pi(4), B("ip"), 3, None, OP.arith_shift_right)
     cp(B("ul"), B("iu"))
-    ts(B("maskd"), B("kbi", 0, 256), pf(1), BIG, OP.not_equal, OP.mult)
-    ts(B("sg"), B("kbi", 0, 256), 0.0, None, OP.is_gt)
+    cp(B("pf", 1, 5), B("pi", 1, 5))
+    fill(B("ct", 0, 4 * (TC + 16)), 0.0)
+    ts(pf(5), pf(1), -BIG, None, OP.mult)
+    fill(B("wk"), 0.0)
+    act(B("fb"), B("zz", 0, 7 * WS), AF.Identity, bias=1.0)
+    act(B("sg"), B("kbi", 0, 256), AF.Sign)
+    act(B("maskd"), B("kbi"), AF.Abs, scale=BIG, bias=pf(5))
     act(B("hd"), B("sg"), AF.Identity, scale=-BIG, bias=BIG)
-    ts(B("t256"), B("kbi"), pf(1), 256.0, OP.is_equal, OP.mult)
-    act(B("t512"), B("t256"), scale=2.0)
-    for b in range(3):
-        ts(pf(8 + b), pf(1), 1.0 + b, None, OP.is_equal)
+    act(B("ones"), B("zz", 0, 272), AF.Identity, bias=1.0)
+    ts(B("pf", 8, 11), B("ig8", 1, 4), pf(1), None, OP.is_equal)
     ts(B("gm"), B("ig8"), pf(2), None, OP.is_equal)
+    fill(B("sig"), 0.0)
     for b in range(3):
         ts(B("cb%d" % b), B("cb%d" % b), pf(8 + b), None, OP.mult)
-    tt(B("cb0"), B("cb0"), B("cb1"), OP.add)
-    fill(B("sig"), 0.0)
-    tt(B("cb0"), B("cb0"), B("cb2"), OP.add)
-    for gg in range(8):
-        act(B("ct", 4 * CW + 64 * gg, 4 * CW + 64 * gg + 64, 4), B("cb0"), scale=B("gm", gg, gg + 1))
-    act(B("kz"), B("ramp", 0, 256), AF.Identity, scale=COL, bias=80.0 - 127.5 * COL)
-    quant("xqa", 0, 256, B("x0"))
     quant("uq", 0, 128, B("ut"))
+    tt(B("cb0"), B("cb0"), B("cb1"), OP.add)
     ul = B("ul")
     run("V", lambda e: e.tensor_copy(T.ur[:].bitcast(dt.uint32), T.uq[:].bitcast(dt.uint32).indirect(ul[0])), [B("ur")], [B("uq"), ul])
     run("A", lambda e: e.activation(T.urS[:], T.uqS[:].indirect(ul[0]), AF.Copy), [B("urS")], [B("uqS"), ul])
+    tt(B("cb0"), B("cb0"), B("cb2"), OP.add)
+    quant("xqa", 0, 256, B("x0"))
+    for gg in range(8):
+        act(B("ct", 4 * CW + 64 * gg, 4 * CW + 64 * gg + 64, 4), B("cb0"), scale=B("gm", gg, gg + 1))
     unpacker(0, 128, 2)
     unpacker(128, 128, 3)
     unpacker(256, 16, 2)
-
-    def constants_v():
-        ts(B("sig", 0, 16), B("a16"), pf(1), -EPS, OP.is_equal, OP.mult)
-        ts(B("sig", 17, 33), B("a16"), pf(1), EPS, OP.is_equal, OP.mult)
-        ts(B("mneg"), B("kbi", 0, 16), pf(1), 15 / 16, OP.is_equal, OP.mult)
-        ts(pf(3), pf(1), 15.0, 256.0, OP.is_lt, OP.mult)
-        fill(B("ones"), 1.0)
-        fill(B("fb"), 1.0)
-        fill(B("ex"), 0.0)
-        ts(B("mneg"), B("mneg"), -1.0, None, OP.add)
-        ts(B("fb", W - 1, 14 * W, W), B("fb", W - 1, 14 * W, W), EPS, None, OP.mult)
+    unpacker(UNP[0], 128, 0)
+    unpacker(UNP[1], 128, 1)
+    for h in range(2):
+        at = 4 * H1 * h + 1 + 2 * h
+        ts(B("sig", at, at + 64, 4), B("a16"), pf(1), -EPS, OP.is_equal, OP.mult)
+        ts(B("sig", at + 68, at + 132, 4), B("a16"), pf(1), EPS, OP.is_equal, OP.mult)
+    ts(B("ct", 4 * MV, 4 * MV + 64, 4), B("kbi", 0, 16), pf(4), -32 * 16 / EPS, OP.is_equal, OP.mult)
+    ts(B("mneg"), B("ig8"), pf(3), 15 / 16, OP.is_equal, OP.mult)
 
     def constants_a():
-        act(B("ct", 4 * TC + 1, 4 * TC + 64, 4), B("sig", 17, 33), scale=B("gm", 0, 1))
+        act(B("t256"), B("maskd"), AF.Relu, scale=-1.0, bias=256.0)
+        act(B("t512"), B("maskd", 0, 272), AF.Relu, scale=-1.0, bias=512.0)
+        act(B("tneg"), B("t256"), scale=-1 / 512)
+        for h in range(2):
+            act(B("ct", 4 * (TC + 8 * h) + 1 + 2 * h, 4 * (TC + 8 * h + 8), 4), B("sig", 69, 133, 8), scale=B("gm", 0, 1))
         for gg in range(1, 8):
             at = 4 * (TC + 16 + W * (gg - 1))
-            act(B("ct", at + 1, at + 4 * W, 4), B("sig"), scale=B("gm", gg, gg + 1))
-        for h in range(2):
-            act(B("ct", 4 * MV + 32 * h + h, 4 * MV + 32 * h + 32, 4), B("gm"), scale=-32 * 16 / EPS)
+            act(B("ct", at, at + 4 * W), B("sig"), scale=B("gm", gg, gg + 1))
+        act(B("fb", 33, 7 * WS, H1), B("zz", 0, 14), AF.Identity, bias=EPS)
+        act(B("fb", 35, 7 * WS, WS), B("zz", 0, 7), AF.Identity, bias=EPS / 128)
+        act(B("mneg"), B("mneg"), AF.Identity, bias=-1.0)
 
     HB = ((3, 4, 5, 6), (0, 1, 2, 7))
     for r in range(2):
@@ -293,8 +309,8 @@ def rank_program(g, core, T, topo):
         lq, plq, lo, plo = "lq%d" % r, "plq%d" % r, "lo%d" % r, "plo%d" % r
         send([(U8(B(px)), U8(B(xq))), (B(px + "S"), B(xq + "S"))], dst, "rx%d" % r, "lx%d" % r)
         if r == 0:
-            unpacker(UNP[0], 128, 0)
-            unpacker(UNP[1], 128, 1)
+            iota("ex", [[0, 512]], 0, 0)
+            iota("kt", [[0, 17], [1024, 16]], 0, 0)
             for b in range(4):
                 iota(B("dy", 272 * b + 256, 272 * b + 272), [[0, 16]], 0, 0)
         mm(1, 256, "ur", 0, xq, 0)
@@ -303,130 +319,114 @@ def rank_program(g, core, T, topo):
         act(B("ab"), B("ps0", 0, 256), AF.Abs, scale=0.6 * 2.0 ** -23, bias=2.0 ** -122)
         act(B("lb", 0, 256), B("ps0", 0, 256))
         act(B("wk", 0, 1024, 4), B("ps2", 0, 256), AF.Sign, bias=-2.0 ** -100)
-        if r == 0:
-            constants_v()
-        tt(B("sd"), B("ps1", 0, 256), B("maskd"), OP.add)
+        tt(B("sd"), B("ps1", 0, 256), B("maskd", 0, 256), OP.add)
         scan(B("sx"), B("hd"), B("sd"), 0.0, OP.add, OP.min)
         tt(B("lb", 256, 512), B("ps1", 0, 256), B("ab"), OP.add)
+        if r == 0:
+            act(B("kz"), B("ramp", 0, 256), AF.Identity, scale=COL, bias=80.0 - 127.5 * COL)
         row = lambda m: B("lb", 16 * m + 16, 16 * m + 272)
         mine = lambda m: B("sx", 16 * m + 15, 16 * m + 16)
-        blk = lambda name, m, n=1: B(name, 256 * m, 256 * (m + n))
-        for m in range(NA):
-            act(blk("sn", m), row(m), AF.Sign, scale=-1.0, bias=mine(m))
+        blk = lambda name, m: B(name, 256 * m, 256 * m + 256)
+        for m in range(NA + 1):
+            if m < NA:
+                act(blk("sn", m), row(m), AF.Sign, scale=-1.0, bias=mine(m))
             if m:
-                act(blk("cm", m - 1), blk("sn", m - 1), AF.Relu, scale=-1.0, accum=B("acc", m - 1, m))
-        act(blk("cm", NA - 1), blk("sn", NA - 1), AF.Relu, scale=-1.0, accum=B("acc", NA - 1, NA))
-        if r == 0:
-            fill(B("sn", 256 * NA, 256 * NA + 768), 1.0)
-            ts(B("sn", 256 * NA, 256 * NA + 768, 256), B("sn", 256 * NA, 256 * NA + 768, 256), 0.0, None, OP.mult)
-        for m0 in range(NA, 16, 3):
-            n = min(3, 16 - m0)
-            for m in range(m0, m0 + n):
-                ts(blk("cm", m), row(m), mine(m), None, OP.is_gt)
-            if m0 == NA:
+                act(blk("cm", m - 1), blk("sn", m - 1), AF.Sign, bias=1.0, accum=B("acc", m - 1, m))
+        tt(B("et"), B("ps1", 0, 256), B("sx"), OP.is_equal)
+        for m in range(NA, 17):
+            if m < 16:
+                ts(blk("cm", m), row(m), mine(m), None, OP.is_le)
+            if m == NA:
+                scan(B("ets"), B("sg"), B("et"), 0.0, OP.mult, OP.add)
+            else:
+                a = 256 * (m - 1)
+                scan(B("cs", a // 2, a // 2 + 128), B("cm", a, a + 128), B("cm", a + 128, a + 256), B("ets", 16 * m - 1, 16 * m), OP.add, OP.add)
+            if m == NA + 2:
                 if r == 0:
-                    quant("ctq", CW, 128, B("ct", 4 * CW, 4 * CW + 512))
+                    quant("ctq", 0, TC, B("ct", 0, 4 * TC))
                 quant("btq", 0, 256, B("wk"))
                 mm(2, 256, "ctq", CW, "btq", 0)
-                tt(B("et"), B("ps1", 0, 256), B("sx"), OP.is_equal)
-            elif m0 == NA + 3:
-                scan(B("ets"), B("sg"), B("et"), 0.0, OP.mult, OP.add)
-                if r == 0:
-                    quant("eq_", 0, 272, B("ebig", 0, 1088))
-            else:
+            if r == 0 and m == 14:
+                quant("eq_", 0, 272, B("ebig", 0, 1088))
+            if m == 15:
                 tt(B("z"), B("ps2", 0, 256), B("kz"), OP.add)
-            scan(blk("cs", m0, n), blk("sn", NA, n), blk("cm", m0, n), 0.0, OP.mult, OP.add)
-        tt(B("rl", 0, NA), B("ets", 15, 16 * NA, 16), B("acc", 0, NA), OP.subtract)
-        tt(B("rl", NA, 16), B("ets", 16 * NA + 15, 256, 16), B("cs", 256 * NA + 255, 4096, 256), OP.subtract)
+        tt(B("cs", 127, 128 * NA, 128), B("ets", 15, 16 * NA, 16), B("acc", 0, NA), OP.add)
         if r == 0:
             constants_a()
             dma("S", T.wq[:].bitcast(dt.uint8), T.wc[:], [B("wq")], [B("ets")])
             dma("S", T.wqS[:], T.ws[:], [B("wqS")], [B("ets")])
-        ts(B("l1"), B("rl"), 255.0, None, OP.add)
-        rounded(B("wk", 2, 64, 4), B("rl"), 16)
-        tt(B("wk", 3, 64, 4), B("rl"), B("wk", 2, 64, 4), OP.subtract)
+        else:
+            dma("S", T.vt[:], T.v[:], [B("vt")], [B("ets")])
+            unpack("fo", xq, "AAAA")
+        rl, l1 = B("cs", 127, 2048, 128), B("l1")
+        ts(l1, rl, -1.0, None, OP.add)
+        rounded(B("wk", 2, 64, 4), rl, 16)
+        run("V", lambda e: e.tensor_copy(T.zs[:, 16:272].indirect(l1[0]), T.z[:]), [B("zs", 16, 272)], [B("z"), l1])
+        tt(B("wk", 3, 64, 4), rl, B("wk", 2, 64, 4), OP.subtract)
+        cp(B("zs", 0, 16), B("zs", 256, 272))
         quant("rtq", 0, 128, B("wk", 0, 512))
         digits(7, ROT, "rtq")
         digits(0, ROT, "rtq", False)
-        l1 = B("l1")
-        run("V", lambda e: e.tensor_copy(T.zs[:, 16:272].indirect(l1[0]), T.z[:]), [B("zs", 16, 272)], [B("z"), l1])
-        ts(B("l2"), B("ps7", 0, 16), 1 / 32, 255.0, OP.mult, OP.add)
-        cp(B("zs", 0, 16), B("zs", 256, 272))
         if r == 0:
+            scan(B("mh"), B("tneg", 15, 287), B("t512"), 0.0, OP.mult, OP.add)
             quant("eq_", 272, 256, B("ebig", 1088, 2112))
-        for b in range(4):
-            mm(3 + b, 256, "eq_", UNP[b], xq, 0)
-        for b in range(4):
-            act(B("fo", 256 * b, 256 * b + 256), B("ps%d" % (3 + b), 0, 256), scale=1 / 32)
-        scan(B("tb"), B("ones"), B("zs"), 48.0, OP.add, OP.min)
-        if r == 0:
-            quant("ctq", 0, CW, B("ct", 0, 4 * CW))
-        rounded(B("wk", 1, 1024, 4), B("tb", 16, 272), 1, off=B("l2"))
-        if r == 0:
-            tt(B("mh"), B("t512", 16, 288), B("t256", 15, 287), OP.subtract)
-        quant("ttq", 0, 256, B("wk"))
-        for h in range(2):
-            mm(1 + h, 256, "ttq", 128 * h, "ctq", TC)
-        for b in range(4):
-            mm(3 + b, 256, "eq_", UNP[b], px, 0)
+        unpack("fp", px, "AAAA")
         own(B("sh"), B("zs"), 272)
+        scan(B("tb"), B("ones"), B("zs"), 48.0, OP.add, OP.min)
         ends = B("sh", 15, 272, 16)
-        rounded(B("r16"), ends, 16 * COL)
         rounded(B("r256"), ends, 256 * COL)
-        tt(B("ex", 3, 68, 4), ends, B("r16"), OP.subtract)
-        tt(B("ex", 2, 68, 4), B("r16"), B("r256"), OP.subtract)
-        at = lambda k, h: W * (2 * (k - 1) + h)
+        ts(B("l2"), B("ps7", 0, 16), 1 / 32, -1.0, OP.mult, OP.add)
+        tt(B("r16"), ends, B("r256"), OP.subtract)
+        rounded(B("wk", 1, 512, 2), B("tb", 16, 272), 1, off=B("l2"))
+        ts(B(lo, 0, 17), B("r16"), 1 / COL, 127.5, OP.mult, OP.add)
+        send([(B(plo, 0, 17), B(lo, 0, 17))], dst, "ro%d" % r, "lo%d" % r)
+        if r == 0:
+            quant("ctq", TC, 506, B("ct", 4 * TC, 2600))
+        quant("ttq", 0, 128, B("wk", 0, 512))
+        mm(1, 16 + 2 * W, "ttq", 0, "ctq", TC)
+        mm(2, 5 * W, "ttq", 0, "ctq", TC + 16 + 2 * W)
+        rounded(B("ex", 2, 68, 4), B("r16"), 16 * COL)
+        if r == 0:
+            ts(pf(6), pf(1), -1024.0, None, OP.mult)
+        tt(B("ex", 3, 68, 4), B("r16"), B("ex", 2, 68, 4), OP.subtract)
+        beside = {2: lambda: (quant("r2q", 0, 128, B("ex")), digits(7, ROT, "r2q")),
+                  6: lambda: ts(B("l3"), B("ps7", 0, 17), 1 / (32 * COL), 127.5, OP.mult, OP.add)}
+        if r == 0:
+            beside[4] = lambda: ts(pf(7), pf(1), 15.0, 256.0, OP.is_lt, OP.mult)
+        sort = lambda q, b: gather(q, B("fs", 272 * b, 272 * b + 272), B("fp", 256 * b, 256 * b + 256), B(plo, 0, 17))
         for h in range(2):
-            ts(B("fb", at(1, h), at(1, h) + 16, 2), B("ps%d" % (1 + h), 0, 16, 2), -15.5 * EPS, None, OP.is_le)
-        quant("r2q", 0, 128, B("ex"))
-        digits(7, UNP[2:], "r2q")
+            ts(B("fb", H1 * h, H1 * h + 16, 2), B("ps1", 8 * h, 8 * h + 8), -15.5 * EPS, None, OP.is_le)
         for k in range(1, 8):
+            if k == 4:
+                sort("A", 0)
+            c = WS * (k - 1)
+            p = B("ps1", 16 + W * (k - 1), 16 + W * k) if k < 3 else B("ps2", W * (k - 3), W * (k - 2))
+            scan(B("so", c, c + W), p, B("fb", c, c + W), EPS / 128, OP.subtract, OP.min)
+            beside.get(2 * k, lambda: None)()
+            if k < 7:
+                tt(B("fb", c + WS, c + WS + 52, 2), B("fb", c, c + 52, 2), B("so", c + 17, c + 69, 2), OP.is_ge)
+            beside.get(2 * k + 1, lambda: None)()
             for h in range(2):
-                c, p = at(k, h), 16 + W * (k - 1)
-                scan(B("so", c, c + W), B("ps%d" % (1 + h), p, p + W), B("fb", c, c + W), EPS / 128, OP.subtract, OP.min)
-            for h in range(2):
-                c = at(k, h)
-                if k < 7:
-                    tt(B("fb", c + 2 * W, c + 2 * W + 16, 2), B("fb", c, c + 16, 2), B("so", c + 17, c + 33, 2), OP.is_ge)
-            if k == 1:
-                ts(B(lo, 0, 18), B("ps7", 0, 18), 1 / (32 * COL), 127.5, OP.mult, OP.add)
-                send([(B(plo, 0, 18), B(lo, 0, 18))], dst, "ro%d" % r, "lo%d" % r)
-                digits(7, ROT, "r2q")
-            if k == 3:
-                ts(B("l3"), B("ps7", 0, 17), 1 / (32 * COL), 127.5, OP.mult, OP.add)
-            if k <= 4:
-                b = k - 1
-                act(B("fp", 256 * b, 256 * b + 256), B("ps%d" % (3 + b), 0, 256), scale=1 / 32)
-            for h in range(2):
-                c = at(k, h)
-                act(B("ex", 64 * k + h, 64 * k + 64, 4), B("mneg"), AF.Relu, scale=B("so", c + 15, c + 16), bias=B("so", c + 33, c + 34))
+                a = c + H1 * h
+                act(B("ex", 64 * k + 4 * h, 64 * k + 64, 8), B("mneg"), AF.Relu, scale=B("so", a + 15, a + 16), bias=B("so", a + 33, a + 34))
         quant("exq", 0, 128, B("ex"))
         mm(0, 128, "exq", 0, "ctq", MV, False, True)
-        ts(B(lq), B("ps0", 0, 16), 1 / 32, 271.25, OP.mult, OP.add)
+        ts(B(lq), B("ps0", 0, 16), 1 / 32, 15.25, OP.mult, OP.add)
         send([(B(plq), B(lq))], dst, "rl%d" % r, "ll%d" % r)
-        if r == 1:
-            dma("S", T.vt[:], T.v[:], [B("vt")], [B(lq)])
-        else:
-            act(B("kt"), B("kbi", 0, 272), scale=1024.0)
-            ts(pf(4), pf(1), -1024.0, None, OP.mult)
         for h in range(2):
             for b in range(4):
                 mm(HB[h][b], 128, "eq_", UNP[b], xq, 128 * h, True, False)
-        for b in (2, 3):
-            gather("A", B("fs", 272 * b, 272 * b + 272), B("fp", 256 * b, 256 * b + 256), B(plo, 0, 17))
+        sort("A", 2)
+        sort("A", 3)
         tt(B("key"), B("kt"), B("ramp", 0, 256), OP.add, off=B(lq))
-        act(B("av"), B("key"), AF.Abs, bias=pf(4), off=B("l3"))
-        for b in (0, 1):
-            gather("V", B("fs", 272 * b, 272 * b + 272), B("fp", 256 * b, 256 * b + 256), B(plo, 0, 17))
-        scan(B("s1"), B("t256", 0, 272), B("av"), 256.0, OP.max, OP.min)
-        own(B("s2"), B("s1", 15, 271), 256)
+        act(B("av"), B("key"), AF.Abs, bias=pf(6), off=B("l3"))
+        sort("V", 1)
         for h in range(2):
             for b in range(4):
                 gather("VVAA"[b], B("zt", 512 * h + b, 512 * h + 512, 4), B("fs", 272 * b, 272 * b + 272), B(plq, 8 * h, 8 * h + 8))
             quant(zq, 128 * h, 128, B("zt", 512 * h, 512 * h + 512))
             for b in range(4):
                 mm(HB[h][b], 128, "wq", 128 * b, zq, 128 * h, False, True)
-        ts(B("lt"), B("s2", 15, 256, 16), pf(3), None, OP.add)
         for h in range(2):
             for b in range(4):
                 o, i = B("yt", 512 * h + b, 512 * h + 512, 4), B("ps%d" % HB[h][b], 0, 128)
@@ -437,26 +437,29 @@ def rank_program(g, core, T, topo):
             quant(yq, 128 * h, 128, B("yt", 512 * h, 512 * h + 512))
             q = (128 * h, 128 * h + 128)
             send([(U8(B(py, *q)), U8(B(yq, *q))), (B(py + "S", *q), B(yq + "S", *q))], dst, "ry%d%d" % (r, h), "ly%d%d" % (r, h))
+        scan(B("s1"), B("t256", 0, 272), B("av"), 256.0, OP.max, OP.min)
+        own(B("s2"), B("s1", 15, 271), 256)
+        ts(B("lt"), B("s2", 15, 256, 16), pf(7), None, OP.add)
         gather("A", B("rowt", 0, 256), B("ramp"), B("lt"))
         act(B("rowt", 256, 272), B("rowt", 0, 16))
         gather("A", B("rowk"), B("rowt", 16, 272), l1)
-        own(B("s3"), B("rowk"), 256)
-        ts(B("l4"), B("s3", 15, 256, 16), pf(3), None, OP.add)
+        if r == 0:
+            unpack("fo", xq, "VVVA")
+        else:
+            quant("vq", 0, 128, B("vt"))
+        for h in range(2):
+            for b in range(4):
+                mm(HB[1 - h][b], 128, "eq_", UNP[b], py, 128 * h)
+        for h in range(2):
+            for b in range(4):
+                scaled(("VVVA", "VAVA")[h][b], B("dy", 272 * b + 128 * h, 272 * b + 128 * h + 128), B("ps%d" % HB[1 - h][b], 0, 128), 1 / 32)
+            if h == 0:
+                own(B("s3"), B("rowk"), 256)
+                ts(B("l4"), B("s3", 15, 256, 16), pf(7), None, OP.add)
         if r == 1:
             gather("A", B("orow"), B("ramp"), B(lo, 0, 17))
             gather("A", B("srow"), B("orow"), B(lq))
             dma("S", T.src[:], T.srow[0:128:16, :], [], [B("srow")])
-            quant("vq", 0, 128, B("vt"))
-        for h in range(2):
-            for b in range(4):
-                mm(HB[h][b], 128, "eq_", UNP[b], py, 128 * h)
-        for h in range(2):
-            for b in range(4):
-                o, i = B("dy", 272 * b + 128 * h, 272 * b + 128 * h + 128), B("ps%d" % HB[h][b], 0, 128)
-                if b % 2 == 0:
-                    ts(o, i, 1 / 32, None, OP.mult)
-                else:
-                    act(o, i, scale=1 / 32)
         xn = "x%d" % (r + 1)
         for b in range(4):
             tt(B(xn, b, 1024, 4), B("dy", 272 * b, 272 * b + 272), B("fo", 256 * b, 256 * b + 256), OP.add, off=B("l4"))

@@ -34,9 +34,9 @@ def _pieces(base, dtype, **bufs):
     SCRATCH[base] = ("sbuf", [128, at], dtype)
 
 
-_add(BF, x0=1024, x1=1024, x2=1024, ut=512, vt=512, zz=512, wk=1024, ex=512, ct=2600, ebig=2112, kbi=288, ramp=272, ones=272, t256=288, t512=272,
+_add(BF, x0=1024, x1=1024, x2=1024, ut=512, vt=512, zz=512, wk=1024, ex=512, e2=512, ct=2600, ebig=2112, kbi=288, ramp=272, ones=272, t256=288, t512=272,
      tneg=288, mh=272, kt=272, sg=256, et=256, ets=256, sn=4096, cm=4096, cs=2048, fo=1024, fp=1024, fs=1088, zt=1024, yt=1024, dy=1088,
-     fb=7 * WS, sig=4 * W, av=272, s1=272, s2=256, rowt=272, rowk=256, s3=256, orow=272)
+     fb=7 * WS, sig=2 * W, av=272, s1=272, s2=256, rowt=272, rowk=256, s3=256, orow=272)
 _add(F4, maskd=288, hd=256, kz=256, lb=512, ab=256, sd=256, sx=256, z=256, zs=272, tb=272, sh=272, so=7 * WS, key=256, srow=256, yout=256)
 _pieces("f4s", F4, pf=16, cb0=16, cb1=16, cb2=16, gm=8, ig8=8, a16=16, mneg=8, acc=16, r16=17, r256=17)
 _pieces("i4s", I4, ip=1, pi=8, iu=8)
@@ -252,40 +252,39 @@ def rank_program(g, core, T, topo):
     ts(pi(2), B("ip"), 4, None, OP.arith_shift_right)
     ts(pi(3), B("ip"), 7, None, OP.bitwise_and)
     ts(pi(4), B("ip"), 3, None, OP.arith_shift_right)
-    cp(B("ul"), B("iu"))
     cp(B("pf", 1, 5), B("pi", 1, 5))
-    fill(B("ct", 0, 4 * (TC + 16)), 0.0)
+    cp(B("ul"), B("iu"))
     ts(pf(5), pf(1), -BIG, None, OP.mult)
-    fill(B("wk"), 0.0)
+    fill(B("ct", 0, 4 * (TC + 16)), 0.0)
     act(B("fb"), B("zz", 0, 7 * WS), AF.Identity, bias=1.0)
+    act(B("sig"), B("zz", 0, 2 * W))
     act(B("sg"), B("kbi", 0, 256), AF.Sign)
     act(B("maskd"), B("kbi"), AF.Abs, scale=BIG, bias=pf(5))
     act(B("hd"), B("sg"), AF.Identity, scale=-BIG, bias=BIG)
     act(B("ones"), B("zz", 0, 272), AF.Identity, bias=1.0)
     ts(B("pf", 8, 11), B("ig8", 1, 4), pf(1), None, OP.is_equal)
     ts(B("gm"), B("ig8"), pf(2), None, OP.is_equal)
-    fill(B("sig"), 0.0)
     for b in range(3):
         ts(B("cb%d" % b), B("cb%d" % b), pf(8 + b), None, OP.mult)
-    quant("uq", 0, 128, B("ut"))
+    ts(B("a16"), B("a16"), pf(1), EPS, OP.is_equal, OP.mult)
+    for h in range(2):
+        at = 2 * H1 * h + h
+        act(B("sig", at, at + 32, 2), B("a16"), scale=-1.0)
+        act(B("sig", at + 34, at + 66, 2), B("a16"))
     tt(B("cb0"), B("cb0"), B("cb1"), OP.add)
+    fill(B("wk"), 0.0)
+    tt(B("cb0"), B("cb0"), B("cb2"), OP.add)
+    quant("uq", 0, 128, B("ut"))
     ul = B("ul")
     run("V", lambda e: e.tensor_copy(T.ur[:].bitcast(dt.uint32), T.uq[:].bitcast(dt.uint32).indirect(ul[0])), [B("ur")], [B("uq"), ul])
     run("A", lambda e: e.activation(T.urS[:], T.uqS[:].indirect(ul[0]), AF.Copy), [B("urS")], [B("uqS"), ul])
-    tt(B("cb0"), B("cb0"), B("cb2"), OP.add)
+    ts(B("ct", 4 * MV, 4 * MV + 64, 4), B("kbi", 0, 16), pf(4), -32 * 16 / EPS, OP.is_equal, OP.mult)
     quant("xqa", 0, 256, B("x0"))
     for gg in range(8):
         act(B("ct", 4 * CW + 64 * gg, 4 * CW + 64 * gg + 64, 4), B("cb0"), scale=B("gm", gg, gg + 1))
     unpacker(0, 128, 2)
     unpacker(128, 128, 3)
     unpacker(256, 16, 2)
-    unpacker(UNP[0], 128, 0)
-    unpacker(UNP[1], 128, 1)
-    for h in range(2):
-        at = 4 * H1 * h + 1 + 2 * h
-        ts(B("sig", at, at + 64, 4), B("a16"), pf(1), -EPS, OP.is_equal, OP.mult)
-        ts(B("sig", at + 68, at + 132, 4), B("a16"), pf(1), EPS, OP.is_equal, OP.mult)
-    ts(B("ct", 4 * MV, 4 * MV + 64, 4), B("kbi", 0, 16), pf(4), -32 * 16 / EPS, OP.is_equal, OP.mult)
     ts(B("mneg"), B("ig8"), pf(3), 15 / 16, OP.is_equal, OP.mult)
 
     def constants_a():
@@ -293,10 +292,10 @@ def rank_program(g, core, T, topo):
         act(B("t512"), B("maskd", 0, 272), AF.Relu, scale=-1.0, bias=512.0)
         act(B("tneg"), B("t256"), scale=-1 / 512)
         for h in range(2):
-            act(B("ct", 4 * (TC + 8 * h) + 1 + 2 * h, 4 * (TC + 8 * h + 8), 4), B("sig", 69, 133, 8), scale=B("gm", 0, 1))
+            act(B("ct", 4 * (TC + 8 * h) + 1 + 2 * h, 4 * (TC + 8 * h + 8), 4), B("sig", 34, 66, 4), scale=B("gm", 0, 1))
         for gg in range(1, 8):
             at = 4 * (TC + 16 + W * (gg - 1))
-            act(B("ct", at, at + 4 * W), B("sig"), scale=B("gm", gg, gg + 1))
+            act(B("ct", at + 1, at + 4 * W, 2), B("sig"), scale=B("gm", gg, gg + 1))
         act(B("fb", 33, 7 * WS, H1), B("zz", 0, 14), AF.Identity, bias=EPS)
         act(B("fb", 35, 7 * WS, WS), B("zz", 0, 7), AF.Identity, bias=EPS / 128)
         act(B("mneg"), B("mneg"), AF.Identity, bias=-1.0)
@@ -309,7 +308,11 @@ def rank_program(g, core, T, topo):
         lq, plq, lo, plo = "lq%d" % r, "plq%d" % r, "lo%d" % r, "plo%d" % r
         send([(U8(B(px)), U8(B(xq))), (B(px + "S"), B(xq + "S"))], dst, "rx%d" % r, "lx%d" % r)
         if r == 0:
+            iota(B("ct", 4 * (TC + 16), 2600, 2), [[0, 980]], 0, 0)
+            unpacker(UNP[0], 128, 0)
+            unpacker(UNP[1], 128, 1)
             iota("ex", [[0, 512]], 0, 0)
+            iota("e2", [[0, 512]], 0, 0)
             iota("kt", [[0, 17], [1024, 16]], 0, 0)
             for b in range(4):
                 iota(B("dy", 272 * b + 256, 272 * b + 272), [[0, 16]], 0, 0)
@@ -359,45 +362,48 @@ def rank_program(g, core, T, topo):
             dma("S", T.vt[:], T.v[:], [B("vt")], [B("ets")])
             unpack("fo", xq, "AAAA")
         rl, l1 = B("cs", 127, 2048, 128), B("l1")
-        ts(l1, rl, -1.0, None, OP.add)
         rounded(B("wk", 2, 64, 4), rl, 16)
-        run("V", lambda e: e.tensor_copy(T.zs[:, 16:272].indirect(l1[0]), T.z[:]), [B("zs", 16, 272)], [B("z"), l1])
+        ts(l1, rl, -1.0, None, OP.add)
         tt(B("wk", 3, 64, 4), rl, B("wk", 2, 64, 4), OP.subtract)
-        cp(B("zs", 0, 16), B("zs", 256, 272))
+        run("V", lambda e: e.tensor_copy(T.zs[:, 16:272].indirect(l1[0]), T.z[:]), [B("zs", 16, 272)], [B("z"), l1])
         quant("rtq", 0, 128, B("wk", 0, 512))
         digits(7, ROT, "rtq")
         digits(0, ROT, "rtq", False)
+        cp(B("zs", 0, 16), B("zs", 256, 272))
         if r == 0:
-            scan(B("mh"), B("tneg", 15, 287), B("t512"), 0.0, OP.mult, OP.add)
             quant("eq_", 272, 256, B("ebig", 1088, 2112))
         unpack("fp", px, "AAAA")
-        own(B("sh"), B("zs"), 272)
         scan(B("tb"), B("ones"), B("zs"), 48.0, OP.add, OP.min)
-        ends = B("sh", 15, 272, 16)
-        rounded(B("r256"), ends, 256 * COL)
         ts(B("l2"), B("ps7", 0, 16), 1 / 32, -1.0, OP.mult, OP.add)
-        tt(B("r16"), ends, B("r256"), OP.subtract)
+        if r == 0:
+            scan(B("mh"), B("tneg", 15, 287), B("t512"), 0.0, OP.mult, OP.add)
         rounded(B("wk", 1, 512, 2), B("tb", 16, 272), 1, off=B("l2"))
-        ts(B(lo, 0, 17), B("r16"), 1 / COL, 127.5, OP.mult, OP.add)
-        send([(B(plo, 0, 17), B(lo, 0, 17))], dst, "ro%d" % r, "lo%d" % r)
         if r == 0:
             quant("ctq", TC, 506, B("ct", 4 * TC, 2600))
         quant("ttq", 0, 128, B("wk", 0, 512))
         mm(1, 16 + 2 * W, "ttq", 0, "ctq", TC)
         mm(2, 5 * W, "ttq", 0, "ctq", TC + 16 + 2 * W)
-        rounded(B("ex", 2, 68, 4), B("r16"), 16 * COL)
+        own(B("sh"), B("zs"), 272)
+        ends = B("sh", 15, 272, 16)
+
+        def order_list():
+            ts(B(lo, 0, 17), B("r16"), 1 / COL, 127.5, OP.mult, OP.add)
+            send([(B(plo, 0, 17), B(lo, 0, 17))], dst, "ro%d" % r, "lo%d" % r)
+        beside = {2: lambda: tt(B("r16"), ends, B("r256"), OP.subtract),
+                  3: order_list,
+                  4: lambda: rounded(B("e2", 2, 68, 4), B("r16"), 16 * COL),
+                  5: lambda: tt(B("e2", 3, 68, 4), B("r16"), B("e2", 2, 68, 4), OP.subtract),
+                  6: lambda: (quant("r2q", 0, 128, B("e2")), digits(7, ROT, "r2q")),
+                  9: lambda: ts(B("l3"), B("ps7", 0, 17), 1 / (32 * COL), 127.5, OP.mult, OP.add)}
         if r == 0:
-            ts(pf(6), pf(1), -1024.0, None, OP.mult)
-        tt(B("ex", 3, 68, 4), B("r16"), B("ex", 2, 68, 4), OP.subtract)
-        beside = {2: lambda: (quant("r2q", 0, 128, B("ex")), digits(7, ROT, "r2q")),
-                  6: lambda: ts(B("l3"), B("ps7", 0, 17), 1 / (32 * COL), 127.5, OP.mult, OP.add)}
-        if r == 0:
-            beside[4] = lambda: ts(pf(7), pf(1), 15.0, 256.0, OP.is_lt, OP.mult)
+            beside[7] = lambda: ts(pf(7), pf(1), 15.0, 256.0, OP.is_lt, OP.mult)
+            beside[8] = lambda: ts(pf(6), pf(1), -1024.0, None, OP.mult)
         sort = lambda q, b: gather(q, B("fs", 272 * b, 272 * b + 272), B("fp", 256 * b, 256 * b + 256), B(plo, 0, 17))
         for h in range(2):
             ts(B("fb", H1 * h, H1 * h + 16, 2), B("ps1", 8 * h, 8 * h + 8), -15.5 * EPS, None, OP.is_le)
+        rounded(B("r256"), ends, 256 * COL)
         for k in range(1, 8):
-            if k == 4:
+            if k == 5:
                 sort("A", 0)
             c = WS * (k - 1)
             p = B("ps1", 16 + W * (k - 1), 16 + W * k) if k < 3 else B("ps2", W * (k - 3), W * (k - 2))
@@ -424,37 +430,36 @@ def rank_program(g, core, T, topo):
         for h in range(2):
             for b in range(4):
                 gather("VVAA"[b], B("zt", 512 * h + b, 512 * h + 512, 4), B("fs", 272 * b, 272 * b + 272), B(plq, 8 * h, 8 * h + 8))
+            if h == 0:
+                scan(B("s1"), B("t256", 0, 272), B("av"), 256.0, OP.max, OP.min)
+            else:
+                own(B("s2"), B("s1", 15, 271), 256)
             quant(zq, 128 * h, 128, B("zt", 512 * h, 512 * h + 512))
             for b in range(4):
                 mm(HB[h][b], 128, "wq", 128 * b, zq, 128 * h, False, True)
         for h in range(2):
             for b in range(4):
-                o, i = B("yt", 512 * h + b, 512 * h + 512, 4), B("ps%d" % HB[h][b], 0, 128)
-                if b % 2 == 0:
-                    ts(o, i, 0.03125, None, OP.mult)
-                else:
-                    act(o, i, scale=0.03125)
+                scaled("VAVA"[b], B("yt", 512 * h + b, 512 * h + 512, 4), B("ps%d" % HB[h][b], 0, 128), 0.03125)
+            if h == 0:
+                ts(B("lt"), B("s2", 15, 256, 16), pf(7), None, OP.add)
             quant(yq, 128 * h, 128, B("yt", 512 * h, 512 * h + 512))
             q = (128 * h, 128 * h + 128)
             send([(U8(B(py, *q)), U8(B(yq, *q))), (B(py + "S", *q), B(yq + "S", *q))], dst, "ry%d%d" % (r, h), "ly%d%d" % (r, h))
-        scan(B("s1"), B("t256", 0, 272), B("av"), 256.0, OP.max, OP.min)
-        own(B("s2"), B("s1", 15, 271), 256)
-        ts(B("lt"), B("s2", 15, 256, 16), pf(7), None, OP.add)
         gather("A", B("rowt", 0, 256), B("ramp"), B("lt"))
         act(B("rowt", 256, 272), B("rowt", 0, 16))
         gather("A", B("rowk"), B("rowt", 16, 272), l1)
         if r == 0:
-            unpack("fo", xq, "VVVA")
+            unpack("fo", xq, "VVVV")
         else:
             quant("vq", 0, 128, B("vt"))
+        own(B("s3"), B("rowk"), 256)
         for h in range(2):
             for b in range(4):
                 mm(HB[1 - h][b], 128, "eq_", UNP[b], py, 128 * h)
         for h in range(2):
             for b in range(4):
-                scaled(("VVVA", "VAVA")[h][b], B("dy", 272 * b + 128 * h, 272 * b + 128 * h + 128), B("ps%d" % HB[1 - h][b], 0, 128), 1 / 32)
+                scaled("VAVA"[b], B("dy", 272 * b + 128 * h, 272 * b + 128 * h + 128), B("ps%d" % HB[1 - h][b], 0, 128), 1 / 32)
             if h == 0:
-                own(B("s3"), B("rowk"), 256)
                 ts(B("l4"), B("s3", 15, 256, 16), pf(7), None, OP.add)
         if r == 1:
             gather("A", B("orow"), B("ramp"), B(lo, 0, 17))

@@ -11,10 +11,13 @@ def grid(step):
     return 1.5 * 2.0 ** 23 * step
 
 
-EPS = 2.0 ** -9
+EPS = 2.0 ** -7
 COL = 2.0 ** -13
 W, H1, WS = 70, 36, 72
-NA = 7
+NAS = [7, 6]
+ZT, YT, DY = ["VVAA", "VVAA"], ["VAVA", "VAVA"], ["VAVA", "VAAA"]
+SORT_AT, AV, SV = [], 0, 1
+HB_EARLY = [(0, 0), (0, 1), (0, 2), (0, 3), (1, 1), (1, 3)]
 STEP = [1, 2]
 
 F4, BF, I4, U2, CODE, U1 = "float32", "bfloat16", "int32", "uint16", "float8_e4m3fn_x4", "uint8"
@@ -34,23 +37,23 @@ def _pieces(base, dtype, **bufs):
     SCRATCH[base] = ("sbuf", [128, at], dtype)
 
 
-_add(BF, x0=1024, x1=1024, x2=1024, ut=512, vt=512, zz=512, wk=1024, ex=512, e2=512, ct=2600, ebig=2112, kbi=288, ramp=272, ones=272, t256=288, t512=272,
-     tneg=288, mh=272, kt=272, sg=256, et=256, ets=256, sn=4096, cm=4096, cs=2048, fo=1024, fp=1024, fs=1088, zt=1024, yt=1024, dy=1088,
-     fb=7 * WS, sig=2 * W, av=272, s1=272, s2=256, rowt=272, rowk=256, s3=256, orow=272)
+_add(BF, x0=1024, x1=1024, x2=1024, ut=512, vt=512, zz=516, wk=1024, ct=2536, ebig=516, rot=512, kbi=288, ramp=272, ones=272, t256=288, t512=272,
+     tneg=288, mh=272, sg=256, et=256, ets=256, sn=4096, cm=4096, cs=2048, fo=1024, fp=1024, fs=1088, zt=1024, yt=1024, dy=1088,
+     fb=7 * WS, sig=2 * W, av=272, s1=272, s2=256, rowt=256, rowk=256, s3=256, orow=272)
 _add(F4, maskd=288, hd=256, kz=256, lb=512, ab=256, sd=256, sx=256, z=256, zs=272, tb=272, sh=272, so=7 * WS, key=256, srow=256, yout=256)
-_pieces("f4s", F4, pf=16, cb0=16, cb1=16, cb2=16, gm=8, ig8=8, a16=16, mneg=8, acc=16, r16=17, r256=17)
-_pieces("i4s", I4, ip=1, pi=8, iu=8)
-_pieces("u2s", U2, ul=8, l1=16, l2=16, l3=17, l4=16, lt=16)
+_pieces("f4s", F4, pf=16, cb0=16, cb1=16, cb2=16, gm=8, g8=16, a16=16, mneg=8, acc=16, r16=17, r256=17, of=17)
+_pieces("i4s", I4, ip=1, pi=4, iu=8, li=16)
+_pieces("u2s", U2, ul=8, l5=16, l1=16, l2=16, l3=17, l4=16, lt=16)
 _add(U2, lq0=16, lq1=16, plq0=16, plq1=16, lo0=32, lo1=32, plo0=32, plo1=32)
 for _n, _w in (("uq", 128), ("ur", 128), ("vq", 128), ("wq", 512), ("xqa", 256), ("xqb", 256), ("xqc", 256), ("pxa", 256), ("pxb", 256),
-               ("ctq", 650), ("eq_", 528), ("btq", 256), ("rtq", 128), ("ttq", 128), ("r2q", 128),
+               ("ctq", 634), ("eq_", 640), ("btq", 256), ("rtq", 128), ("ttq", 128), ("r2q", 128),
                ("exq", 128), ("zqa", 256), ("zqb", 256), ("yqa", 256), ("yqb", 256), ("pya", 256), ("pyb", 256)):
     SCRATCH[_n] = ("sbuf", [128, _w], CODE)
     SCRATCH[_n + "S"] = ("sbuf", [128, _w], U1)
 for _k in range(8):
     SCRATCH["ps%d" % _k] = ("psum", [128, 512], F4)
-UNP = (272, 400, 0, 128)
-ROT = (16, 144)
+UNP = (0, 128, 256, 384)
+ROT = 512
 CW, MV, TC = 0, 128, 144
 
 NDMA = 16
@@ -186,9 +189,8 @@ def rank_program(g, core, T, topo):
             [B(name, 0, n)], [B(st, a, a + 128), B(st + "S", a, a + 128), B(mvg, b, b + n), B(mvg + "S", b, b + n)],
             free=() if start else (name,))
 
-    def digits(bank, views, code, stop=True):
-        mm(bank, 128, "eq_", views[0], code, 0, True, False)
-        mm(bank, 128, "eq_", views[1], code, 0, False, stop)
+    def digits(bank, code, stop=True):
+        mm(bank, 128, "eq_", ROT, code, 0, True, stop)
 
     def scaled(q, out, a, c):
         if q == "V":
@@ -212,9 +214,8 @@ def rank_program(g, core, T, topo):
         else:
             run("G", lambda e: e.iota(out[0], pattern, base, cm), [out], [])
 
-    def unpacker(at, n, b):
-        o, i = B("ebig", 4 * at, 4 * (at + n)), B("zz", 0, 4 * n)
-        run("G", lambda e: e.affine_select(o[0], i[0], [[1, 4 * n]], OP.not_equal, 32.0, -b, -4), [o], [i])
+    def unpacker(b):
+        quant("eq_", UNP[b], 128, B("ebig", 4 - b, 516 - b))
 
     def send(parts, dst, rsem, lsem):
         engs = topo.engines(core, dst)
@@ -239,94 +240,106 @@ def rank_program(g, core, T, topo):
     iota("ip", [[0, 1]], 0, 1)
     iota("iu", [[16, 8]], 0, 0)
     iota("kbi", [[0, 18], [1, 16]], 0, 0)
-    iota("ig8", [[1, 8]], 0, 0)
-    iota("cb0", [[0, 8], [-64, 2]], 32, 0)
-    iota("cb1", [[0, 4], [-64, 2], [0, 2]], 32, 0)
-    iota("cb2", [[0, 2], [-64, 2], [0, 4]], 32, 0)
+    iota("cb0", [[0, 8], [-32, 2]], 16, 0)
+    iota("cb1", [[0, 4], [-32, 2], [0, 2]], 16, 0)
+    iota("cb2", [[0, 2], [-32, 2], [0, 4]], 16, 0)
     iota("a16", [[1, 8], [0, 2]], 0, 0)
     iota("ramp", [[1, 272]], 0, 0)
     fill(B("zz"), 0.0)
-    pi = lambda k: B("pi", k, k + 1)
+    o, i = B("ebig"), B("zz")
+    run("G", lambda e: e.affine_select(o[0], i[0], [[1, 516]], OP.not_equal, 32.0, -4, -4), [o], [i])
+    for o, n, base in ((B("rot", 0, 448), 112, -1016), (B("rot", 448, 512), 16, -1000)):
+        i = B("zz", 0, 4 * n)
+        run("G", lambda e: e.affine_select(o[0], i[0], [[-1, n], [1000, 2], [0, 2]], OP.not_equal, 32.0, base, 1), [o], [i])
     pf = lambda k: B("pf", k, k + 1)
-    ts(pi(1), B("ip"), 15, None, OP.bitwise_and)
-    ts(pi(2), B("ip"), 4, None, OP.arith_shift_right)
-    ts(pi(3), B("ip"), 7, None, OP.bitwise_and)
-    ts(pi(4), B("ip"), 3, None, OP.arith_shift_right)
-    cp(B("pf", 1, 5), B("pi", 1, 5))
+    for k, (c, op) in enumerate(((15, OP.bitwise_and), (7, OP.bitwise_and), (4, OP.arith_shift_right), (3, OP.arith_shift_right))):
+        ts(B("pi", k, k + 1), B("ip"), c, None, op)
     cp(B("ul"), B("iu"))
+    cp(B("pf", 1, 5), B("pi"))
+    fill(B("ct", 0, 4 * TC), 0.0)
     ts(pf(5), pf(1), -BIG, None, OP.mult)
-    fill(B("ct", 0, 4 * (TC + 16)), 0.0)
+    ts(pf(6), pf(1), 8.0, None, OP.is_ge)
+    ts(B("pf", 8, 11), B("kbi", 1, 4), pf(1), None, OP.is_equal)
+    ts(B("gm"), B("kbi", 0, 8), pf(3), None, OP.is_equal)
     act(B("fb"), B("zz", 0, 7 * WS), AF.Identity, bias=1.0)
     act(B("sig"), B("zz", 0, 2 * W))
     act(B("sg"), B("kbi", 0, 256), AF.Sign)
     act(B("maskd"), B("kbi"), AF.Abs, scale=BIG, bias=pf(5))
     act(B("hd"), B("sg"), AF.Identity, scale=-BIG, bias=BIG)
-    act(B("ones"), B("zz", 0, 272), AF.Identity, bias=1.0)
-    ts(B("pf", 8, 11), B("ig8", 1, 4), pf(1), None, OP.is_equal)
-    ts(B("gm"), B("ig8"), pf(2), None, OP.is_equal)
+    act(B("t256"), B("maskd"), AF.Relu, scale=-1.0, bias=256.0)
+    for k, (lower, upper) in enumerate(((grid(1), grid(32)), (32.0 - 127.5 * COL, -9.0 - 127.5 * COL), (-1.0, 1.0), (1.0, 4.0))):
+        act(pf(11 + k), pf(6), AF.Identity, scale=upper - lower, bias=lower)
     for b in range(3):
         ts(B("cb%d" % b), B("cb%d" % b), pf(8 + b), None, OP.mult)
-    ts(B("a16"), B("a16"), pf(1), EPS, OP.is_equal, OP.mult)
-    for h in range(2):
-        at = 2 * H1 * h + h
-        act(B("sig", at, at + 32, 2), B("a16"), scale=-1.0)
-        act(B("sig", at + 34, at + 66, 2), B("a16"))
+    fill(B("wk", 0, 512), 0.0)
     tt(B("cb0"), B("cb0"), B("cb1"), OP.add)
-    fill(B("wk"), 0.0)
+    fill(B("wk", 512, 1024), 0.0)
     tt(B("cb0"), B("cb0"), B("cb2"), OP.add)
     quant("uq", 0, 128, B("ut"))
+    ts(B("cb0", 8, 16), B("cb0", 8, 16), 2.5 / 16, None, OP.mult)
     ul = B("ul")
     run("V", lambda e: e.tensor_copy(T.ur[:].bitcast(dt.uint32), T.uq[:].bitcast(dt.uint32).indirect(ul[0])), [B("ur")], [B("uq"), ul])
     run("A", lambda e: e.activation(T.urS[:], T.uqS[:].indirect(ul[0]), AF.Copy), [B("urS")], [B("uqS"), ul])
-    ts(B("ct", 4 * MV, 4 * MV + 64, 4), B("kbi", 0, 16), pf(4), -32 * 16 / EPS, OP.is_equal, OP.mult)
+    ts(B("mneg"), B("kbi", 0, 8), pf(2), 17 / 16, OP.is_equal, OP.subtract)
     quant("xqa", 0, 256, B("x0"))
+    ts(B("g8"), B("kbi", 0, 16), pf(4), None, OP.is_equal)
+    ts(B("a16"), B("a16"), pf(2), EPS, OP.is_equal, OP.mult)
+    ts(B("ct", 4 * MV + 1, 4 * MV + 64, 4), B("kbi", 0, 16), pf(4), -32 * 16 / EPS, OP.is_equal, OP.mult)
+    tt(B("g8", 2, 3), B("g8", 2, 3), B("g8", 1, 2), OP.add)
+    unpacker(0)
+    unpacker(1)
     for gg in range(8):
         act(B("ct", 4 * CW + 64 * gg, 4 * CW + 64 * gg + 64, 4), B("cb0"), scale=B("gm", gg, gg + 1))
-    unpacker(0, 128, 2)
-    unpacker(128, 128, 3)
-    unpacker(256, 16, 2)
-    ts(B("mneg"), B("ig8"), pf(3), 15 / 16, OP.is_equal, OP.mult)
+    act(B("kz"), B("ramp", 0, 256), AF.Identity, scale=COL, bias=pf(12))
+
+    iota(B("ct", 4 * TC, 4 * (TC + 7 * W), 2), [[0, 14 * W]], 0, 0)
+    fill(B("ones"), 1.0)
+
+    def constants_g():
+        for v, n, c in ((B("fb", 33, 7 * WS, H1), 14, EPS), (B("fb", 0, 16, 2), 8, 0.0), (B("fb", H1, H1 + 16, 2), 8, 0.0),
+                        (B("fb", 35, 7 * WS, WS), 7, EPS / 128)):
+            i = B("zz", 0, n)
+            run("G", lambda e: e.affine_select(v[0], i[0], [[0, n]], OP.is_gt, c, 0, 0), [v], [i])
+        for b in range(4):
+            iota(B("dy", 272 * b + 256, 272 * b + 272), [[0, 16]], 0, 0)
 
     def constants_a():
-        act(B("t256"), B("maskd"), AF.Relu, scale=-1.0, bias=256.0)
+        for h in range(2):
+            for part in range(2):
+                at = 2 * H1 * h + h + 34 * part
+                act(B("sig", at, at + 32, 2), B("a16"), scale=pf(13 + part))
+        for gg in range(1, 8):
+            at = 4 * (TC + W * (gg - 1))
+            act(B("ct", at + 1, at + 4 * W, 2), B("sig"), scale=B("g8", 2 * gg, 2 * gg + 1))
         act(B("t512"), B("maskd", 0, 272), AF.Relu, scale=-1.0, bias=512.0)
         act(B("tneg"), B("t256"), scale=-1 / 512)
-        for h in range(2):
-            act(B("ct", 4 * (TC + 8 * h) + 1 + 2 * h, 4 * (TC + 8 * h + 8), 4), B("sig", 34, 66, 4), scale=B("gm", 0, 1))
-        for gg in range(1, 8):
-            at = 4 * (TC + 16 + W * (gg - 1))
-            act(B("ct", at + 1, at + 4 * W, 2), B("sig"), scale=B("gm", gg, gg + 1))
-        act(B("fb", 33, 7 * WS, H1), B("zz", 0, 14), AF.Identity, bias=EPS)
-        act(B("fb", 35, 7 * WS, WS), B("zz", 0, 7), AF.Identity, bias=EPS / 128)
-        act(B("mneg"), B("mneg"), AF.Identity, bias=-1.0)
+
+    def classes():
+        quant("btq", 0, 256, B("wk"))
+        mm(2, 256, "ctq", CW, "btq", 0)
 
     HB = ((3, 4, 5, 6), (0, 1, 2, 7))
     for r in range(2):
         dst = T.cores[rank ^ STEP[r]]
-        L = "abc"
+        L, NA = "abc", NAS[r]
         xq, px, zq, yq, py = "xq" + L[r], "px" + L[r], "zq" + L[r], "yq" + L[r], "py" + L[r]
         lq, plq, lo, plo = "lq%d" % r, "plq%d" % r, "lo%d" % r, "plo%d" % r
+        mm(0, 256, "ur", 0, xq, 0)
+        mm(1, 256, "ur", 0, xq, 0)
+        mm(2, 256, "uq", 0, xq, 0)
         send([(U8(B(px)), U8(B(xq))), (B(px + "S"), B(xq + "S"))], dst, "rx%d" % r, "lx%d" % r)
         if r == 0:
-            iota(B("ct", 4 * (TC + 16), 2600, 2), [[0, 980]], 0, 0)
-            unpacker(UNP[0], 128, 0)
-            unpacker(UNP[1], 128, 1)
-            iota("ex", [[0, 512]], 0, 0)
-            iota("e2", [[0, 512]], 0, 0)
-            iota("kt", [[0, 17], [1024, 16]], 0, 0)
-            for b in range(4):
-                iota(B("dy", 272 * b + 256, 272 * b + 272), [[0, 16]], 0, 0)
-        mm(1, 256, "ur", 0, xq, 0)
-        mm(0, 256, "ur", 0, xq, 0)
-        mm(2, 256, "uq", 0, xq, 0)
+            constants_g()
         act(B("ab"), B("ps0", 0, 256), AF.Abs, scale=0.6 * 2.0 ** -23, bias=2.0 ** -122)
         act(B("lb", 0, 256), B("ps0", 0, 256))
         act(B("wk", 0, 1024, 4), B("ps2", 0, 256), AF.Sign, bias=-2.0 ** -100)
         tt(B("sd"), B("ps1", 0, 256), B("maskd", 0, 256), OP.add)
-        scan(B("sx"), B("hd"), B("sd"), 0.0, OP.add, OP.min)
         tt(B("lb", 256, 512), B("ps1", 0, 256), B("ab"), OP.add)
+        scan(B("sx"), B("hd"), B("sd"), 0.0, OP.add, OP.min)
         if r == 0:
-            act(B("kz"), B("ramp", 0, 256), AF.Identity, scale=COL, bias=80.0 - 127.5 * COL)
+            quant("ctq", CW, 128, B("ct", 4 * CW, 4 * CW + 512))
+        else:
+            classes()
         row = lambda m: B("lb", 16 * m + 16, 16 * m + 272)
         mine = lambda m: B("sx", 16 * m + 15, 16 * m + 16)
         blk = lambda name, m: B(name, 256 * m, 256 * m + 256)
@@ -339,22 +352,22 @@ def rank_program(g, core, T, topo):
         for m in range(NA, 17):
             if m < 16:
                 ts(blk("cm", m), row(m), mine(m), None, OP.is_le)
+            if m == 16 and r == 0:
+                tt(B("z"), B("ps2", 0, 256), B("kz"), OP.add)
             if m == NA:
                 scan(B("ets"), B("sg"), B("et"), 0.0, OP.mult, OP.add)
             else:
                 a = 256 * (m - 1)
                 scan(B("cs", a // 2, a // 2 + 128), B("cm", a, a + 128), B("cm", a + 128, a + 256), B("ets", 16 * m - 1, 16 * m), OP.add, OP.add)
-            if m == NA + 2:
-                if r == 0:
-                    quant("ctq", 0, TC, B("ct", 0, 4 * TC))
-                quant("btq", 0, 256, B("wk"))
-                mm(2, 256, "ctq", CW, "btq", 0)
-            if r == 0 and m == 14:
-                quant("eq_", 0, 272, B("ebig", 0, 1088))
-            if m == 15:
-                tt(B("z"), B("ps2", 0, 256), B("kz"), OP.add)
-        tt(B("cs", 127, 128 * NA, 128), B("ets", 15, 16 * NA, 16), B("acc", 0, NA), OP.add)
+            if m == 12 and r == 0:
+                classes()
         if r == 0:
+            quant("eq_", ROT, 128, B("rot"))
+        tt(B("cs", 127, 128 * NA, 128), B("ets", 15, 16 * NA, 16), B("acc", 0, NA), OP.add)
+        if r == 1:
+            tt(B("z"), B("ps2", 0, 256), B("kz"), OP.add)
+        if r == 0:
+            unpacker(2)
             constants_a()
             dma("S", T.wq[:].bitcast(dt.uint8), T.wc[:], [B("wq")], [B("ets")])
             dma("S", T.wqS[:], T.ws[:], [B("wqS")], [B("ets")])
@@ -364,49 +377,60 @@ def rank_program(g, core, T, topo):
         rl, l1 = B("cs", 127, 2048, 128), B("l1")
         rounded(B("wk", 2, 64, 4), rl, 16)
         ts(l1, rl, -1.0, None, OP.add)
+        if r == 0:
+            unpacker(3)
         tt(B("wk", 3, 64, 4), rl, B("wk", 2, 64, 4), OP.subtract)
         run("V", lambda e: e.tensor_copy(T.zs[:, 16:272].indirect(l1[0]), T.z[:]), [B("zs", 16, 272)], [B("z"), l1])
         quant("rtq", 0, 128, B("wk", 0, 512))
-        digits(7, ROT, "rtq")
-        digits(0, ROT, "rtq", False)
+        digits(7, "rtq")
+        digits(0, "rtq", False)
         cp(B("zs", 0, 16), B("zs", 256, 272))
+        cut = (MV, MV + 170, MV + 338, MV + 506)
+        third = lambda k: quant("ctq", cut[k], cut[k + 1] - cut[k], B("ct", 4 * cut[k], 4 * cut[k + 1]))
         if r == 0:
-            quant("eq_", 272, 256, B("ebig", 1088, 2112))
-        unpack("fp", px, "AAAA")
-        scan(B("tb"), B("ones"), B("zs"), 48.0, OP.add, OP.min)
+            third(0)
+        else:
+            unpack("fp", px, "AAAA")
+        scan(B("tb"), B("ones"), B("zs"), 16.0, OP.add, OP.min)
         ts(B("l2"), B("ps7", 0, 16), 1 / 32, -1.0, OP.mult, OP.add)
         if r == 0:
-            scan(B("mh"), B("tneg", 15, 287), B("t512"), 0.0, OP.mult, OP.add)
-        rounded(B("wk", 1, 512, 2), B("tb", 16, 272), 1, off=B("l2"))
+            third(1)
+        ts(B("wk", 1, 512, 2), B("tb", 16, 272), pf(11), pf(11), OP.add, OP.subtract, B("l2"))
         if r == 0:
-            quant("ctq", TC, 506, B("ct", 4 * TC, 2600))
+            scan(B("mh"), B("tneg", 15, 287), B("t512"), 0.0, OP.mult, OP.add)
         quant("ttq", 0, 128, B("wk", 0, 512))
-        mm(1, 16 + 2 * W, "ttq", 0, "ctq", TC)
-        mm(2, 5 * W, "ttq", 0, "ctq", TC + 16 + 2 * W)
+        mm(1, 2 * W, "ttq", 0, "ctq", TC)
+        if r == 0:
+            third(2)
+        mm(2, 5 * W, "ttq", 0, "ctq", TC + 2 * W)
+        if r == 0:
+            unpack("fp", px, "AAAA")
         own(B("sh"), B("zs"), 272)
         ends = B("sh", 15, 272, 16)
 
         def order_list():
             ts(B(lo, 0, 17), B("r16"), 1 / COL, 127.5, OP.mult, OP.add)
             send([(B(plo, 0, 17), B(lo, 0, 17))], dst, "ro%d" % r, "lo%d" % r)
-        beside = {2: lambda: tt(B("r16"), ends, B("r256"), OP.subtract),
-                  3: order_list,
-                  4: lambda: rounded(B("e2", 2, 68, 4), B("r16"), 16 * COL),
-                  5: lambda: tt(B("e2", 3, 68, 4), B("r16"), B("e2", 2, 68, 4), OP.subtract),
-                  6: lambda: (quant("r2q", 0, 128, B("e2")), digits(7, ROT, "r2q")),
-                  9: lambda: ts(B("l3"), B("ps7", 0, 17), 1 / (32 * COL), 127.5, OP.mult, OP.add)}
+        beside = {2: lambda: rounded(B("r256"), ends, 256 * COL),
+                  3: lambda: tt(B("r16"), ends, B("r256"), OP.subtract),
+                  4: order_list,
+                  5: lambda: ts(B("of"), B("r16"), 1 / COL, None, OP.mult),
+                  6: lambda: rounded(B("wk", 2, 68, 4), B("of"), 16),
+                  7: lambda: tt(B("wk", 3, 68, 4), B("of"), B("wk", 2, 68, 4), OP.subtract),
+                  8: lambda: (quant("r2q", 0, 128, B("wk", 0, 512)), digits(7, "r2q")),
+                  9: lambda: ts(B("li"), rl, 15.0, None, OP.add),
+                  10: lambda: ts(B("li"), B("li"), 255, None, OP.bitwise_and),
+                  11: lambda: (ts(B("l3"), B("ps7", 0, 17), 1 / 32, 127.5, OP.mult, OP.add), [waiting(h, b) for h, b in HB_EARLY]),
+                  12: lambda: cp(B("l5"), B("li"))}
         if r == 0:
-            beside[7] = lambda: ts(pf(7), pf(1), 15.0, 256.0, OP.is_lt, OP.mult)
-            beside[8] = lambda: ts(pf(6), pf(1), -1024.0, None, OP.mult)
+            beside[13] = lambda: ts(pf(7), pf(1), 15.0, 256.0, OP.is_lt, OP.mult)
+        waiting = lambda h, b: mm(HB[h][b], 128, "eq_", UNP[b], xq, 128 * h, True, False)
         sort = lambda q, b: gather(q, B("fs", 272 * b, 272 * b + 272), B("fp", 256 * b, 256 * b + 256), B(plo, 0, 17))
-        for h in range(2):
-            ts(B("fb", H1 * h, H1 * h + 16, 2), B("ps1", 8 * h, 8 * h + 8), -15.5 * EPS, None, OP.is_le)
-        rounded(B("r256"), ends, 256 * COL)
         for k in range(1, 8):
-            if k == 5:
-                sort("A", 0)
+            if k in SORT_AT:
+                sort("A", SORT_AT.index(k))
             c = WS * (k - 1)
-            p = B("ps1", 16 + W * (k - 1), 16 + W * k) if k < 3 else B("ps2", W * (k - 3), W * (k - 2))
+            p = B("ps1", W * (k - 1), W * k) if k < 3 else B("ps2", W * (k - 3), W * (k - 2))
             scan(B("so", c, c + W), p, B("fb", c, c + W), EPS / 128, OP.subtract, OP.min)
             beside.get(2 * k, lambda: None)()
             if k < 7:
@@ -414,40 +438,53 @@ def rank_program(g, core, T, topo):
             beside.get(2 * k + 1, lambda: None)()
             for h in range(2):
                 a = c + H1 * h
-                act(B("ex", 64 * k + 4 * h, 64 * k + 64, 8), B("mneg"), AF.Relu, scale=B("so", a + 15, a + 16), bias=B("so", a + 33, a + 34))
-        quant("exq", 0, 128, B("ex"))
+                act(B("wk", 513 + 64 * k + 4 * h, 576 + 64 * k, 8), B("mneg"), AF.Relu, scale=B("so", a + 15, a + 16), bias=B("so", a + 33, a + 34))
+        quant("exq", 0, 128, B("wk", 512, 1024))
         mm(0, 128, "exq", 0, "ctq", MV, False, True)
         ts(B(lq), B("ps0", 0, 16), 1 / 32, 15.25, OP.mult, OP.add)
         send([(B(plq), B(lq))], dst, "rl%d" % r, "ll%d" % r)
-        for h in range(2):
-            for b in range(4):
-                mm(HB[h][b], 128, "eq_", UNP[b], xq, 128 * h, True, False)
-        sort("A", 2)
-        sort("A", 3)
-        tt(B("key"), B("kt"), B("ramp", 0, 256), OP.add, off=B(lq))
-        act(B("av"), B("key"), AF.Abs, bias=pf(6), off=B("l3"))
-        sort("V", 1)
-        for h in range(2):
-            for b in range(4):
-                gather("VVAA"[b], B("zt", 512 * h + b, 512 * h + 512, 4), B("fs", 272 * b, 272 * b + 272), B(plq, 8 * h, 8 * h + 8))
-            if h == 0:
-                scan(B("s1"), B("t256", 0, 272), B("av"), 256.0, OP.max, OP.min)
-            else:
-                own(B("s2"), B("s1", 15, 271), 256)
+        waiting(1, 2)
+        waiting(1, 0)
+        for b in range(len(SORT_AT), 4 - SV):
+            sort("A", b)
+        tt(B("key"), B("maskd", 0, 272), B("ramp", 0, 256), OP.add, off=B(lq))
+        if AV == 0:
+            gather("A", B("av"), B("key"), B("l3"))
+        for b in range(4 - SV, 4):
+            sort("V", b)
+        def mosaic(h, b):
+            gather(ZT[h][b], B("zt", 512 * h + b, 512 * h + 512, 4), B("fs", 272 * b, 272 * b + 272), B(plq, 8 * h, 8 * h + 8))
+
+        def layer(h):
             quant(zq, 128 * h, 128, B("zt", 512 * h, 512 * h + 512))
             for b in range(4):
                 mm(HB[h][b], 128, "wq", 128 * b, zq, 128 * h, False, True)
+        for b in range(4):
+            mosaic(0, b)
+        mosaic(1, 0)
+        layer(0)
+        for b in range(1, 4):
+            mosaic(1, b)
+        steps = [lambda: scan(B("s1"), B("t256", 0, 272), B("av"), 256.0, OP.max, OP.min), lambda: own(B("s2"), B("s1", 15, 271), 256),
+                 lambda: ts(B("lt"), B("s2", 15, 256, 16), pf(7), None, OP.add), lambda: None]
+        if AV == 0:
+            steps.pop(0)()
+        else:
+            gather("A", B("av"), B("key"), B("l3"))
+        layer(1)
+        if AV == 0:
+            steps.pop(0)()
         for h in range(2):
             for b in range(4):
-                scaled("VAVA"[b], B("yt", 512 * h + b, 512 * h + 512, 4), B("ps%d" % HB[h][b], 0, 128), 0.03125)
-            if h == 0:
-                ts(B("lt"), B("s2", 15, 256, 16), pf(7), None, OP.add)
+                scaled(YT[h][b], B("yt", 512 * h + b, 512 * h + 512, 4), B("ps%d" % HB[h][b], 0, 128), 0.03125)
+            steps.pop(0)()
             quant(yq, 128 * h, 128, B("yt", 512 * h, 512 * h + 512))
             q = (128 * h, 128 * h + 128)
             send([(U8(B(py, *q)), U8(B(yq, *q))), (B(py + "S", *q), B(yq + "S", *q))], dst, "ry%d%d" % (r, h), "ly%d%d" % (r, h))
-        gather("A", B("rowt", 0, 256), B("ramp"), B("lt"))
-        act(B("rowt", 256, 272), B("rowt", 0, 16))
-        gather("A", B("rowk"), B("rowt", 16, 272), l1)
+        for f in steps:
+            f()
+        gather("A", B("rowt"), B("ramp"), B("lt"))
+        gather("A", B("rowk"), B("rowt"), B("l5"))
         if r == 0:
             unpack("fo", xq, "VVVV")
         else:
@@ -458,24 +495,26 @@ def rank_program(g, core, T, topo):
                 mm(HB[1 - h][b], 128, "eq_", UNP[b], py, 128 * h)
         for h in range(2):
             for b in range(4):
-                scaled("VAVA"[b], B("dy", 272 * b + 128 * h, 272 * b + 128 * h + 128), B("ps%d" % HB[1 - h][b], 0, 128), 1 / 32)
+                scaled(DY[h][b], B("dy", 272 * b + 128 * h, 272 * b + 128 * h + 128), B("ps%d" % HB[1 - h][b], 0, 128), 1 / 32)
             if h == 0:
                 ts(B("l4"), B("s3", 15, 256, 16), pf(7), None, OP.add)
+        xn = "x%d" % (r + 1)
         if r == 1:
             gather("A", B("orow"), B("ramp"), B(lo, 0, 17))
             gather("A", B("srow"), B("orow"), B(lq))
             dma("S", T.src[:], T.srow[0:128:16, :], [], [B("srow")])
-        xn = "x%d" % (r + 1)
         for b in range(4):
             tt(B(xn, b, 1024, 4), B("dy", 272 * b, 272 * b + 272), B("fo", 256 * b, 256 * b + 256), OP.add, off=B("l4"))
         quant("xq" + L[r + 1], 0, 256, B(xn))
     dma("S", T.oc[:], T.xqc[:].bitcast(dt.uint8), [], [B("xqc")])
     for k in range(4):
         dma("A", T.osc[4 * k:4 * k + 4, :], T.xqcS[32 * k:32 * k + 4, :], [], [B("xqcS")])
-    mm(2, 256, "vq", 0, "xqc", 0)
-    cp(B("yout"), B("ps2", 0, 256))
+    for h in range(2):
+        mm(2 + h, 128, "vq", 0, "xqc", 128 * h)
+    for h in range(2):
+        cp(B("yout", 128 * h, 128 * h + 128), B("ps%d" % (2 + h), 0, 128))
     dma("S", T.y[:], T.yout[:], [], [B("yout")])
-    for q in ("V", "A", "P", "G"):
+    for q in ("G", "P", "A", "V"):
         need("G", q, cnt[q])
     for sem, val in final.items():
         need("G", sem, val)

@@ -14,11 +14,16 @@ def grid(step):
 EPS = 2.0 ** -7
 COL = 2.0 ** -13
 W, H1, WS = 70, 36, 72
-NAS = [7, 6]
-ZT, YT, DY = ["VVAA", "VVAA"], ["VAVA", "VAVA"], ["VAVA", "VAAA"]
-SORT_AT, AV, SV = [], 0, 1
-HB_EARLY = [(0, 0), (0, 1), (0, 2), (0, 3), (1, 1), (1, 3)]
+LATE = 3
+LAG = 3
+EARLY = (0, 0, 4)
+NAS = [11, 10]
+SORT_AT = [[], [4, 5]]
+ZT, YT, DY = ["VVAA", "VVAA"], ["AVAV", "AAAV"], ["VAVA", "VAAA"]
+SV = 0
+HB_EARLY = [(0, 0), (0, 1), (0, 2), (0, 3), (1, 1)]
 STEP = [1, 2]
+OLDB = 1
 
 F4, BF, I4, U2, CODE, U1 = "float32", "bfloat16", "int32", "uint16", "float8_e4m3fn_x4", "uint8"
 SCRATCH, PART = {}, {}
@@ -37,16 +42,16 @@ def _pieces(base, dtype, **bufs):
     SCRATCH[base] = ("sbuf", [128, at], dtype)
 
 
-_add(BF, x0=1024, x1=1024, x2=1024, ut=512, vt=512, zz=516, wk=1024, ct=2536, ebig=516, rot=512, kbi=288, ramp=272, ones=272, t256=288, t512=272,
-     tneg=288, mh=272, sg=256, et=256, ets=256, sn=4096, cm=4096, cs=2048, fo=1024, fp=1024, fs=1088, zt=1024, yt=1024, dy=1088,
-     fb=7 * WS, sig=2 * W, av=272, s1=272, s2=256, rowt=256, rowk=256, s3=256, orow=272)
-_add(F4, maskd=288, hd=256, kz=256, lb=512, ab=256, sd=256, sx=256, z=256, zs=272, tb=272, sh=272, so=7 * WS, key=256, srow=256, yout=256)
-_pieces("f4s", F4, pf=16, cb0=16, cb1=16, cb2=16, gm=8, g8=16, a16=16, mneg=8, acc=16, r16=17, r256=17, of=17)
+_add(BF, x0=1024, x1=1024, x2=1024, ut=512, vt=512, zz=516, wk=516, ex=512, ct=1696, ebig=516, rot=512, kbi=288, ramp=272, ones=272, t256=288, t512=288,
+     tneg=288, mh=272, one=512, ets=256, sn=4096, ca=1024, cm=4 * 480, cs=2048, fo=1024, fp=1024, fs=1088, zt=1024, yt=1024, dy=1088, tk=512,
+     fb=7 * WS, sig=2 * W, av=272, s1=272, s2=256, rowt=256, rowk=256, s3=256, orow=272, tb=272, gi=128, gt=512, cb4=64, spare=32)
+_add(F4, maskd=288, hd=256, kz=256, sd=256, sx=256, cw=256, mr=256, z=256, zs=272, sh=272, so=7 * WS, key=256, srow=256, yout=256)
+_pieces("f4s", F4, pf=16, cb0=16, cb1=16, cb2=16, gm=8, g8=16, a16=16, mneg=8, acc=16, r16=17, r256=17, of=17, kc=16, ek=16, rh=16)
 _pieces("i4s", I4, ip=1, pi=4, iu=8, li=16)
-_pieces("u2s", U2, ul=8, l5=16, l1=16, l2=16, l3=17, l4=16, lt=16)
-_add(U2, lq0=16, lq1=16, plq0=16, plq1=16, lo0=32, lo1=32, plo0=32, plo1=32)
+_pieces("u2s", U2, ul=8, l5=16, l3=17, l4=16, lt=16)
+_add(U2, l1=16, l2=16, lq0=16, lq1=16, plq0=16, plq1=16, lo0=32, lo1=32, plo0=32, plo1=32)
 for _n, _w in (("uq", 128), ("ur", 128), ("vq", 128), ("wq", 512), ("xqa", 256), ("xqb", 256), ("xqc", 256), ("pxa", 256), ("pxb", 256),
-               ("ctq", 634), ("eq_", 640), ("btq", 256), ("rtq", 128), ("ttq", 128), ("r2q", 128),
+               ("ctq", 634), ("eq_", 896), ("btq", 256), ("cmq", 480), ("gq", 256), ("ttq", 256), ("r2q", 128),
                ("exq", 128), ("zqa", 256), ("zqb", 256), ("yqa", 256), ("yqb", 256), ("pya", 256), ("pyb", 256)):
     SCRATCH[_n] = ("sbuf", [128, _w], CODE)
     SCRATCH[_n + "S"] = ("sbuf", [128, _w], U1)
@@ -54,9 +59,13 @@ for _k in range(8):
     SCRATCH["ps%d" % _k] = ("psum", [128, 512], F4)
 UNP = (0, 128, 256, 384)
 ROT = 512
+DIG = (0, 18, 36, 52)
+ONE = {2: 640, 3: 768}
 CW, MV, TC = 0, 128, 144
+OFF = 192.0
+TRI = ((13, 0, 208), (9, 208, 144), (5, 352, 128))
 
-NDMA = 16
+NDMA = 20
 SEMAPHORES = (["V", "A", "P", "G"] + ["d%d" % k for k in range(NDMA)]
               + [k + "%d" % r for k in ("rx", "lx", "rl", "ll", "ro", "lo") for r in (0, 1)]
               + [k + "%d%d" % (r, h) for k in ("ry", "ly") for r in (0, 1) for h in (0, 1)])
@@ -88,7 +97,7 @@ def rank_program(g, core, T, topo):
     def clash(u, v):
         if u[3] <= v[2] or v[3] <= u[2]:
             return False
-        return not (u[4] == v[4] > 1 and (u[2] - v[2]) % u[4])
+        return not (u[4] > 1 and v[4] > 1 and not set(range(*u[2:])) & set(range(*v[2:])))
 
     def need(q, sem, val):
         if seen[q].get(sem, 0) < val:
@@ -189,8 +198,8 @@ def rank_program(g, core, T, topo):
             [B(name, 0, n)], [B(st, a, a + 128), B(st + "S", a, a + 128), B(mvg, b, b + n), B(mvg + "S", b, b + n)],
             free=() if start else (name,))
 
-    def digits(bank, code, stop=True):
-        mm(bank, 128, "eq_", ROT, code, 0, True, stop)
+    def digits(bank, k, stop=True):
+        mm(bank, 128, "eq_", ROT, "r2q", 0, True, stop)
 
     def scaled(q, out, a, c):
         if q == "V":
@@ -199,9 +208,9 @@ def rank_program(g, core, T, topo):
             act(out, a, scale=c)
 
     def unpack(name, code, queues):
-        for b in range(4):
+        for b in range(len(queues)):
             mm(3 + b, 256, "eq_", UNP[b], code, 0)
-        for b in range(4):
+        for b in range(len(queues)):
             scaled(queues[b], B(name, 256 * b, 256 * b + 256), B("ps%d" % (3 + b), 0, 256), 1 / 32)
 
     def gather(q, out, win, off):
@@ -243,6 +252,11 @@ def rank_program(g, core, T, topo):
     iota("cb0", [[0, 8], [-32, 2]], 16, 0)
     iota("cb1", [[0, 4], [-32, 2], [0, 2]], 16, 0)
     iota("cb2", [[0, 2], [-32, 2], [0, 4]], 16, 0)
+    iota("gi", [[1, 8], [0, 16]], 0, 0)
+    NA = NAS[0]
+    iota(B("kc", 0, 1), [[0, 1]], 240 - 512, 0)
+    iota(B("kc", 1, NA), [[-16, NA - 1]], 240 - 512, 0)
+    iota(B("kc", NA, 16), [[-16, 16 - NA]], 256 - 16 * NA, 0)
     iota("a16", [[1, 8], [0, 2]], 0, 0)
     iota("ramp", [[1, 272]], 0, 0)
     fill(B("zz"), 0.0)
@@ -250,73 +264,82 @@ def rank_program(g, core, T, topo):
     run("G", lambda e: e.affine_select(o[0], i[0], [[1, 516]], OP.not_equal, 32.0, -4, -4), [o], [i])
     for o, n, base in ((B("rot", 0, 448), 112, -1016), (B("rot", 448, 512), 16, -1000)):
         i = B("zz", 0, 4 * n)
-        run("G", lambda e: e.affine_select(o[0], i[0], [[-1, n], [1000, 2], [0, 2]], OP.not_equal, 32.0, base, 1), [o], [i])
+        run("G", lambda e: e.affine_select(o[0], i[0], [[-1, n], [0, 2], [1000, 2]], OP.not_equal, 32.0, base, 1), [o], [i])
     pf = lambda k: B("pf", k, k + 1)
     for k, (c, op) in enumerate(((15, OP.bitwise_and), (7, OP.bitwise_and), (4, OP.arith_shift_right), (3, OP.arith_shift_right))):
         ts(B("pi", k, k + 1), B("ip"), c, None, op)
     cp(B("ul"), B("iu"))
+    fill(B("cb4"), 0.0)
+    fill(B("ca", 896, 1024), 0.0)
     cp(B("pf", 1, 5), B("pi"))
-    fill(B("ct", 0, 4 * TC), 0.0)
+    tail = [B("cm", 4 * a + 64 * (m - 3), 4 * (a + n)) for m, a, n in TRI]
+    fill(tail[2], 0.0)
+    fill(B("gt", 0, 512, 4), 0.0)
     ts(pf(5), pf(1), -BIG, None, OP.mult)
-    ts(pf(6), pf(1), 8.0, None, OP.is_ge)
     ts(B("pf", 8, 11), B("kbi", 1, 4), pf(1), None, OP.is_equal)
     ts(B("gm"), B("kbi", 0, 8), pf(3), None, OP.is_equal)
-    act(B("fb"), B("zz", 0, 7 * WS), AF.Identity, bias=1.0)
-    act(B("sig"), B("zz", 0, 2 * W))
-    act(B("sg"), B("kbi", 0, 256), AF.Sign)
+    ts(pf(6), pf(1), 8.0, None, OP.is_ge)
+    act(B("ones"), B("zz", 0, 272), AF.Identity, bias=1.0)
+    act(B("hd"), B("kbi", 0, 256), AF.Relu, scale=-BIG, bias=BIG)
     act(B("maskd"), B("kbi"), AF.Abs, scale=BIG, bias=pf(5))
-    act(B("hd"), B("sg"), AF.Identity, scale=-BIG, bias=BIG)
-    act(B("t256"), B("maskd"), AF.Relu, scale=-1.0, bias=256.0)
-    for k, (lower, upper) in enumerate(((grid(1), grid(32)), (32.0 - 127.5 * COL, -9.0 - 127.5 * COL), (-1.0, 1.0), (1.0, 4.0))):
-        act(pf(11 + k), pf(6), AF.Identity, scale=upper - lower, bias=lower)
-    for b in range(3):
+    act(pf(12), pf(6), AF.Identity, -32.0 - 1 / 16, OFF + 32.0 - 127.5 * COL)
+    for v in [B("wk"), B("sig"), B("ct", 4 * MV, 4 * (TC + W)), B("ex")]:
+        z = B("zz", 0, v[3] - v[2])
+        dma("S", v[0], z[0], [v], [z, B("x0")])
+    for b in range(2):
         ts(B("cb%d" % b), B("cb%d" % b), pf(8 + b), None, OP.mult)
-    fill(B("wk", 0, 512), 0.0)
-    tt(B("cb0"), B("cb0"), B("cb1"), OP.add)
-    fill(B("wk", 512, 1024), 0.0)
-    tt(B("cb0"), B("cb0"), B("cb2"), OP.add)
     quant("uq", 0, 128, B("ut"))
-    ts(B("cb0", 8, 16), B("cb0", 8, 16), 2.5 / 16, None, OP.mult)
+    ts(B("cb2"), B("cb2"), pf(10), None, OP.mult)
+    tt(B("cb0"), B("cb0"), B("cb1"), OP.add)
+    fill(tail[0], 0.0)
     ul = B("ul")
     run("V", lambda e: e.tensor_copy(T.ur[:].bitcast(dt.uint32), T.uq[:].bitcast(dt.uint32).indirect(ul[0])), [B("ur")], [B("uq"), ul])
     run("A", lambda e: e.activation(T.urS[:], T.uqS[:].indirect(ul[0]), AF.Copy), [B("urS")], [B("uqS"), ul])
-    ts(B("mneg"), B("kbi", 0, 8), pf(2), 17 / 16, OP.is_equal, OP.subtract)
-    quant("xqa", 0, 256, B("x0"))
-    ts(B("g8"), B("kbi", 0, 16), pf(4), None, OP.is_equal)
-    ts(B("a16"), B("a16"), pf(2), EPS, OP.is_equal, OP.mult)
-    ts(B("ct", 4 * MV + 1, 4 * MV + 64, 4), B("kbi", 0, 16), pf(4), -32 * 16 / EPS, OP.is_equal, OP.mult)
-    tt(B("g8", 2, 3), B("g8", 2, 3), B("g8", 1, 2), OP.add)
-    unpacker(0)
-    unpacker(1)
+    act(B("t512"), B("maskd"), AF.Relu, scale=-1.0, bias=512.0)
+    tt(B("cb0"), B("cb0"), B("cb2"), OP.add)
+    fill(tail[1], 0.0)
+    ts(pf(7), pf(1), 15.0, 256.0, OP.is_lt, OP.mult)
+    group = lambda t, c: ts(B("gt", t, 512, 4), B("gi"), pf(3), c, OP.is_equal, OP.mult)
+    group(1, 1.0)
+    cp(B("cb4", 0, 32, 4), B("cb0", 0, 8))
+    ts(B("cb4", 32, 64, 4), B("cb0", 8, 16), 5 / 512, None, OP.mult)
+    for h in range(2):
+        quant("xqa", 128 * h, 128, B("x0", 512 * h, 512 * h + 512))
+    group(2, -1.0)
+    group(3, -1.0)
+    ts(B("kc"), B("kc"), pf(1), pf(7), OP.subtract, OP.subtract)
+    act(B("tneg"), B("t512"), scale=-1 / 1024)
     for gg in range(8):
-        act(B("ct", 4 * CW + 64 * gg, 4 * CW + 64 * gg + 64, 4), B("cb0"), scale=B("gm", gg, gg + 1))
-    act(B("kz"), B("ramp", 0, 256), AF.Identity, scale=COL, bias=pf(12))
-
-    iota(B("ct", 4 * TC, 4 * (TC + 7 * W), 2), [[0, 14 * W]], 0, 0)
-    fill(B("ones"), 1.0)
-
-    def constants_g():
-        for v, n, c in ((B("fb", 33, 7 * WS, H1), 14, EPS), (B("fb", 0, 16, 2), 8, 0.0), (B("fb", H1, H1 + 16, 2), 8, 0.0),
-                        (B("fb", 35, 7 * WS, WS), 7, EPS / 128)):
-            i = B("zz", 0, n)
-            run("G", lambda e: e.affine_select(v[0], i[0], [[0, n]], OP.is_gt, c, 0, 0), [v], [i])
-        for b in range(4):
-            iota(B("dy", 272 * b + 256, 272 * b + 272), [[0, 16]], 0, 0)
+        act(B("ct", 4 * CW + 64 * gg, 4 * CW + 64 * gg + 64), B("cb4"), scale=B("gm", gg, gg + 1))
 
     def constants_a():
+        act(B("kz"), B("ramp", 0, 256), AF.Identity, COL, pf(12))
+        act(pf(11), B("g8", 2, 3), AF.Identity, bias=B("g8", 1, 2))
+        for k, (lower, upper) in enumerate(((-1.0, 32.0), (1.0, 128.0))):
+            act(pf(13 + k), pf(6), AF.Identity, scale=upper - lower, bias=lower)
         for h in range(2):
             for part in range(2):
                 at = 2 * H1 * h + h + 34 * part
                 act(B("sig", at, at + 32, 2), B("a16"), scale=pf(13 + part))
-        for gg in range(1, 8):
-            at = 4 * (TC + W * (gg - 1))
-            act(B("ct", at + 1, at + 4 * W, 2), B("sig"), scale=B("g8", 2 * gg, 2 * gg + 1))
-        act(B("t512"), B("maskd", 0, 272), AF.Relu, scale=-1.0, bias=512.0)
-        act(B("tneg"), B("t256"), scale=-1 / 512)
+        for gg in (2, 5, 1, 3, 4, 6, 7):
+            at = 4 * (TC + W * (gg - 1)) + 1 if gg < 5 else 4 * (TC + W * (gg - 4))
+            act(B("ct", at, at + 4 * W - 1, 2), B("sig"), scale=B("g8", 2 * gg, 2 * gg + 1) if gg > 1 else pf(11))
+            if gg == 1:
+                act(B("ct", 4 * MV + 1, 4 * MV + 64, 4), B("g8"), scale=-32 * 16 / EPS)
+        act(B("mneg"), B("a16", 0, 16, 2), AF.Identity, scale=1 / EPS, bias=-17 / 16)
+        act(B("fb"), B("zz", 0, 7 * WS), AF.Identity, bias=1.0)
 
-    def classes():
-        quant("btq", 0, 256, B("wk"))
-        mm(2, 256, "ctq", CW, "btq", 0)
+    def bounds():
+        for v, n, c in ((B("fb", 33, 7 * WS, H1), 14, EPS), (B("fb", 0, 16, 2), 8, 0.0), (B("fb", H1, H1 + 16, 2), 8, 0.0),
+                        (B("fb", 35, 7 * WS, WS), 7, EPS / 128)):
+            act(v, B("zz", 0, n), AF.Identity, bias=c)
+        act(B("t256"), B("t512"), scale=0.5)
+
+    def slot(m, a, b):
+        if m > TRI[0][0]:
+            return B("ca", 4 * a + 17 - m, 4 * b, 4)
+        top, at, n = [e for e in TRI if e[0] >= m][-1]
+        return B("cm", 4 * (at + a) + top - m, 4 * (at + b), 4)
 
     HB = ((3, 4, 5, 6), (0, 1, 2, 7))
     for r in range(2):
@@ -324,113 +347,139 @@ def rank_program(g, core, T, topo):
         L, NA = "abc", NAS[r]
         xq, px, zq, yq, py = "xq" + L[r], "px" + L[r], "zq" + L[r], "yq" + L[r], "py" + L[r]
         lq, plq, lo, plo = "lq%d" % r, "plq%d" % r, "lo%d" % r, "plo%d" % r
-        mm(0, 256, "ur", 0, xq, 0)
-        mm(1, 256, "ur", 0, xq, 0)
+        once = (lambda f, *a: f(*a)) if r == 0 else (lambda f, *a: None)
+        for h in range(2):
+            mm(3 + h, 128, "ur", 0, xq, 128 * h)
         mm(2, 256, "uq", 0, xq, 0)
+        mm(1, 256, "ur", 0, xq, 0)
+        mm(0, 256, "ur", 0, xq, 0)
         send([(U8(B(px)), U8(B(xq))), (B(px + "S"), B(xq + "S"))], dst, "rx%d" % r, "lx%d" % r)
         if r == 0:
-            constants_g()
-        act(B("ab"), B("ps0", 0, 256), AF.Abs, scale=0.6 * 2.0 ** -23, bias=2.0 ** -122)
-        act(B("lb", 0, 256), B("ps0", 0, 256))
-        act(B("wk", 0, 1024, 4), B("ps2", 0, 256), AF.Sign, bias=-2.0 ** -100)
-        tt(B("sd"), B("ps1", 0, 256), B("maskd", 0, 256), OP.add)
-        tt(B("lb", 256, 512), B("ps1", 0, 256), B("ab"), OP.add)
-        scan(B("sx"), B("hd"), B("sd"), 0.0, OP.add, OP.min)
-        if r == 0:
-            quant("ctq", CW, 128, B("ct", 4 * CW, 4 * CW + 512))
-        else:
-            classes()
-        row = lambda m: B("lb", 16 * m + 16, 16 * m + 272)
+            o, i = B("one"), B("zz", 0, 512)
+            run("G", lambda e: e.affine_select(o[0], i[0], [[1, 512]], OP.not_equal, 1.0, -3, -4), [o], [i])
+            for b in range(4):
+                iota(B("dy", 272 * b + 256, 272 * b + 272), [[0, 16]], 0, 0)
+        half = lambda name, h: B(name, 128 * h, 128 * h + 128)
+        for h in range(2):
+            tt(half("sd", h), B("ps%d" % (3 + h), 0, 128), half("maskd", h), OP.add)
+        for h in range(2):
+            scan(half("sx", h), half("hd", h), half("sd", h), 0.0, OP.add, OP.min)
+        once(quant, "gq", 0, 128, B("gt"))
         mine = lambda m: B("sx", 16 * m + 15, 16 * m + 16)
-        blk = lambda name, m: B(name, 256 * m, 256 * m + 256)
-        for m in range(NA + 1):
-            if m < NA:
-                act(blk("sn", m), row(m), AF.Sign, scale=-1.0, bias=mine(m))
+        window = lambda m: (0, 16 * m) if m else (16, 32)
+        signs = lambda m: B("sn", 256 * m, 256 * m + max(16 * m, 16))
+        first = lambda m: act(signs(m), B("ps0" if m > 7 else "ps3", *window(m)), AF.Sign, scale=-1.0, bias=mine(m))
+
+        def second(m):
+            out = slot(m, 0, 16 * m) if m > 1 else B("spare", 16 * m, 16 * m + 16)
             if m:
-                act(blk("cm", m - 1), blk("sn", m - 1), AF.Sign, bias=1.0, accum=B("acc", m - 1, m))
-        tt(B("et"), B("ps1", 0, 256), B("sx"), OP.is_equal)
-        for m in range(NA, 17):
-            if m < 16:
-                ts(blk("cm", m), row(m), mine(m), None, OP.is_le)
-            if m == 16 and r == 0:
-                tt(B("z"), B("ps2", 0, 256), B("kz"), OP.add)
-            if m == NA:
-                scan(B("ets"), B("sg"), B("et"), 0.0, OP.mult, OP.add)
+                act(out, signs(m), AF.Relu, accum=B("acc", m, m + 1))
             else:
-                a = 256 * (m - 1)
-                scan(B("cs", a // 2, a // 2 + 128), B("cm", a, a + 128), B("cm", a + 128, a + 256), B("ets", 16 * m - 1, 16 * m), OP.add, OP.add)
-            if m == 12 and r == 0:
-                classes()
-        if r == 0:
-            quant("eq_", ROT, 128, B("rot"))
-        tt(B("cs", 127, 128 * NA, 128), B("ets", 15, 16 * NA, 16), B("acc", 0, NA), OP.add)
+                act(out, signs(m), AF.Sign, bias=1.0, accum=B("acc", m, m + 1))
+        act(B("ca", 0, 1024, 4), B("ps2", 0, 256), AF.Sign, bias=-2.0 ** -100)
+        blocks = [7, 6] + list(range(NA - 1, 7, -1)) + list(range(5, -1, -1))
+        for k in range(NA + LAG):
+            if k < NA:
+                first(blocks[k])
+            if k >= LAG:
+                second(blocks[k - LAG])
+        compare = lambda m: ts(slot(m, 0, 16 * m), B("ps1", 0, 16 * m), mine(m), None, OP.is_lt)
+        count = lambda m: scan(B("cs", 128 * m + 128 - 8 * m, 128 * m + 128), slot(m, 0, 8 * m), slot(m, 8 * m, 16 * m), B("ek", m, m + 1),
+                               OP.add, OP.add)
+
+        def sums(k):
+            m, a, n = TRI[k]
+            quant("cmq", a, n, B("cm", 4 * a, 4 * (a + n)))
+            mm(7, n, "gq", 128, "cmq", a, False, k == 2)
+        tt(B("ca", 1, 1024, 4), B("ps1", 0, 256), B("sx"), OP.is_gt)
+        for m in range(15, NA - 1, -1):
+            compare(m)
+            if m == 14:
+                scan(B("ets"), B("kbi", 0, 256), B("ca", 1, 1024, 4), 0.0, OP.min, OP.add)
+                once(group, 0, -1.0)
+                once(group, 1, -1.0)
+            if m == NA:
+                tt(B("ek"), B("kc"), B("ets", 15, 256, 16), OP.subtract)
+            if m == 13:
+                quant("btq", 0, 256, B("ca"))
+                mm(7, 256, "gq", 0, "btq", 0, True, False)
+                if r == 1:
+                    mm(2, 256, "ctq", CW, "btq", 0)
+        once(quant, "gq", 128, 128, B("gt"))
+        once(ts, B("a16"), B("a16"), pf(2), EPS, OP.is_equal, OP.mult)
+        once(ts, B("g8"), B("kbi", 0, 16), pf(4), None, OP.is_equal)
+        once(constants_a)
+        for m in range(15, NA - 1, -1):
+            if m == 13:
+                once(scan, B("mr"), B("tneg", 0, 256), B("t512", 1, 257), -512.0, OP.mult, OP.subtract)
+            for k in range(3):
+                if m == max(15 - EARLY[k], NA):
+                    sums(k)
+            count(m)
+        once(quant, "ctq", CW, 128, B("ct", 4 * CW, 4 * CW + 512))
+        once(mm, 2, 256, "ctq", CW, "btq", 0)
+        tt(B("mr", 15, 16 * NA, 16), B("ek", 0, NA), B("acc", 0, NA), OP.add)
+        ts(B("mr", 16 * NA + 15, 256, 16), B("cs", 128 * NA + 127, 2048, 128), -512.0, None, OP.add)
+        once(quant, "eq_", ROT, 128, B("rot"))
+        scan(B("cw"), B("ps7", 0, 256), B("mr"), -512.0, OP.max, OP.add)
+        tt(B("z"), B("ps2", 0, 256), B("kz"), OP.add)
+        l1, rl = B("l1"), B("cw", 15, 256, 16)
         if r == 1:
-            tt(B("z"), B("ps2", 0, 256), B("kz"), OP.add)
-        if r == 0:
-            unpacker(2)
-            constants_a()
-            dma("S", T.wq[:].bitcast(dt.uint8), T.wc[:], [B("wq")], [B("ets")])
-            dma("S", T.wqS[:], T.ws[:], [B("wqS")], [B("ets")])
-        else:
-            dma("S", T.vt[:], T.v[:], [B("vt")], [B("ets")])
-            unpack("fo", xq, "AAAA")
-        rl, l1 = B("cs", 127, 2048, 128), B("l1")
-        rounded(B("wk", 2, 64, 4), rl, 16)
-        ts(l1, rl, -1.0, None, OP.add)
-        if r == 0:
-            unpacker(3)
-        tt(B("wk", 3, 64, 4), rl, B("wk", 2, 64, 4), OP.subtract)
-        run("V", lambda e: e.tensor_copy(T.zs[:, 16:272].indirect(l1[0]), T.z[:]), [B("zs", 16, 272)], [B("z"), l1])
-        quant("rtq", 0, 128, B("wk", 0, 512))
-        digits(7, "rtq")
-        digits(0, "rtq", False)
-        cp(B("zs", 0, 16), B("zs", 256, 272))
-        cut = (MV, MV + 170, MV + 338, MV + 506)
-        third = lambda k: quant("ctq", cut[k], cut[k + 1] - cut[k], B("ct", 4 * cut[k], 4 * cut[k + 1]))
-        if r == 0:
-            third(0)
-        else:
             unpack("fp", px, "AAAA")
-        scan(B("tb"), B("ones"), B("zs"), 16.0, OP.add, OP.min)
-        ts(B("l2"), B("ps7", 0, 16), 1 / 32, -1.0, OP.mult, OP.add)
+        digit = lambda k, n: B("wk", 1 + 2 * k, 4 * n, 4)
+        rounded(digit(0, 16), rl, 32)
+        ts(l1, rl, 511.0, None, OP.add)
+        tt(digit(1, 16), rl, digit(0, 16), OP.subtract)
+        run("V", lambda e: e.tensor_copy(T.zs[:, 16:272].indirect(l1[0]), T.z[:]), [B("zs", 16, 272)], [B("z"), l1])
+        cut = (MV, TC + 2 * W, TC + 4 * W)
+        third = lambda k: quant("ctq", cut[k], cut[k + 1] - cut[k], B("ct", 4 * cut[k], 4 * cut[k + 1]))
+        quant("r2q", 0, 128, B("wk", 0, 512))
+        digits(7, 0)
+        digits(0, 0, False)
+        cp(B("zs", 0, 16), B("zs", 256, 272))
+        once(third, 0)
+        scan(B("tb"), B("ones"), B("zs"), OFF + 16.0, OP.add, OP.min)
+        ends = B("sh", 15, 272, 16)
+        ts(B("l2"), B("ps7", 0, 16), 1 / 32, 511.0, OP.mult, OP.add)
+        once(scan, B("mh"), B("tneg", 15, 287), B("t512", 0, 272), 0.0, OP.mult, OP.add)
+        ts(B("wk", 1, 256, 2), B("tb", 16, 272), -OFF, None, OP.add, off=B("l2", 0, 8))
+        act(B("wk", 257, 512, 2), B("tb", 16, 272), AF.Identity, bias=-OFF, off=B("l2", 8, 16))
+        once(bounds)
         if r == 0:
-            third(1)
-        ts(B("wk", 1, 512, 2), B("tb", 16, 272), pf(11), pf(11), OP.add, OP.subtract, B("l2"))
-        if r == 0:
-            scan(B("mh"), B("tneg", 15, 287), B("t512"), 0.0, OP.mult, OP.add)
+            dma("S", T.wq[:].bitcast(dt.uint8), T.wc[:], [B("wq")], [B(px)])
+            dma("S", T.wqS[:], T.ws[:], [B("wqS")], [B(px)])
+        else:
+            dma("S", T.vt[:], T.v[:], [B("vt")], [B("cw")])
+        own(B("sh"), B("zs"), 272)
         quant("ttq", 0, 128, B("wk", 0, 512))
         mm(1, 2 * W, "ttq", 0, "ctq", TC)
-        if r == 0:
-            third(2)
-        mm(2, 5 * W, "ttq", 0, "ctq", TC + 2 * W)
-        if r == 0:
-            unpack("fp", px, "AAAA")
-        own(B("sh"), B("zs"), 272)
-        ends = B("sh", 15, 272, 16)
+        once(third, 1)
+        mm(2, 2 * W, "ttq", 0, "ctq", TC + 2 * W)
+        quant("ttq", 128, 128, B("wk", 1, 513))
+        mm(7, 3 * W, "ttq", 128, "ctq", TC + W)
+        rounded(B("r256"), ends, 256 * COL)
 
         def order_list():
             ts(B(lo, 0, 17), B("r16"), 1 / COL, 127.5, OP.mult, OP.add)
             send([(B(plo, 0, 17), B(lo, 0, 17))], dst, "ro%d" % r, "lo%d" % r)
-        beside = {2: lambda: rounded(B("r256"), ends, 256 * COL),
-                  3: lambda: tt(B("r16"), ends, B("r256"), OP.subtract),
-                  4: order_list,
-                  5: lambda: ts(B("of"), B("r16"), 1 / COL, None, OP.mult),
-                  6: lambda: rounded(B("wk", 2, 68, 4), B("of"), 16),
-                  7: lambda: tt(B("wk", 3, 68, 4), B("of"), B("wk", 2, 68, 4), OP.subtract),
-                  8: lambda: (quant("r2q", 0, 128, B("wk", 0, 512)), digits(7, "r2q")),
-                  9: lambda: ts(B("li"), rl, 15.0, None, OP.add),
-                  10: lambda: ts(B("li"), B("li"), 255, None, OP.bitwise_and),
-                  11: lambda: (ts(B("l3"), B("ps7", 0, 17), 1 / 32, 127.5, OP.mult, OP.add), [waiting(h, b) for h, b in HB_EARLY]),
-                  12: lambda: cp(B("l5"), B("li"))}
+        small = [lambda: tt(B("r16"), ends, B("r256"), OP.subtract),
+                 order_list,
+                 lambda: rounded(digit(0, 17), B("r16"), 16 * COL),
+                 lambda: tt(digit(1, 17), B("r16"), digit(0, 17), OP.subtract),
+                 lambda: (quant("r2q", 0, 128, B("wk", 0, 512)), digits(1, 0)),
+                 lambda: (ts(B("li"), rl, 512.0 + 15.0, None, OP.add), [waiting(0, b) for b in range(4)]),
+                 lambda: (ts(B("l3"), B("ps1", 0, 17), 1 / 32 / COL, 127.5, OP.mult, OP.add), waiting(1, 1)),
+                 lambda: ts(B("li"), B("li"), 255, None, OP.bitwise_and),
+                 lambda: cp(B("l5"), B("li"))]
         if r == 0:
-            beside[13] = lambda: ts(pf(7), pf(1), 15.0, 256.0, OP.is_lt, OP.mult)
+            small[2:2] = [lambda: unpacker(0), lambda: unpacker(1), lambda: unpacker(2), lambda: (unpacker(3), unpack("fp", px, "AAAA"))]
+        beside = dict(enumerate(small, 2))
         waiting = lambda h, b: mm(HB[h][b], 128, "eq_", UNP[b], xq, 128 * h, True, False)
         sort = lambda q, b: gather(q, B("fs", 272 * b, 272 * b + 272), B("fp", 256 * b, 256 * b + 256), B(plo, 0, 17))
         for k in range(1, 8):
-            if k in SORT_AT:
-                sort("A", SORT_AT.index(k))
             c = WS * (k - 1)
-            p = B("ps1", W * (k - 1), W * k) if k < 3 else B("ps2", W * (k - 3), W * (k - 2))
+            bank, at = (1, k - 1) if k < 3 else (2, k - 3) if k < 5 else (7, k - 5)
+            p = B("ps%d" % bank, W * at, W * at + W)
             scan(B("so", c, c + W), p, B("fb", c, c + W), EPS / 128, OP.subtract, OP.min)
             beside.get(2 * k, lambda: None)()
             if k < 7:
@@ -438,20 +487,86 @@ def rank_program(g, core, T, topo):
             beside.get(2 * k + 1, lambda: None)()
             for h in range(2):
                 a = c + H1 * h
-                act(B("wk", 513 + 64 * k + 4 * h, 576 + 64 * k, 8), B("mneg"), AF.Relu, scale=B("so", a + 15, a + 16), bias=B("so", a + 33, a + 34))
-        quant("exq", 0, 128, B("wk", 512, 1024))
+                act(B("ex", 1 + 64 * k + 4 * h, 64 + 64 * k, 8), B("mneg"), AF.Relu, scale=B("so", a + 15, a + 16), bias=B("so", a + 33, a + 34))
+            if k in SORT_AT[r]:
+                sort("A", SORT_AT[r].index(k))
+            if k == 2 and r == 1:
+                gather("A", B("orow"), B("ramp"), B(lo, 0, 17))
+        quant("exq", 0, 128, B("ex"))
         mm(0, 128, "exq", 0, "ctq", MV, False, True)
-        ts(B(lq), B("ps0", 0, 16), 1 / 32, 15.25, OP.mult, OP.add)
+        ts(B(lq), B("ps0", 0, 16), 1 / 32, 512 + 15.25, OP.mult, OP.add)
         send([(B(plq), B(lq))], dst, "rl%d" % r, "ll%d" % r)
         waiting(1, 2)
+        waiting(1, 3)
         waiting(1, 0)
-        for b in range(len(SORT_AT), 4 - SV):
+        if OLDB:
+            for b in range(len(SORT_AT[r]), 4):
+                sort("A", b)
+            tt(B("key"), B("maskd", 0, 272), B("ramp", 0, 256), OP.add, off=B(lq))
+            if r == 1:
+                gather("A", B("srow"), B("orow"), B(lq))
+                dma("S", T.src[:], T.srow[0:128:16, :], [], [B("srow")])
+            if NAS[1] < NAS[0]:
+                once(ts, B("kc", NAS[1], NAS[0]), B("kc", NAS[1], NAS[0]), 512.0, None, OP.add)
+            gather("V", B("av", 0, 128), B("key"), B("l3", 0, 8))
+            gather("A", B("av", 128, 272), B("key"), B("l3", 8, 17))
+            mosaic = lambda h, b: gather("VVAA"[b], B("zt", 512 * h + b, 512 * h + 512, 4), B("fs", 272 * b, 272 * b + 272), B(plq, 8 * h, 8 * h + 8))
+
+            def layer(h):
+                quant(zq, 128 * h, 128, B("zt", 512 * h, 512 * h + 512))
+                for b in range(4):
+                    mm(HB[h][b], 128, "wq", 128 * b, zq, 128 * h, False, True)
+            for b in range(4):
+                mosaic(0, b)
+            mosaic(1, 0)
+            layer(0)
+            for b in range(1, 4):
+                mosaic(1, b)
+            scan(B("s1"), B("t256", 0, 272), B("av"), 256.0, OP.max, OP.min)
+            layer(1)
+            own(B("s2"), B("s1", 15, 271), 256)
+            for h in range(2):
+                for b in range(4):
+                    scaled(YT[h][b], B("yt", 512 * h + b, 512 * h + 512, 4), B("ps%d" % HB[h][b], 0, 128), 0.03125)
+                if h == 0:
+                    ts(B("lt"), B("s2", 15, 256, 16), pf(7), None, OP.add)
+                quant(yq, 128 * h, 128, B("yt", 512 * h, 512 * h + 512))
+                q = (128 * h, 128 * h + 128)
+                send([(U8(B(py, *q)), U8(B(yq, *q))), (B(py + "S", *q), B(yq + "S", *q))], dst, "ry%d%d" % (r, h), "ly%d%d" % (r, h))
+            gather("A", B("rowt"), B("ramp"), B("lt"))
+            gather("A", B("rowk"), B("rowt"), B("l5"))
+            if r == 0:
+                quant("eq_", ONE[3], 128, B("one"))
+            else:
+                quant("vq", 0, 128, B("vt"))
+            unpack("fo", xq, "VVV")
+            own(B("s3"), B("rowk"), 256)
+            for h in range(2):
+                for b in range(4):
+                    mm(HB[1 - h][b], 128, "eq_", UNP[b], py, 128 * h)
+            for h in range(2):
+                for b in range(4):
+                    scaled(DY[h][b], B("dy", 272 * b + 128 * h, 272 * b + 128 * h + 128), B("ps%d" % HB[1 - h][b], 0, 128), 1 / 32)
+                if h == 0:
+                    ts(B("l4"), B("s3", 15, 256, 16), pf(7), None, OP.add)
+            xn = "x%d" % (r + 1)
+            mm(0, 256, "eq_", ONE[3], xq, 0)
+            gather("A", B("tk", 0, 256), B("dy", 272 * 3, 272 * 4), B("l4"))
+            for b in range(3):
+                tt(B(xn, b, 1024, 4), B("dy", 272 * b, 272 * b + 272), B("fo", 256 * b, 256 * b + 256), OP.add, off=B("l4"))
+            for h in range(2):
+                tt(B(xn, 512 * h + 3, 512 * h + 512, 4), B("ps0", 128 * h, 128 * h + 128), B("tk", 128 * h, 128 * h + 128), OP.add)
+            for h in range(2):
+                quant("xq" + L[r + 1], 128 * h, 128, B(xn, 512 * h, 512 * h + 512))
+            continue
+        for b in range(4 - SV):
             sort("A", b)
         tt(B("key"), B("maskd", 0, 272), B("ramp", 0, 256), OP.add, off=B(lq))
-        if AV == 0:
-            gather("A", B("av"), B("key"), B("l3"))
         for b in range(4 - SV, 4):
             sort("V", b)
+        once(ts, B("t256"), B("kbi"), pf(1), 256.0, OP.is_equal, OP.mult)
+        gather("V", B("av"), B("key"), B("l3"))
+        scan(B("s1"), B("t256", 0, 272), B("av"), 256.0, OP.max, OP.min)
         def mosaic(h, b):
             gather(ZT[h][b], B("zt", 512 * h + b, 512 * h + 512, 4), B("fs", 272 * b, 272 * b + 272), B(plq, 8 * h, 8 * h + 8))
 
@@ -465,46 +580,45 @@ def rank_program(g, core, T, topo):
         layer(0)
         for b in range(1, 4):
             mosaic(1, b)
-        steps = [lambda: scan(B("s1"), B("t256", 0, 272), B("av"), 256.0, OP.max, OP.min), lambda: own(B("s2"), B("s1", 15, 271), 256),
-                 lambda: ts(B("lt"), B("s2", 15, 256, 16), pf(7), None, OP.add), lambda: None]
-        if AV == 0:
-            steps.pop(0)()
-        else:
-            gather("A", B("av"), B("key"), B("l3"))
         layer(1)
-        if AV == 0:
-            steps.pop(0)()
         for h in range(2):
             for b in range(4):
                 scaled(YT[h][b], B("yt", 512 * h + b, 512 * h + 512, 4), B("ps%d" % HB[h][b], 0, 128), 0.03125)
-            steps.pop(0)()
             quant(yq, 128 * h, 128, B("yt", 512 * h, 512 * h + 512))
             q = (128 * h, 128 * h + 128)
             send([(U8(B(py, *q)), U8(B(yq, *q))), (B(py + "S", *q), B(yq + "S", *q))], dst, "ry%d%d" % (r, h), "ly%d%d" % (r, h))
-        for f in steps:
-            f()
-        gather("A", B("rowt"), B("ramp"), B("lt"))
-        gather("A", B("rowk"), B("rowt"), B("l5"))
+        own(B("s2"), B("s1", 15, 271), 256)
+        for b in range(4):
+            once(act, B("dy", 272 * b + 256, 272 * b + 272), B("zz", 0, 16))
+        unpack("fo", xq, "AA")
+        ts(B("lt"), B("s2", 15, 256, 16), pf(7), None, OP.add)
+        once(ts, B("ebig", 0, 516), B("ebig", 0, 516), 1 / 32, None, OP.mult)
+        gather("V", B("rowt"), B("ramp"), B("lt"))
+        once(quant, "eq_", ONE[2], 128, B("ebig", 2, 514))
+        gather("V", B("rowk"), B("rowt"), B("l5"))
         if r == 0:
-            unpack("fo", xq, "VVVV")
+            quant("eq_", ONE[3], 128, B("ebig", 1, 513))
         else:
             quant("vq", 0, 128, B("vt"))
+            gather("A", B("orow"), B("ramp"), B(lo, 0, 17))
+            gather("A", B("srow"), B("orow"), B(lq))
+            dma("S", T.src[:], T.srow[0:128:16, :], [], [B("srow")])
         own(B("s3"), B("rowk"), 256)
+        ts(B("l4"), B("s3", 15, 256, 16), pf(7), None, OP.add)
         for h in range(2):
             for b in range(4):
                 mm(HB[1 - h][b], 128, "eq_", UNP[b], py, 128 * h)
         for h in range(2):
             for b in range(4):
                 scaled(DY[h][b], B("dy", 272 * b + 128 * h, 272 * b + 128 * h + 128), B("ps%d" % HB[1 - h][b], 0, 128), 1 / 32)
-            if h == 0:
-                ts(B("l4"), B("s3", 15, 256, 16), pf(7), None, OP.add)
         xn = "x%d" % (r + 1)
-        if r == 1:
-            gather("A", B("orow"), B("ramp"), B(lo, 0, 17))
-            gather("A", B("srow"), B("orow"), B(lq))
-            dma("S", T.src[:], T.srow[0:128:16, :], [], [B("srow")])
-        for b in range(4):
+        for b in (2, 3):
+            mm(b - 2, 256, "eq_", ONE[b], xq, 0)
+            gather("A", B("tk", 256 * b - 512, 256 * b - 256), B("dy", 272 * b, 272 * b + 272), B("l4"))
+        for b in (0, 1):
             tt(B(xn, b, 1024, 4), B("dy", 272 * b, 272 * b + 272), B("fo", 256 * b, 256 * b + 256), OP.add, off=B("l4"))
+        for b in (2, 3):
+            tt(B(xn, b, 1024, 4), B("ps%d" % (b - 2), 0, 256), B("tk", 256 * b - 512, 256 * b - 256), OP.add)
         quant("xq" + L[r + 1], 0, 256, B(xn))
     dma("S", T.oc[:], T.xqc[:].bitcast(dt.uint8), [], [B("xqc")])
     for k in range(4):
@@ -512,7 +626,7 @@ def rank_program(g, core, T, topo):
     for h in range(2):
         mm(2 + h, 128, "vq", 0, "xqc", 128 * h)
     for h in range(2):
-        cp(B("yout", 128 * h, 128 * h + 128), B("ps%d" % (2 + h), 0, 128))
+        (cp, act)[h](B("yout", 128 * h, 128 * h + 128), B("ps%d" % (2 + h), 0, 128))
     dma("S", T.y[:], T.yout[:], [], [B("yout")])
     for q in ("G", "P", "A", "V"):
         need("G", q, cnt[q])

import numpy as np
from concourse.bass import DstId, RemoteDMATransfer
from concourse.mybir import dt, AluOpType, AxisListType, ActivationFunctionType

OP = AluOpType
AF = ActivationFunctionType
BIG = 2.0 ** 90


def grid(step):
    return 1.5 * 2.0 ** 23 * step


EPS = 2.0 ** -7
COL = 2.0 ** -13
W, H1, WS = 70, 36, 72
LATE = 3
LAG = 3
EARLY = (0, 0, 4)
NAS = [11, 10]
SORT_AT = [[], [4, 5]]
ZT, YT, DY = ["VVAA", "VVAA"], ["AVAV", "AAAV"], ["VAVA", "VAAA"]
SV = 0
HB_EARLY = [(0, 0), (0, 1), (0, 2), (0, 3), (1, 1)]
STEP = [1, 2]
OLDB = 1

F4, BF, I4, U2, CODE, U1 = "float32", "bfloat16", "int32", "uint16", "float8_e4m3fn_x4", "uint8"
SCRATCH, PART = {}, {}


def _add(dtype, **bufs):
    for k, n in bufs.items():
        SCRATCH[k] = ("sbuf", [128, n], dtype)


def _pieces(base, dtype, **bufs):
    at = 0
    for k, n in bufs.items():
        PART[k] = (base, at, n)
        at += (n + 15) // 16 * 16
    SCRATCH[base] = ("sbuf", [128, at], dtype)


_add(BF, x0=1024, x1=1024, x2=1024, ut=512, vt=512, zz=516, wk=516, ex=512, ct=1696, ebig=516, rot=512, kbi=288, ramp=272, ones=272, t256=288, t512=288,
     tneg=288, mh=272, one=512, ets=256, sn=4096, ca=1024, cm=4 * 480, cs=2048, fo=1024, fp=1024, fs=1088, zt=1024, yt=1024, dy=1088, tk=512,
     fb=7 * WS, sig=2 * W, av=272, s1=272, s2=256, rowt=256, rowk=256, s3=256, orow=272, tb=272, gi=128, gt=512, cb4=64, spare=32)
_add(F4, maskd=288, hd=256, kz=256, sd=256, sx=256, cw=256, mr=256, z=256, zs=272, sh=272, so=7 * WS, key=256, srow=256, yout=256)
_pieces("f4s", F4, pf=16, cb0=16, cb1=16, cb2=16, gm=8, g8=16, a16=16, mneg=8, acc=16, r16=17, r256=17, of=17, kc=16, ek=16, rh=16)
_pieces("i4s", I4, ip=1, pi=4, iu=8, li=16)
_pieces("u2s", U2, ul=8, l5=16, l3=17, l4=16, lt=16)
_add(U2, l1=16, l2=16, lq0=16, lq1=16, plq0=16, plq1=16, lo0=32, lo1=32, plo0=32, plo1=32)
for _n, _w in (("uq", 128), ("ur", 128), ("vq", 128), ("wq", 512), ("xqa", 256), ("xqb", 256), ("xqc", 256), ("pxa", 256), ("pxb", 256),
               ("ctq", 634), ("eq_", 896), ("btq", 256), ("cmq", 480), ("gq", 256), ("ttq", 256), ("r2q", 128),
               ("exq", 128), ("zqa", 256), ("zqb", 256), ("yqa", 256), ("yqb", 256), ("pya", 256), ("pyb", 256)):
    SCRATCH[_n] = ("sbuf", [128, _w], CODE)
    SCRATCH[_n + "S"] = ("sbuf", [128, _w], U1)
for _k in range(8):
    SCRATCH["ps%d" % _k] = ("psum", [128, 512], F4)
UNP = (0, 128, 256, 384)
ROT = 512
DIG = (0, 18, 36, 52)
ONE = {2: 640, 3: 768}
CW, MV, TC = 0, 128, 144
OFF = 192.0
TRI = ((13, 0, 208), (9, 208, 144), (5, 352, 128))

NDMA = 20
SEMAPHORES = (["V", "A", "P", "G"] + ["d%d" % k for k in range(NDMA)]
              + [k + "%d" % r for k in ("rx", "lx", "rl", "ll", "ro", "lo") for r in (0, 1)]
              + [k + "%d%d" % (r, h) for k in ("ry", "ly") for r in (0, 1) for h in (0, 1)])


def rank_program(g, core, T, topo):
    rank = T.rank_of(core)
    if rank is None:
        return
    eng = {"V": g.vector, "A": g.scalar, "P": g.tensor, "G": g, "S": g.sync}
    cnt = {"V": 0, "A": 0, "P": 0, "G": 0}
    seen = {q: {} for q in eng}
    log = {}
    ndma = [0]
    final = {}

    def B(name, a=0, b=None, s=1):
        if name in PART:
            base, at, n = PART[name]
            name, a, b = base, a + at, at + (n if b is None else b)
        elif b is None:
            b = SCRATCH[name][1][1]
        ap = T[name][:, a:b] if s == 1 else T[name][:, a:b:s]
        return (ap, name, a, b, s)

    def U8(v):
        return (v[0].bitcast(dt.uint8),) + v[1:]

    def clash(u, v):
        if u[3] <= v[2] or v[3] <= u[2]:
            return False
        return not (u[4] > 1 and v[4] > 1 and not set(range(*u[2:])) & set(range(*v[2:])))

    def need(q, sem, val):
        if seen[q].get(sem, 0) < val:
            eng[q].wait_ge(T.sem[sem], val)
            seen[q][sem] = val

    def order(q, reads, writes, free=()):
        wants = {}
        for kind, views in (("r", reads), ("w", writes)):
            for v in views:
                ps = v[1][:2] == "ps"
                for k, u, uq, sem, val in log.get(v[1], ()):
                    if ps:
                        hit = uq != q or ((kind, k) != ("r", "r") and (kind == "r" or k == "r" or v[1] not in free))
                    else:
                        hit = (kind, k) != ("r", "r") and clash(v, u)
                    if hit:
                        wants[sem] = max(val, wants.get(sem, 0))
        for sem, val in wants.items():
            need(q, sem, val)

    def note(q, reads, writes, sem, val):
        for v in writes:
            old = log.get(v[1], [])
            keep = [e for e in old if not (v[1][:2] == "ps" or (v[4] == 1 and v[2] <= e[1][2] and e[1][3] <= v[3])
                                           or (v[4] == e[1][4] and v[2] == e[1][2] and v[3] == e[1][3]))]
            log[v[1]] = keep + [("w", v, q, sem, val)]
        for v in reads:
            log.setdefault(v[1], []).append(("r", v, q, sem, val))

    def run(q, fn, outs, ins, free=()):
        order(q, ins, outs, free)
        cnt[q] += 1
        fn(eng[q]).then_inc(T.sem[q], 1)
        note(q, ins, outs, q, cnt[q])

    def dma(q, out, in_, outs, ins):
        order(q, ins, outs)
        sem = "d%d" % ndma[0]
        ndma[0] += 1
        eng[q].dma_start(out, in_).then_inc(T.sem[sem], 16)
        final[sem] = 16
        note(q, ins, outs, sem, 16)

    def picked(a, off):
        return (a[0], [a]) if off is None else (a[0].indirect(off[0]), [a, off])

    def ts(out, a, s1, s2, op0, op1=None, off=None):
        src, ins = picked(a, off)
        ins = ins + [s for s in (s1, s2) if isinstance(s, tuple)]
        v1, v2 = [s[0] if isinstance(s, tuple) else s for s in (s1, s2)]
        if op1 is None:
            run("V", lambda e: e.tensor_scalar(out[0], src, v1, None, op0), [out], ins)
        else:
            run("V", lambda e: e.tensor_scalar(out[0], src, v1, v2, op0, op1), [out], ins)

    def tt(out, a, b, op, off=None):
        src, ins = picked(a, off)
        run("V", lambda e: e.tensor_tensor(out[0], src, b[0], op), [out], ins + [b])

    def cp(out, a, off=None):
        src, ins = picked(a, off)
        run("V", lambda e: e.tensor_copy(out[0], src), [out], ins)

    def scan(out, a, b, init, op0, op1):
        col = isinstance(init, tuple)
        run("V", lambda e: e.tensor_tensor_scan(out[0], a[0], b[0], init[0] if col else init, op0, op1), [out], [a, b] + [init] * col)

    def fill(out, c):
        run("V", lambda e: e.memset(out[0], c), [out], [])

    def rounded(out, a, step, off=None):
        ts(out, a, grid(step), grid(step), OP.add, OP.subtract, off)

    def quant(code, a, n, tile):
        run("V", lambda e: e.quantize_mx(T[code][:, a:a + n], T[code + "S"][:, a:a + n], tile[0]),
            [B(code, a, a + n), B(code + "S", a, a + n)], [tile])

    def act(out, a, func=AF.Copy, scale=1.0, bias=None, accum=None, off=None):
        src, ins = picked(a, off)
        ins = ins + [s for s in (scale, bias) if isinstance(s, tuple)]
        outs = [out] + ([accum] if accum is not None else [])
        kw = {}
        if bias is not None:
            kw["bias"] = bias[0] if isinstance(bias, tuple) else bias
        if isinstance(scale, tuple):
            kw["scale"] = scale[0]
        elif scale != 1.0:
            kw["scale"] = scale
        if accum is not None:
            kw["accum_out"] = accum[0]
        run("A", lambda e: e.activation(out[0], src, func, **kw), outs, ins)

    def mm(bank, n, st, a, mvg, b, start=True, stop=True):
        name = "ps%d" % bank
        run("P", lambda e: e.matmul_mx(T[name][:, 0:n], T[st][:, a:a + 128], T[st + "S"][:, a:a + 128],
                                       T[mvg][:, b:b + n], T[mvg + "S"][:, b:b + n], start, stop),
            [B(name, 0, n)], [B(st, a, a + 128), B(st + "S", a, a + 128), B(mvg, b, b + n), B(mvg + "S", b, b + n)],
            free=() if start else (name,))

    def digits(bank, k, stop=True):
        mm(bank, 128, "eq_", ROT, "r2q", 0, True, stop)

    def scaled(q, out, a, c):
        if q == "V":
            ts(out, a, c, None, OP.mult)
        else:
            act(out, a, scale=c)

    def unpack(name, code, queues):
        for b in range(len(queues)):
            mm(3 + b, 256, "eq_", UNP[b], code, 0)
        for b in range(len(queues)):
            scaled(queues[b], B(name, 256 * b, 256 * b + 256), B("ps%d" % (3 + b), 0, 256), 1 / 32)

    def gather(q, out, win, off):
        (cp if q == "V" else act)(out, win, off=off)

    def iota(out, pattern, base, cm):
        out = B(out) if isinstance(out, str) else out
        if SCRATCH[out[1]][2] != I4:
            run("G", lambda e: e.iota(out[0], pattern, base, cm, allow_small_or_imprecise_dtypes=True), [out], [])
        else:
            run("G", lambda e: e.iota(out[0], pattern, base, cm), [out], [])

    def unpacker(b):
        quant("eq_", UNP[b], 128, B("ebig", 4 - b, 516 - b))

    def send(parts, dst, rsem, lsem):
        engs = topo.engines(core, dst)
        rid, pid, _s = topo.addr(dst)
        m = topo.mask(core, dst)
        order("G", [s for d, s in parts], [])
        tot = 0
        for d, s in parts:
            g.remote_dma(d[0], s[0], T.sem[rsem], T.sem[lsem], pid, rid, m)
            tot += len(engs)
        final[lsem] = tot
        final[rsem] = tot
        for d, s in parts:
            note("G", [s], [], lsem, tot)
            note("R", [], [d], rsem, tot)

    def own(out, row, n):
        scan(out, B("mh", 0, n), row, 0.0, OP.add, OP.min)

    dma("S", T.x0[:], T.x[:], [B("x0")], [])
    dma("A", T.ut[:], T.u[:], [B("ut")], [])
    iota("ip", [[0, 1]], 0, 1)
    iota("iu", [[16, 8]], 0, 0)
    iota("kbi", [[0, 18], [1, 16]], 0, 0)
    iota("cb0", [[0, 8], [-32, 2]], 16, 0)
    iota("cb1", [[0, 4], [-32, 2], [0, 2]], 16, 0)
    iota("cb2", [[0, 2], [-32, 2], [0, 4]], 16, 0)
    iota("gi", [[1, 8], [0, 16]], 0, 0)
    NA = NAS[0]
    iota(B("kc", 0, 1), [[0, 1]], 240 - 512, 0)
    iota(B("kc", 1, NA), [[-16, NA - 1]], 240 - 512, 0)
    iota(B("kc", NA, 16), [[-16, 16 - NA]], 256 - 16 * NA, 0)
    iota("a16", [[1, 8], [0, 2]], 0, 0)
    iota("ramp", [[1, 272]], 0, 0)
    fill(B("zz"), 0.0)
    o, i = B("ebig"), B("zz")
    run("G", lambda e: e.affine_select(o[0], i[0], [[1, 516]], OP.not_equal, 32.0, -4, -4), [o], [i])
    for o, n, base in ((B("rot", 0, 448), 112, -1016), (B("rot", 448, 512), 16, -1000)):
        i = B("zz", 0, 4 * n)
        run("G", lambda e: e.affine_select(o[0], i[0], [[-1, n], [0, 2], [1000, 2]], OP.not_equal, 32.0, base, 1), [o], [i])
    pf = lambda k: B("pf", k, k + 1)
    for k, (c, op) in enumerate(((15, OP.bitwise_and), (7, OP.bitwise_and), (4, OP.arith_shift_right), (3, OP.arith_shift_right))):
        ts(B("pi", k, k + 1), B("ip"), c, None, op)
    cp(B("ul"), B("iu"))
    fill(B("cb4"), 0.0)
    fill(B("ca", 896, 1024), 0.0)
    cp(B("pf", 1, 5), B("pi"))
    tail = [B("cm", 4 * a + 64 * (m - 3), 4 * (a + n)) for m, a, n in TRI]
    fill(tail[2], 0.0)
    fill(B("gt", 0, 512, 4), 0.0)
    ts(pf(5), pf(1), -BIG, None, OP.mult)
    ts(B("pf", 8, 11), B("kbi", 1, 4), pf(1), None, OP.is_equal)
    ts(B("gm"), B("kbi", 0, 8), pf(3), None, OP.is_equal)
    ts(pf(6), pf(1), 8.0, None, OP.is_ge)
    act(B("ones"), B("zz", 0, 272), AF.Identity, bias=1.0)
    act(B("hd"), B("kbi", 0, 256), AF.Relu, scale=-BIG, bias=BIG)
    act(B("maskd"), B("kbi"), AF.Abs, scale=BIG, bias=pf(5))
    act(pf(12), pf(6), AF.Identity, -32.0 - 1 / 16, OFF + 32.0 - 127.5 * COL)
    for v in [B("wk"), B("sig"), B("ct", 4 * MV, 4 * (TC + W)), B("ex")]:
        z = B("zz", 0, v[3] - v[2])
        dma("S", v[0], z[0], [v], [z, B("x0")])
    for b in range(2):
        ts(B("cb%d" % b), B("cb%d" % b), pf(8 + b), None, OP.mult)
    quant("uq", 0, 128, B("ut"))
    ts(B("cb2"), B("cb2"), pf(10), None, OP.mult)
    tt(B("cb0"), B("cb0"), B("cb1"), OP.add)
    fill(tail[0], 0.0)
    ul = B("ul")
    run("V", lambda e: e.tensor_copy(T.ur[:].bitcast(dt.uint32), T.uq[:].bitcast(dt.uint32).indirect(ul[0])), [B("ur")], [B("uq"), ul])
    run("A", lambda e: e.activation(T.urS[:], T.uqS[:].indirect(ul[0]), AF.Copy), [B("urS")], [B("uqS"), ul])
    act(B("t512"), B("maskd"), AF.Relu, scale=-1.0, bias=512.0)
    tt(B("cb0"), B("cb0"), B("cb2"), OP.add)
    fill(tail[1], 0.0)
    ts(pf(7), pf(1), 15.0, 256.0, OP.is_lt, OP.mult)
    group = lambda t, c: ts(B("gt", t, 512, 4), B("gi"), pf(3), c, OP.is_equal, OP.mult)
    group(1, 1.0)
    cp(B("cb4", 0, 32, 4), B("cb0", 0, 8))
    ts(B("cb4", 32, 64, 4), B("cb0", 8, 16), 5 / 512, None, OP.mult)
    for h in range(2):
        quant("xqa", 128 * h, 128, B("x0", 512 * h, 512 * h + 512))
    group(2, -1.0)
    group(3, -1.0)
    ts(B("kc"), B("kc"), pf(1), pf(7), OP.subtract, OP.subtract)
    act(B("tneg"), B("t512"), scale=-1 / 1024)
    for gg in range(8):
        act(B("ct", 4 * CW + 64 * gg, 4 * CW + 64 * gg + 64), B("cb4"), scale=B("gm", gg, gg + 1))

    def constants_a():
        act(B("kz"), B("ramp", 0, 256), AF.Identity, COL, pf(12))
        act(pf(11), B("g8", 2, 3), AF.Identity, bias=B("g8", 1, 2))
        for k, (lower, upper) in enumerate(((-1.0, 32.0), (1.0, 128.0))):
            act(pf(13 + k), pf(6), AF.Identity, scale=upper - lower, bias=lower)
        for h in range(2):
            for part in range(2):
                at = 2 * H1 * h + h + 34 * part
                act(B("sig", at, at + 32, 2), B("a16"), scale=pf(13 + part))
        for gg in (2, 5, 1, 3, 4, 6, 7):
            at = 4 * (TC + W * (gg - 1)) + 1 if gg < 5 else 4 * (TC + W * (gg - 4))
            act(B("ct", at, at + 4 * W - 1, 2), B("sig"), scale=B("g8", 2 * gg, 2 * gg + 1) if gg > 1 else pf(11))
            if gg == 1:
                act(B("ct", 4 * MV + 1, 4 * MV + 64, 4), B("g8"), scale=-32 * 16 / EPS)
        act(B("mneg"), B("a16", 0, 16, 2), AF.Identity, scale=1 / EPS, bias=-17 / 16)
        act(B("fb"), B("zz", 0, 7 * WS), AF.Identity, bias=1.0)

    def bounds():
        for v, n, c in ((B("fb", 33, 7 * WS, H1), 14, EPS), (B("fb", 0, 16, 2), 8, 0.0), (B("fb", H1, H1 + 16, 2), 8, 0.0),
                        (B("fb", 35, 7 * WS, WS), 7, EPS / 128)):
            act(v, B("zz", 0, n), AF.Identity, bias=c)
        act(B("t256"), B("t512"), scale=0.5)

    def slot(m, a, b):
        if m > TRI[0][0]:
            return B("ca", 4 * a + 17 - m, 4 * b, 4)
        top, at, n = [e for e in TRI if e[0] >= m][-1]
        return B("cm", 4 * (at + a) + top - m, 4 * (at + b), 4)

    HB = ((3, 4, 5, 6), (0, 1, 2, 7))
    for r in range(2):
        dst = T.cores[rank ^ STEP[r]]
        L, NA = "abc", NAS[r]
        xq, px, zq, yq, py = "xq" + L[r], "px" + L[r], "zq" + L[r], "yq" + L[r], "py" + L[r]
        lq, plq, lo, plo = "lq%d" % r, "plq%d" % r, "lo%d" % r, "plo%d" % r
        once = (lambda f, *a: f(*a)) if r == 0 else (lambda f, *a: None)
        for h in range(2):
            mm(3 + h, 128, "ur", 0, xq, 128 * h)
        mm(2, 256, "uq", 0, xq, 0)
        mm(1, 256, "ur", 0, xq, 0)
        mm(0, 256, "ur", 0, xq, 0)
        send([(U8(B(px)), U8(B(xq))), (B(px + "S"), B(xq + "S"))], dst, "rx%d" % r, "lx%d" % r)
        if r == 0:
            o, i = B("one"), B("zz", 0, 512)
            run("G", lambda e: e.affine_select(o[0], i[0], [[1, 512]], OP.not_equal, 1.0, -3, -4), [o], [i])
            for b in range(4):
                iota(B("dy", 272 * b + 256, 272 * b + 272), [[0, 16]], 0, 0)
        half = lambda name, h: B(name, 128 * h, 128 * h + 128)
        for h in range(2):
            tt(half("sd", h), B("ps%d" % (3 + h), 0, 128), half("maskd", h), OP.add)
        for h in range(2):
            scan(half("sx", h), half("hd", h), half("sd", h), 0.0, OP.add, OP.min)
        once(quant, "gq", 0, 128, B("gt"))
        mine = lambda m: B("sx", 16 * m + 15, 16 * m + 16)
        window = lambda m: (0, 16 * m) if m else (16, 32)
        signs = lambda m: B("sn", 256 * m, 256 * m + max(16 * m, 16))
        first = lambda m: act(signs(m), B("ps0" if m > 7 else "ps3", *window(m)), AF.Sign, scale=-1.0, bias=mine(m))

        def second(m):
            out = slot(m, 0, 16 * m) if m > 1 else B("spare", 16 * m, 16 * m + 16)
            if m:
                act(out, signs(m), AF.Relu, accum=B("acc", m, m + 1))
            else:
                act(out, signs(m), AF.Sign, bias=1.0, accum=B("acc", m, m + 1))
        act(B("ca", 0, 1024, 4), B("ps2", 0, 256), AF.Sign, bias=-2.0 ** -100)
        blocks = [7, 6] + list(range(NA - 1, 7, -1)) + list(range(5, -1, -1))
        for k in range(NA + LAG):
            if k < NA:
                first(blocks[k])
            if k >= LAG:
                second(blocks[k - LAG])
        compare = lambda m: ts(slot(m, 0, 16 * m), B("ps1", 0, 16 * m), mine(m), None, OP.is_lt)
        count = lambda m: scan(B("cs", 128 * m + 128 - 8 * m, 128 * m + 128), slot(m, 0, 8 * m), slot(m, 8 * m, 16 * m), B("ek", m, m + 1),
                               OP.add, OP.add)

        def sums(k):
            m, a, n = TRI[k]
            quant("cmq", a, n, B("cm", 4 * a, 4 * (a + n)))
            mm(7, n, "gq", 128, "cmq", a, False, k == 2)
        tt(B("ca", 1, 1024, 4), B("ps1", 0, 256), B("sx"), OP.is_gt)
        for m in range(15, NA - 1, -1):
            compare(m)
            if m == 14:
                scan(B("ets"), B("kbi", 0, 256), B("ca", 1, 1024, 4), 0.0, OP.min, OP.add)
                once(group, 0, -1.0)
                once(group, 1, -1.0)
            if m == NA:
                tt(B("ek"), B("kc"), B("ets", 15, 256, 16), OP.subtract)
            if m == 13:
                quant("btq", 0, 256, B("ca"))
                mm(7, 256, "gq", 0, "btq", 0, True, False)
                if r == 1:
                    mm(2, 256, "ctq", CW, "btq", 0)
        once(quant, "gq", 128, 128, B("gt"))
        once(ts, B("a16"), B("a16"), pf(2), EPS, OP.is_equal, OP.mult)
        once(ts, B("g8"), B("kbi", 0, 16), pf(4), None, OP.is_equal)
        once(constants_a)
        for m in range(15, NA - 1, -1):
            if m == 13:
                once(scan, B("mr"), B("tneg", 0, 256), B("t512", 1, 257), -512.0, OP.mult, OP.subtract)
            for k in range(3):
                if m == max(15 - EARLY[k], NA):
                    sums(k)
            count(m)
        once(quant, "ctq", CW, 128, B("ct", 4 * CW, 4 * CW + 512))
        once(mm, 2, 256, "ctq", CW, "btq", 0)
        tt(B("mr", 15, 16 * NA, 16), B("ek", 0, NA), B("acc", 0, NA), OP.add)
        ts(B("mr", 16 * NA + 15, 256, 16), B("cs", 128 * NA + 127, 2048, 128), -512.0, None, OP.add)
        once(quant, "eq_", ROT, 128, B("rot"))
        scan(B("cw"), B("ps7", 0, 256), B("mr"), -512.0, OP.max, OP.add)
        tt(B("z"), B("ps2", 0, 256), B("kz"), OP.add)
        l1, rl = B("l1"), B("cw", 15, 256, 16)
        if r == 1:
            unpack("fp", px, "AAAA")
        digit = lambda k, n: B("wk", 1 + 2 * k, 4 * n, 4)
        rounded(digit(0, 16), rl, 32)
        ts(l1, rl, 511.0, None, OP.add)
        tt(digit(1, 16), rl, digit(0, 16), OP.subtract)
        run("V", lambda e: e.tensor_copy(T.zs[:, 16:272].indirect(l1[0]), T.z[:]), [B("zs", 16, 272)], [B("z"), l1])
        cut = (MV, TC + 2 * W, TC + 4 * W)
        third = lambda k: quant("ctq", cut[k], cut[k + 1] - cut[k], B("ct", 4 * cut[k], 4 * cut[k + 1]))
        quant("r2q", 0, 128, B("wk", 0, 512))
        digits(7, 0)
        digits(0, 0, False)
        cp(B("zs", 0, 16), B("zs", 256, 272))
        once(third, 0)
        scan(B("tb"), B("ones"), B("zs"), OFF + 16.0, OP.add, OP.min)
        ends = B("sh", 15, 272, 16)
        ts(B("l2"), B("ps7", 0, 16), 1 / 32, 511.0, OP.mult, OP.add)
        once(scan, B("mh"), B("tneg", 15, 287), B("t512", 0, 272), 0.0, OP.mult, OP.add)
        ts(B("wk", 1, 256, 2), B("tb", 16, 272), -OFF, None, OP.add, off=B("l2", 0, 8))
        act(B("wk", 257, 512, 2), B("tb", 16, 272), AF.Identity, bias=-OFF, off=B("l2", 8, 16))
        once(bounds)
        if r == 0:
            dma("S", T.wq[:].bitcast(dt.uint8), T.wc[:], [B("wq")], [B(px)])
            dma("S", T.wqS[:], T.ws[:], [B("wqS")], [B(px)])
        else:
            dma("S", T.vt[:], T.v[:], [B("vt")], [B("cw")])
        own(B("sh"), B("zs"), 272)
        quant("ttq", 0, 128, B("wk", 0, 512))
        mm(1, 2 * W, "ttq", 0, "ctq", TC)
        once(third, 1)
        mm(2, 2 * W, "ttq", 0, "ctq", TC + 2 * W)
        quant("ttq", 128, 128, B("wk", 1, 513))
        mm(7, 3 * W, "ttq", 128, "ctq", TC + W)
        rounded(B("r256"), ends, 256 * COL)

        def order_list():
            ts(B(lo, 0, 17), B("r16"), 1 / COL, 127.5, OP.mult, OP.add)
            send([(B(plo, 0, 17), B(lo, 0, 17))], dst, "ro%d" % r, "lo%d" % r)
        small = [lambda: tt(B("r16"), ends, B("r256"), OP.subtract),
                 order_list,
                 lambda: rounded(digit(0, 17), B("r16"), 16 * COL),
                 lambda: tt(digit(1, 17), B("r16"), digit(0, 17), OP.subtract),
                 lambda: (quant("r2q", 0, 128, B("wk", 0, 512)), digits(1, 0)),
                 lambda: (ts(B("li"), rl, 512.0 + 15.0, None, OP.add), [waiting(0, b) for b in range(4)]),
                 lambda: (ts(B("l3"), B("ps1", 0, 17), 1 / 32 / COL, 127.5, OP.mult, OP.add), waiting(1, 1)),
                 lambda: ts(B("li"), B("li"), 255, None, OP.bitwise_and),
                 lambda: cp(B("l5"), B("li"))]
        if r == 0:
            small[2:2] = [lambda: unpacker(0), lambda: unpacker(1), lambda: unpacker(2), lambda: (unpacker(3), unpack("fp", px, "AAAA"))]
        beside = dict(enumerate(small, 2))
        waiting = lambda h, b: mm(HB[h][b], 128, "eq_", UNP[b], xq, 128 * h, True, False)
        sort = lambda q, b: gather(q, B("fs", 272 * b, 272 * b + 272), B("fp", 256 * b, 256 * b + 256), B(plo, 0, 17))
        for k in range(1, 8):
            c = WS * (k - 1)
            bank, at = (1, k - 1) if k < 3 else (2, k - 3) if k < 5 else (7, k - 5)
            p = B("ps%d" % bank, W * at, W * at + W)
            scan(B("so", c, c + W), p, B("fb", c, c + W), EPS / 128, OP.subtract, OP.min)
            beside.get(2 * k, lambda: None)()
            if k < 7:
                tt(B("fb", c + WS, c + WS + 52, 2), B("fb", c, c + 52, 2), B("so", c + 17, c + 69, 2), OP.is_ge)
            beside.get(2 * k + 1, lambda: None)()
            for h in range(2):
                a = c + H1 * h
                act(B("ex", 1 + 64 * k + 4 * h, 64 + 64 * k, 8), B("mneg"), AF.Relu, scale=B("so", a + 15, a + 16), bias=B("so", a + 33, a + 34))
            if k in SORT_AT[r]:
                sort("A", SORT_AT[r].index(k))
            if k == 2 and r == 1:
                gather("A", B("orow"), B("ramp"), B(lo, 0, 17))
        quant("exq", 0, 128, B("ex"))
        mm(0, 128, "exq", 0, "ctq", MV, False, True)
        ts(B(lq), B("ps0", 0, 16), 1 / 32, 512 + 15.25, OP.mult, OP.add)
        send([(B(plq), B(lq))], dst, "rl%d" % r, "ll%d" % r)
        waiting(1, 2)
        waiting(1, 3)
        waiting(1, 0)
        if OLDB:
            for b in range(len(SORT_AT[r]), 4):
                sort("A", b)
            tt(B("key"), B("maskd", 0, 272), B("ramp", 0, 256), OP.add, off=B(lq))
            if r == 1:
                gather("A", B("srow"), B("orow"), B(lq))
                dma("S", T.src[:], T.srow[0:128:16, :], [], [B("srow")])
            if NAS[1] < NAS[0]:
                once(ts, B("kc", NAS[1], NAS[0]), B("kc", NAS[1], NAS[0]), 512.0, None, OP.add)
            gather("V", B("av", 0, 128), B("key"), B("l3", 0, 8))
            gather("A", B("av", 128, 272), B("key"), B("l3", 8, 17))
            mosaic = lambda h, b: gather("VVAA"[b], B("zt", 512 * h + b, 512 * h + 512, 4), B("fs", 272 * b, 272 * b + 272), B(plq, 8 * h, 8 * h + 8))

            def layer(h):
                quant(zq, 128 * h, 128, B("zt", 512 * h, 512 * h + 512))
                for b in range(4):
                    mm(HB[h][b], 128, "wq", 128 * b, zq, 128 * h, False, True)
            for b in range(4):
                mosaic(0, b)
            mosaic(1, 0)
            layer(0)
            for b in range(1, 4):
                mosaic(1, b)
            scan(B("s1"), B("t256", 0, 272), B("av"), 256.0, OP.max, OP.min)
            layer(1)
            own(B("s2"), B("s1", 15, 271), 256)
            for h in range(2):
                for b in range(4):
                    scaled(YT[h][b], B("yt", 512 * h + b, 512 * h + 512, 4), B("ps%d" % HB[h][b], 0, 128), 0.03125)
                if h == 0:
                    ts(B("lt"), B("s2", 15, 256, 16), pf(7), None, OP.add)
                quant(yq, 128 * h, 128, B("yt", 512 * h, 512 * h + 512))
                q = (128 * h, 128 * h + 128)
                send([(U8(B(py, *q)), U8(B(yq, *q))), (B(py + "S", *q), B(yq + "S", *q))], dst, "ry%d%d" % (r, h), "ly%d%d" % (r, h))
            gather("A", B("rowt"), B("ramp"), B("lt"))
            gather("A", B("rowk"), B("rowt"), B("l5"))
            if r == 0:
                quant("eq_", ONE[3], 128, B("one"))
            else:
                quant("vq", 0, 128, B("vt"))
            unpack("fo", xq, "VVV")
            own(B("s3"), B("rowk"), 256)
            for h in range(2):
                for b in range(4):
                    mm(HB[1 - h][b], 128, "eq_", UNP[b], py, 128 * h)
            for h in range(2):
                for b in range(4):
                    scaled(DY[h][b], B("dy", 272 * b + 128 * h, 272 * b + 128 * h + 128), B("ps%d" % HB[1 - h][b], 0, 128), 1 / 32)
                if h == 0:
                    ts(B("l4"), B("s3", 15, 256, 16), pf(7), None, OP.add)
            xn = "x%d" % (r + 1)
            mm(0, 256, "eq_", ONE[3], xq, 0)
            gather("A", B("tk", 0, 256), B("dy", 272 * 3, 272 * 4), B("l4"))
            for b in range(3):
                tt(B(xn, b, 1024, 4), B("dy", 272 * b, 272 * b + 272), B("fo", 256 * b, 256 * b + 256), OP.add, off=B("l4"))
            for h in range(2):
                tt(B(xn, 512 * h + 3, 512 * h + 512, 4), B("ps0", 128 * h, 128 * h + 128), B("tk", 128 * h, 128 * h + 128), OP.add)
            for h in range(2):
                quant("xq" + L[r + 1], 128 * h, 128, B(xn, 512 * h, 512 * h + 512))
            continue
        for b in range(4 - SV):
            sort("A", b)
        tt(B("key"), B("maskd", 0, 272), B("ramp", 0, 256), OP.add, off=B(lq))
        for b in range(4 - SV, 4):
            sort("V", b)
        once(ts, B("t256"), B("kbi"), pf(1), 256.0, OP.is_equal, OP.mult)
        gather("V", B("av"), B("key"), B("l3"))
        scan(B("s1"), B("t256", 0, 272), B("av"), 256.0, OP.max, OP.min)
        def mosaic(h, b):
            gather(ZT[h][b], B("zt", 512 * h + b, 512 * h + 512, 4), B("fs", 272 * b, 272 * b + 272), B(plq, 8 * h, 8 * h + 8))

        def layer(h):
            quant(zq, 128 * h, 128, B("zt", 512 * h, 512 * h + 512))
            for b in range(4):
                mm(HB[h][b], 128, "wq", 128 * b, zq, 128 * h, False, True)
        for b in range(4):
            mosaic(0, b)
        mosaic(1, 0)
        layer(0)
        for b in range(1, 4):
            mosaic(1, b)
        layer(1)
        for h in range(2):
            for b in range(4):
                scaled(YT[h][b], B("yt", 512 * h + b, 512 * h + 512, 4), B("ps%d" % HB[h][b], 0, 128), 0.03125)
            quant(yq, 128 * h, 128, B("yt", 512 * h, 512 * h + 512))
            q = (128 * h, 128 * h + 128)
            send([(U8(B(py, *q)), U8(B(yq, *q))), (B(py + "S", *q), B(yq + "S", *q))], dst, "ry%d%d" % (r, h), "ly%d%d" % (r, h))
        own(B("s2"), B("s1", 15, 271), 256)
        for b in range(4):
            once(act, B("dy", 272 * b + 256, 272 * b + 272), B("zz", 0, 16))
        unpack("fo", xq, "AA")
        ts(B("lt"), B("s2", 15, 256, 16), pf(7), None, OP.add)
        once(ts, B("ebig", 0, 516), B("ebig", 0, 516), 1 / 32, None, OP.mult)
        gather("V", B("rowt"), B("ramp"), B("lt"))
        once(quant, "eq_", ONE[2], 128, B("ebig", 2, 514))
        gather("V", B("rowk"), B("rowt"), B("l5"))
        if r == 0:
            quant("eq_", ONE[3], 128, B("ebig", 1, 513))
        else:
            quant("vq", 0, 128, B("vt"))
            gather("A", B("orow"), B("ramp"), B(lo, 0, 17))
            gather("A", B("srow"), B("orow"), B(lq))
            dma("S", T.src[:], T.srow[0:128:16, :], [], [B("srow")])
        own(B("s3"), B("rowk"), 256)
        ts(B("l4"), B("s3", 15, 256, 16), pf(7), None, OP.add)
        for h in range(2):
            for b in range(4):
                mm(HB[1 - h][b], 128, "eq_", UNP[b], py, 128 * h)
        for h in range(2):
            for b in range(4):
                scaled(DY[h][b], B("dy", 272 * b + 128 * h, 272 * b + 128 * h + 128), B("ps%d" % HB[1 - h][b], 0, 128), 1 / 32)
        xn = "x%d" % (r + 1)
        for b in (2, 3):
            mm(b - 2, 256, "eq_", ONE[b], xq, 0)
            gather("A", B("tk", 256 * b - 512, 256 * b - 256), B("dy", 272 * b, 272 * b + 272), B("l4"))
        for b in (0, 1):
            tt(B(xn, b, 1024, 4), B("dy", 272 * b, 272 * b + 272), B("fo", 256 * b, 256 * b + 256), OP.add, off=B("l4"))
        for b in (2, 3):
            tt(B(xn, b, 1024, 4), B("ps%d" % (b - 2), 0, 256), B("tk", 256 * b - 512, 256 * b - 256), OP.add)
        quant("xq" + L[r + 1], 0, 256, B(xn))
    dma("S", T.oc[:], T.xqc[:].bitcast(dt.uint8), [], [B("xqc")])
    for k in range(4):
        dma("A", T.osc[4 * k:4 * k + 4, :], T.xqcS[32 * k:32 * k + 4, :], [], [B("xqcS")])
    for h in range(2):
        mm(2 + h, 128, "vq", 0, "xqc", 128 * h)
    for h in range(2):
        (cp, act)[h](B("yout", 128 * h, 128 * h + 128), B("ps%d" % (2 + h), 0, 128))
    dma("S", T.y[:], T.yout[:], [], [B("yout")])
    for q in ("G", "P", "A", "V"):
        need("G", q, cnt[q])
    for sem, val in final.items():
        need("G", sem, val)
